import numpy as np, ml_dtypes
CORES = [24,25,26,27,28,29,30,31]
N = 8
BF = ml_dtypes.bfloat16
def gentries(a):
    return np.ascontiguousarray(a.reshape(8, 16, -1).transpose(0, 2, 1)).reshape(8, -1)
def gtable(e):
    e = np.asarray(e); return np.ascontiguousarray(e.reshape(8, -1, 16).transpose(0, 2, 1)).reshape(128, -1).astype(np.int32)
W, K, RO, S, TH, AG = 2048, 384, 2, 4, 70, 9
L0 = 16 - RO
B = K // N
def hubbed(rng, hub, n, share):
    return np.where(rng.random((N, 8, n)) < share, np.take_along_axis(hub, rng.integers(0, 32, (N, 8, n)), 2), rng.integers(0, W, (N, 8, n)))
def parts(rng):
    x = np.where(rng.random((N, 8, 1, W)) < 0.875, rng.integers(0, 16, (N, 8, 16, W)), rng.integers(4, 12, (N, 8, 16, W)))
    hub = rng.integers(0, W, (N, 8, 32)); a = hubbed(rng, hub, L0 * W, 0.1).reshape(N, 8, L0, W)
    a = np.where(rng.random(a.shape) < rng.choice(np.array([0.05, 0.2, 0.45]), (N, 8, 1, 1)), -1, a)
    return x, a, hubbed(rng, hub, W, 0.25), rng.integers(0, W, (N, 8, K))
def pack(x, a, s, p):
    a = np.concatenate([a, np.full((N, 8, RO, W), -1)], axis=2)
    return {"x0": np.ascontiguousarray(x.reshape(N, 128, W)).astype(np.float32).astype(BF), "lk": np.ascontiguousarray(a.reshape(N, 128, W)).astype(np.int32),
            "nx": np.ascontiguousarray(s).astype(np.int32), "w0": np.stack([gtable(e) for e in p])}
def setup_inputs(rng):
    return pack(*parts(rng))
def setup_inputs_ties(rng):
    x, a, s, p = parts(rng); h = W // 2
    x[..., :h] = rng.integers(0, 16, (N, 8, 16, h))
    t = TH - 1 + rng.integers(0, 3, (N, 8, 1, h)); o = np.argsort(rng.random((N, 8, 16, h)), axis=2)
    x[..., h:2 * h] = x[..., :h] + np.where(x[..., :h] < 8, 1, -1) * ((t >> 4) + (o < (t & 15)))
    i = np.arange(L0)[None, None, :, None]; at = rng.integers(0, L0, (N, 8, 1, h)); bare = rng.random((N, 8, 1, h)) < 0.5
    a[..., :h] = np.where(i == at, h + np.arange(h), np.where((i > at) | bare, -1, a[..., :h]))
    return pack(x, a, s, rng.integers(0, h, (N, 8, K)))
def setup_inputs_votes(rng):
    x, a, s, p = parts(rng); h = K // 2
    for q in range(N):
        for g in range(8):
            if q < N - 1 and g % 4 == 3: continue
            c = rng.permutation(W)[:K * (S + 1)].reshape(K, S + 1); a[q, g] = -1
            s[q, g, c[:, :S]] = c[:, 1:]
            if q == N - 1:
                y = rng.integers(5, 8, (16, K, S)); e = np.where(np.arange(K) < h, 15, rng.integers(8, 11, (16, K)))
                s[q, g, c[:h, S]] = c[h + rng.permutation(h), 2]
                p[q, g] = c[:, 0]
            elif g % 2 == 1:
                n = K - 1 if g == 1 else int(rng.integers(h, K))
                y = rng.integers(0, 8, (16, K, S)); y[rng.permutation(16)[AG - 1:], n] += 8
                e = rng.integers(0, 16, (16, K)); e[:, 0] = 8
                s[q, g, c[:, S - 1]] = c[0, S]
                p[q, g] = c[:, 0]
            else:
                y = rng.integers(2, 14, (16, K, S)); y[:, h:] = np.where(rng.random((1, K - h, 1)) < 0.5, 2, 13)
                z = y[:, :, 0]
                for k in range(1, S): z = (z + y[:, :, k]) >> 1
                o = np.argsort(rng.random((16, K)), axis=0); n = AG - 1 + rng.integers(0, 3, (1, K))
                e = z + np.where(o < n, rng.integers(1, 3, (16, K)), -rng.integers(0, 2, (16, K)))
                s[q, g, c[h:, S - 1]] = np.where(rng.random(K - h) < 0.75, c[:K - h, S], c[h:, S])
                p[q, g] = c[rng.permutation(K), 0]
            x[q, g][:, c[:, :S].reshape(-1)] = y.reshape(16, K * S); x[q, g][:, c[:, S]] = e
    return pack(x, a, s, p)
def setup_inputs_alike(rng):
    x, a, s, p = parts(rng); few = np.array([0, W - 1, W // 2, 5])
    a[:, ::2] = np.where(a[:, ::2] < 0, -1, rng.choice(few, (N, 4, L0, W)))
    a[:, 1] = np.where(a[:, 1] < 0, -1, np.arange(W)); s[:, 1] = np.arange(W)
    s[:, 0] = W - 1; s[:, 4] = 0; s[:, 2] = rng.choice(few, (N, W))
    p[:, 3] = p[:, 3, :1]; p[:, 5] = rng.choice(few, (N, K)); p[:, 6] = np.where(rng.random((N, K)) < 0.5, 0, W - 1)
    return pack(x, a, s, p)
def setup_inputs_full(rng):
    x, a, s, p = parts(rng)
    x[:, ::2] = rng.integers(6, 10, (N, 4, 16, W)); x[:, 1::2] = 15 * rng.integers(0, 2, (N, 4, 16, W))
    a = np.where(a < 0, rng.integers(0, W, a.shape), a)
    return pack(x, a, s, p)
def setup_inputs_spread(rng):
    x, a, s, p = parts(rng)
    x = np.minimum((np.exp2(1 + 3 * rng.random((N, 8, 1, W))) * rng.random((N, 8, 16, W))).astype(np.int64), 15)
    a = np.where(a < 0, -1, (W * rng.random(a.shape) ** 3).astype(np.int64)); s = (W * rng.random(s.shape) ** 2).astype(np.int64)
    return pack(x, np.minimum(a, W - 1), np.minimum(s, W - 1), p)
def check_inputs(d):
    bad = []
    x = d["x0"].astype(np.float32)
    if not np.all((x >= 0) & (x <= 15) & (x == np.floor(x))): bad.append("x0 whole numbers from 0 to 15")
    for k, lo in (("lk", -1), ("nx", 0), ("w0", 0)):
        if np.min(d[k]) < lo or np.max(d[k]) > W - 1: bad.append("range of " + k)
    if np.any(d["lk"].reshape(-1, 8, 16, W)[:, :, L0:] != -1): bad.append("upper links of lk empty")
    return bad
def reference(x0, lk, nx, w0):
    M = W + RO * K
    X = np.zeros((N, 8, 16, M), np.int64); X[..., :W] = x0.astype(np.float32).astype(np.int64).reshape(N, 8, 16, W)
    ad = np.full((N, 8, 16, M), -1, np.int64); ad[..., :W] = lk.reshape(N, 8, 16, W)
    sc = np.zeros((N, 8, M), np.int64); sc[..., :W] = nx
    v = np.stack([gentries(e) for e in w0]).astype(np.int64)
    i = np.arange(16)[:, None]
    for t in range(RO):
        n = W + t * K; Z = np.zeros((N, 8, 16, K), np.int64)
        for r in range(N):
            for g in range(8):
                x, a, s, p = X[r, g], ad[r, g], sc[r, g], v[r, g]
                z = x[:, p]; l = np.full(K, 16)
                for k in range(S):
                    c = a[:, p]
                    dist = np.add.reduce(np.abs(x[:, np.maximum(c, 0)] - z[:, None, :]), axis=0)
                    b = np.max(np.where((c >= 0) & (dist < TH) & (i < l), i, -1), axis=0)
                    p = np.where(b >= 0, c[np.maximum(b, 0), np.arange(K)], s[p]); l = np.where(b >= 0, b, l)
                    y = x[:, p]; yes = np.add.reduce((y > z).astype(np.int64), axis=0) >= AG
                    z = (z + y) >> 1
                Z[r, g] = z; v[r, g] = p
                ends = np.zeros(M, bool); ends[p] = True
                no = np.zeros(M, bool); no[p[~yes]] = True
                x[::2] = np.where(ends & ~no, 15 - x[::2], x[::2])
                u, first = np.unique(p, return_index=True)
                a[L0 + t, u] = n + first; s[n:n + K] = s[p]
        for r in range(N):
            for q in range(N):
                X[q, :, :, n + r * B:n + (r + 1) * B] = np.roll(Z[r, :, :, q * B:(q + 1) * B], (q - r) % N, axis=0)
    return {"yx": X.reshape(N, 128, M).astype(np.float32).astype(BF), "yv": v.astype(np.float32)}

@@ -1,0 +1,525 @@
+from concourse.bass import DstId, RemoteDMATransfer
+from concourse.mybir import AluOpType, ActivationFunctionType
+
+ALU = AluOpType
+ACT = ActivationFunctionType
+H = 8 + 2816
+NA = 2816 + 384
+EPS = 2.0 ** -9
+NB = 1
+ABS = ((2, 2), (4, 2), (6, 4), (10, 2), (12, 3))
+ORDER = (2, 4, 0, 6, 8, 10, 12)
+CY, FV, FS, FP, PE, WAKE = 0.83e-3, 0.06, 0.10, 0.04, 0.45e-3, 0.08
+GA_C, SC_C = 1.5, 3.5
+AHEAD = 2.2
+LOADS = {"dw": 4e3, "dl": 3e3, "dx": 2e3, "dy": 1e3}
+
+SCRATCH = {}
+
+
+def _decl(dtype, where="sbuf", **shapes):
+    for n, sh in shapes.items():
+        SCRATCH[n] = (where, [128] + sh, dtype)
+
+
+_decl("bfloat16", X2=[2 * H], XO=[8 + NA], XM=[384], W3=[768], ZD=[144], BK=[128], ID=[128], NI=[128], PN=[128], DW=[128],
+      TU=[128], ZR=[128], SWB=[512], R1=[384], DIAG=[24, 16], TRI=[24, 16], E=[576, 16], DG=[24, 16], DX=[384], FX=[384],
+      XV=[384], XW=[384], ZN0=[384], ZN1=[384], RZ0=[384], RZ1=[384])
+_decl("float32", AT=[NA], IDT=[2816], C=[32], Q=[144], QX=[24, 16], QX2=[128], QG=[128], T1=[128], T2=[128], SWF=[512],
+      NEWL=[384], DWL=[24], VLF=[24], WT=[24], VF=[384], DM=[384], SC2=[384], RS=[24, 16], RT=[384], S1=[24], S2=[24], S3=[24],
+      S4=[24], GA=[384], GA3=[24, 16])
+_decl("int32", ATI=[2048], W0I=[24], PI=[8], QW=[768])
+_decl("uint16", VL0=[24], VX0=[24], VXN=[24], VB=[49, 16], AOFF=[24], XOFF=[24])
+for _s in "AB":
+    _decl("bfloat16", **{"CD" + _s: [3072], "AB" + _s: [3072], "XG" + _s: [384], "Z" + _s: [384], "ZF" + _s: [12, 16],
+                         "VAL" + _s: [192], "F" + _s: [192], "GT" + _s: [192]})
+    _decl("float32", **{"LT" + _s: [192], "KT" + _s: [192], "SC" + _s: [192]})
+    _decl("int32", **{"VI" + _s: [12], "VJ" + _s: [12]})
+    _decl("uint16", **{"CL" + _s: [192]})
+    _decl("float32", "psum", **{"pD" + _s: [512], "pK" + _s: [32, 16], "pZ" + _s: [32, 16], "pS" + _s: [32, 16]})
+SEMAPHORES = ["sv", "ss", "sp", "sg", "dw", "dl", "dx", "dy", "dd", "do", "dv", "dgA", "dgB", "arr0", "arr1", "lsem"]
+
+
+def schedule(ops):
+    preds, lastw, readers = [], {}, {}
+    for j, o in enumerate(ops):
+        p = {}
+        for k in o["r"]:
+            if k in lastw:
+                p[lastw[k]] = 0 if k[0] == "p" and ops[lastw[k]]["e"] == o["e"] else 1
+            if k[0] == "p":
+                for x in readers.get(k, ()):
+                    p.setdefault(x, 0 if ops[x]["e"] == o["e"] else 1)
+        for k in o["w"]:
+            for x in ([lastw[k]] if k in lastw else []) + readers.get(k, []):
+                same = ops[x]["e"] == o["e"] or (o["sem"] and ops[x]["sem"] == o["sem"])
+                p.setdefault(x, 0 if same else 1)
+        p.pop(j, None)
+        preds.append(p)
+        for k in o["r"]:
+            readers.setdefault(k, []).append(j)
+        for k in o["w"]:
+            lastw[k] = j
+            readers[k] = []
+    n = len(ops)
+    succ = [[] for _ in range(n)]
+    for j in range(n):
+        for i in preds[j]:
+            succ[i].append(j)
+    bl = [0.0] * n
+    for j in range(n - 1, -1, -1):
+        bl[j] = ops[j]["c"] + ops[j]["lat"] + max([bl[x] + WAKE for x in succ[j]] or [0.0])
+    left = [len(preds[j]) for j in range(n)]
+    base = [0.0] * n
+    free, out = {}, []
+    ready = [j for j in range(n) if not left[j]]
+    dmaq = 0.0
+    while ready:
+        st = [max(base[j], free.get(ops[j]["e"], 0.0)) for j in ready]
+        t0 = min(st) + 0.03
+        j = max((bl[x] + ops[x]["first"], -x, x) for x, s in zip(ready, st) if s <= t0)[2]
+        ready.remove(j)
+        o = ops[j]
+        s = max(base[j], free.get(o["e"], 0.0))
+        fin = free[o["e"]] = s + o["c"]
+        if o["lat"]:
+            dmaq = max(dmaq, fin) + o["by"]
+            fin = max(dmaq, fin) + o["lat"]
+        out.append(o)
+        for x in succ[j]:
+            base[x] = max(base[x], fin + WAKE if preds[x][j] else s + o["c"])
+            left[x] -= 1
+            if not left[x]:
+                ready.append(x)
+    return out
+
+
+def emit(g, T, ops):
+    eng = {"V": g.vector, "S": g.scalar, "P": g.tensor, "G": g, "Y": g.sync}
+    sem = {"V": "sv", "S": "ss", "P": "sp", "G": "sg"}
+    cnt = {}
+    know = {e: {} for e in eng}
+    lastw, readers, snaps = {}, {}, {}
+
+    def wait_for(e, r, w, me):
+        need = []
+        for k in r:
+            if k in lastw:
+                need.append((lastw[k], False))
+            if k[0] == "p":
+                need.extend((x, True) for x in readers.get(k, ()))
+        for k in w:
+            if k in lastw:
+                need.append((lastw[k], True))
+            need.extend((x, True) for x in readers.get(k, ()))
+        mx = {}
+        for (s, c), anti in need:
+            if (s == e and (anti or e == "P")) or s == me:
+                continue
+            if s not in eng:
+                c = cnt[s]
+            if know[e].get(s, 0) < c:
+                mx[s] = max(mx.get(s, 0), c)
+        for s in list(mx):
+            if any(s2 != s and mx[s2] and snaps.get((s2, mx[s2]), {}).get(s, 0) >= mx[s] for s2 in mx):
+                know[e][s] = max(know[e].get(s, 0), mx[s])
+                mx[s] = 0
+        for s, c in mx.items():
+            if c:
+                eng[e].wait_ge(T.sem[sem.get(s, s)], c)
+                for s2, c2 in snaps.get((s, c), {}).items():
+                    know[e][s2] = max(know[e].get(s2, 0), c2)
+                know[e][s] = max(know[e].get(s, 0), c)
+
+    for o in ops:
+        e, r, w = o["e"], o["r"], o["w"]
+        if e == "R":
+            cnt[o["sem"]] = 14
+            for k in w:
+                lastw[k] = (o["sem"], 14)
+            continue
+        wait_for(e, r, w, o["sem"])
+        if o["sem"] == "lsem":
+            o["fn"](eng[e])
+            continue
+        s, add = (o["sem"], 16) if o["sem"] else (e, 1)
+        cnt[s] = cnt.get(s, 0) + add
+        o["fn"](eng[e]).then_inc(T.sem[sem.get(s, s)], add)
+        tok = (s, cnt[s])
+        sn = dict(know[e])
+        if s in eng:
+            sn[s] = cnt[s]
+        else:
+            for s2, c2 in snaps.get((s, cnt[s] - 16), {}).items():
+                sn[s2] = max(sn.get(s2, 0), c2)
+        snaps[tok] = sn
+        for k in r:
+            readers.setdefault(k, []).append(tok)
+        for k in w:
+            lastw[k] = tok
+            readers[k] = []
+    for s, c in sorted(cnt.items()):
+        if know["G"].get(s, 0) < c:
+            g.wait_ge(T.sem[sem.get(s, s)], c)
+    g.wait_ge(T.sem.lsem, 28)
+
+
+def rank_program(g, core, T, topo):
+    rank = T.rank_of(core)
+    if rank is None:
+        return
+    ops = []
+    ahead = [0.0]
+
+    def op(e, fn, r, w, c, sem=None, lat=0.0, by=0.0):
+        ops.append({"e": e, "fn": fn, "r": list(r), "w": list(w), "c": c, "sem": sem, "lat": lat, "by": by,
+                    "first": ahead[0] + LOADS.get(sem, 0.0)})
+
+    def V(fn, r, w, n):
+        op("V", fn, r, w, FV + max(64, n) * CY)
+
+    def ts(out, in0, s1, s2, op0, op1, r, w, n=64):
+        if op1 is None:
+            V(lambda v: v.tensor_scalar(out, in0, s1, None, op0), r, w, n)
+        else:
+            V(lambda v: v.tensor_scalar(out, in0, s1, s2, op0, op1), r, w, n)
+
+    def tt(out, in0, in1, o, r, w, n=64):
+        V(lambda v: v.tensor_tensor(out, in0, in1, o), r, w, n)
+
+    def cp(out, in_, r, w, n=64):
+        V(lambda v: v.tensor_copy(out, in_), r, w, n)
+
+    def tr(out, in_, r, w, n=64):
+        V(lambda v: v.transpose(out, in_), r, w, n)
+
+    def ms(ap, x, w, n=64):
+        V(lambda v: v.memset(ap, x), [], w, n)
+
+    def act(out, in_, f, bias, scale, r, w, n):
+        op("S", lambda s: s.activation(out, in_, f, bias=bias, scale=scale), r, w, FS + n * CY)
+
+    def mm(out, lhsT, rhs, start, stop, r, w, n):
+        op("P", lambda t: t.matmul(out, lhsT, rhs, start, stop), r, w, FP + max(64, n) * PE)
+
+    def dma(e, out, in_, sem, r, w, kb):
+        op(e, lambda q: q.dma_start(out=out, in_=in_), r, w, 0.07, sem, 2.0, kb / 200.0)
+
+    B = lambda n, s: T[n + s]
+    st = {"A": 0, "B": 1}
+
+    dma("Y", T.W0I[:], T.w0[:], "dw", [], ["W0I"], 12)
+    for i in range(8):
+        dma("Y", T.ATI[16 * i:16 * i + 15, :], T.lk[16 * i:16 * i + 15, :], "dl", [], ["ATI"], 120)
+    dma("Y", T.ATI[15:128:16, :], T.nx[:, :], "dl", [], ["ATI"], 64)
+    dma("Y", T.XO[:, 8:2056], T.x0[:, :], "dx", [], ["XOb"], 512)
+
+    def both(sem, src, keys):
+        for i in range(8):
+            o, a = (i % 2) * H + 8, 32 * (i // 2)
+            for par in range(2):
+                dma("Y", T.X2[a + 16 * par:a + 16 * par + 16, o:o + 2048], src[16 * i:16 * i + 16, :], sem, keys, ["X2b"], 64)
+    both("dy", T.x0, [])
+
+    def iota(out, pat, base, cm, key, n, flag=True):
+        if flag:
+            op("G", lambda q: q.iota(out, pat, base, cm, allow_small_or_imprecise_dtypes=True), [], [key], 0.13 + 2 * n * CY)
+        else:
+            op("G", lambda q: q.iota(out, pat, base, cm), [], [key], 0.13 + 2 * n * CY)
+    iota(T.PI[:, 0:1], [[1, 1]], 0, 1, "PI", 1, False)
+    iota(T.Q[:], [[1, 144]], 0, 0, "Q", 144)
+    iota(T.QG[:], [[1, 8], [0, 16]], 0, 0, "QG", 128)
+    iota(T.QX2[:], [[0, 8], [1, 16]], 0, 0, "QX2", 128)
+    iota(T.QX[:], [[0, 24], [1, 16]], 0, 0, "QX", 384)
+    iota(T.DWL[:], [[16, 24]], 2816, 0, "DWL", 24)
+    iota(T.QW[:, 0:256], [[32, 8], [0, 2], [1, 16]], 0, 0, "QW", 256, False)
+    iota(T.QW[:, 256:512], [[32, 8], [0, 2], [1, 16]], 16, 0, "QW", 256, False)
+    iota(T.QW[:, 512:768], [[1, 256]], 0, 0, "QW", 256, False)
+    iota(T.NEWL[:], [[1, 384]], 2049, 0, "NEWL", 384)
+    iota(T.IDT[:], [[1, 2816]], 0, 0, "IDT", 2816)
+    c = lambda i: T.C[:, i:i + 1]
+    ms(T.ZR[:], 0.0, ["ZR"])
+    for ph in range(2):
+        ms(T.X2[:, ph * H:ph * H + 8], 255.0, ["X2n"])
+        ms(T.X2[:, ph * H + 2056:ph * H + H], 255.0, ["X2n"], 384)
+    ms(T.XO[:, 0:8], 0.0, ["XOn"])
+    ms(T.XO[:, 2056:8 + NA], 0.0, ["XOn"], 576)
+    ts(T.PI[:, 1:2], T.PI[:, 0:1], 4, None, ALU.arith_shift_right, None, ["PI"], ["PI1"])
+    ts(T.PI[:, 2:3], T.PI[:, 0:1], 15, None, ALU.bitwise_and, None, ["PI"], ["PI2"])
+    ts(T.PI[:, 3:4], T.PI[:, 0:1], 4, 1, ALU.arith_shift_right, ALU.bitwise_and, ["PI"], ["PI3"])
+    ts(T.PI[:, 4:5], T.PI[:, 0:1], 1, None, ALU.bitwise_and, None, ["PI"], ["PI4"])
+    cp(T.C[:, 0:5], T.PI[:, 0:5], ["PI", "PI1", "PI2", "PI3", "PI4"], ["C0"])
+    for o, i, s1, s2, o0, o1, rr in [
+        (6, 2, 15.0, None, ALU.is_equal, None, []),
+        (7, 2, 14.0, None, ALU.is_equal, None, []),
+        (10, 2, 16.0, -209.0, ALU.mult, ALU.add, []),
+        (20, 4, -1.0, 1.0, ALU.mult, ALU.add, []),
+        (16, 3, 1000.0, c(0), ALU.mult, ALU.add, []),
+        (21, 3, -1000.0, 1000.0, ALU.mult, ALU.add, []),
+        (15, 2, -1.0, c(0), ALU.mult, ALU.add, []),
+        (8, 6, 1.0e6, 69.5, ALU.mult, ALU.add, [6]),
+        (22, 6, -16.0, c(2), ALU.mult, ALU.add, [6]),
+        (14, 6, 1.0, None, ALU.subtract, None, [6]),
+        (23, 6, -1.0, 1.0, ALU.mult, ALU.add, [6]),
+        (12, 20, -2.0, None, ALU.mult, None, [20]),
+        (13, 20, 15.0, None, ALU.mult, None, [20]),
+        (17, 16, 16.0, None, ALU.add, None, [16]),
+        (19, 21, c(0), None, ALU.add, None, [21]),
+        (24, 15, 15.0, None, ALU.add, None, [15]),
+        (9, 7, -1000.0, c(8), ALU.mult, ALU.add, [7, 8]),
+        (11, 22, 2.0, 4096.0, ALU.add, ALU.mult, [22]),
+        (18, 19, -16.0, None, ALU.add, None, [19]),
+    ]:
+        ts(c(o), c(i), s1, s2, o0, o1, ["C0"] + ["C%d" % x for x in rr], ["C%d" % o])
+    cp(T.VL0[:], T.W0I[:], ["W0I"], ["VLA", "VLB"])
+    for j, col in enumerate((16, 17, 18, 19)):
+        ts(T.SWB[:, 128 * j:128 * j + 128], T.Q[:, 0:128], c(col), None, ALU.is_equal, None, ["Q", "C%d" % col], ["SWB"], 128)
+    swb = lambda s, d: T.SWB[:, 128 * (2 * s + d):128 * (2 * s + d) + 128]
+    swf = lambda s, d: T.SWF[:, 128 * (2 * s + d):128 * (2 * s + d) + 128]
+    ts(T.ID[:], T.Q[:, 0:128], c(0), None, ALU.is_equal, None, ["Q", "C0"], ["ID"], 128)
+    ts(T.NI[:], T.Q[:, 0:128], c(0), -1.0, ALU.is_equal, ALU.mult, ["Q", "C0"], ["NI"], 128)
+    ts(T.ZD[:], T.Q[:], c(24), None, ALU.is_equal, None, ["Q", "C24"], ["ZD"], 144)
+    cp(T.SWF[:], T.SWB[:], ["SWB"], ["SWF"], 512)
+    ts(T.DW[:], T.Q[:, 0:128], c(0), c(11), ALU.is_equal, ALU.mult, ["Q", "C0", "C11"], ["DW"], 128)
+    ts(T.PN[:], T.Q[:, 0:128], c(0), 128.0, ALU.is_equal, ALU.mult, ["Q", "C0"], ["PN"], 128)
+    ts(T.BK[:], T.QG[:], c(1), None, ALU.is_equal, None, ["QG", "C0"], ["BK"], 128)
+    ts(T.T1[:], T.QX2[:], c(2), -16.0, ALU.is_lt, ALU.mult, ["QX2", "C0"], ["T1"], 128)
+    ts(T.T2[:], T.T1[:], 1.0, c(23), ALU.add, ALU.mult, ["T1", "C23"], ["T2"], 128)
+    tt(T.TU[:], T.T2[:], T.BK[:], ALU.mult, ["T2", "BK"], ["TU"], 256)
+    ts(T.R1[:], T.QX[:], 0.0, None, ALU.is_gt, None, ["QX"], ["R1"], 384)
+    ms(T.AT[:, 2048:NA], -1.0, ["ATn"], 1152)
+    ts(T.DIAG[:], T.QX[:], c(2), None, ALU.is_equal, None, ["QX", "C0"], ["DIAG"], 384)
+    ts(T.TRI[:], T.QX[:], c(2), None, ALU.is_gt, None, ["QX", "C0"], ["TRI"], 384)
+    ts(T.NEWL[:], T.NEWL[:], c(7), None, ALU.mult, None, ["NEWL", "C7"], ["NEWL"], 384)
+    ts(T.DWL[:], T.DWL[:], c(2), None, ALU.add, None, ["DWL", "C0"], ["DWL"])
+    ts(T.QW[:], T.QW[:], 127, None, ALU.bitwise_and, None, ["QW"], ["QW"], 768)
+    ts(T.W3[:], T.QW[:], c(0), None, ALU.is_equal, None, ["QW", "C0"], ["W3"], 768)
+
+    sl = lambda s: slice(12 * st[s], 12 * st[s] + 12)
+    sw = lambda s: slice(192 * st[s], 192 * st[s] + 192)
+    X2ALL, XOALL = ["X2b", "X2n"], ["XOb", "XOn"]
+
+    def vx_lists(s, src, key):
+        for u in range(2):
+            o = 12 * st[s] + 6 * u
+            ts(T.VX0[:, o:o + 6], src(u), 8.0, None, ALU.add, None, [key], ["VX" + s])
+
+    for s in "AB":
+        vx_lists(s, lambda u: T.W0I[:, 12 * st[s] + u:12 * st[s] + 12:2], "W0I")
+    cp(T.AT[:, 0:2048], T.ATI[:], ["ATI"], ["AT"], 2048)
+
+    def agather(s, key=True):
+        act(T.GA[:, sw(s)], T.AT[:].indirect(T.VL0[:, sl(s)]), ACT.Identity, 0.0, 1.0, ["AT", "ATn", "VL" + s], ["GA" + s], 192 * GA_C)
+        if key:
+            dma("Y", T.GA3[:, sl(s), :], T.GA[:, sw(s)], "dg" + s, ["GA" + s], ["G3" + s], 96)
+
+    def xgather(s):
+        act(T.XV[:, sw(s)], T.XO[:].indirect(T.VX0[:, sl(s)]), ACT.Identity, 0.0, 1.0, XOALL + ["VX" + s], ["XV" + s], 192 * GA_C)
+
+    def swap4(out, o0, mat, src, key, r, stop, n=1, f=1):
+        k = 0
+        for rep in range(n):
+            for u in range(2):
+                for v in range(2):
+                    k += 1
+                    mm(out[:, o0 + v:o0 + 12:2, :], mat(v, u), src(u), False, stop and k == 4 * n, r, [key], 96 * f)
+
+    def xv(s):
+        return lambda u: T.XV[:, 192 * st[s] + 96 * u:192 * st[s] + 96 * u + 96]
+
+    def zswap(s, first):
+        o = B("pZ", s)
+        if first:
+            mm(o[:, 0:12, :], T.ZR[:], T.XV[:, sw(s)], True, False, ["ZR", "XV" + s], ["pZ" + s], 192)
+        else:
+            mm(o[:, 0:12, :], T.ID[:], B("Z", s)[:, 0:192], True, False, ["ID", "Z" + s], ["pZ" + s], 192)
+        swap4(o, 0, swb, xv(s), "pZ" + s, ["XV" + s, "SWB"], True, 2 if first else 1)
+
+    def zact(s, first, final=False):
+        bias = 127.75 if first else 63.75
+        src = B("pZ", s)[:, 0:12, :]
+        if final:
+            act(B("ZF", s)[:], src, ACT.Identity, bias, 0.5, ["pZ" + s], ["ZF" + s], 192)
+        else:
+            for d in range(2):
+                act(B("Z", s)[:, 192 * d:192 * d + 192], src, ACT.Identity, bias, 0.5, ["pZ" + s], ["Z" + s], 192)
+
+    def lists(s, L):
+        lt, cl = B("LT", s), B("CL", s)
+        for b in range(6):
+            o = 192 * st[s] + 32 * b
+            tr(lt[:, b:192:6], T.GA[:, o:o + 32], ["GA" + s], ["LT" + s])
+        for g2 in range(2):
+            ts(cl[:, g2:12 * L:2], lt[:, 96 * g2:96 * g2 + 6 * L], 8.0 + H * g2, None, ALU.add, None, ["LT" + s], ["CL" + s], 90)
+
+    def begin(s, L):
+        agather(s)
+        xgather(s)
+        zswap(s, True)
+        zact(s, True)
+        lists(s, L)
+
+    def bulk(s, k, t):
+        L = 14 + t
+        pd, ab, cd, cl, z = B("pD", s), B("AB", s), B("CD", s), B("CL", s), B("Z", s)
+        for i in range(0, 2 * NB, 2):
+            act(B("XG", s)[:], T.X2[:].indirect(cl[:, 12 * i:12 * i + 24]), ACT.Identity, 0.0, 1.0, X2ALL + ["CL" + s], ["XG" + s], 384 * GA_C)
+            o = B("pS", s)[:, 0:24, :]
+            mm(o, T.ID[:], B("XG", s)[:], True, False, ["ID", "XG" + s], ["pS" + s], 384)
+            mm(o, T.NI[:], z[:], False, True, ["NI", "Z" + s], ["pS" + s], 384)
+            act(ab[:, 192 * i:192 * i + 384], o, ACT.Abs, 128.0, 1.0, ["pS" + s], ["AB%s%d" % (s, i), "AB%s%d" % (s, i + 1)], 384)
+        for i in range(2 * NB, L, 2):
+            n = min(2, L - i)
+            tt(cd[:, 192 * i:192 * (i + n)], T.X2[:].indirect(cl[:, 12 * i:12 * (i + n)]), z[:, 0:192 * n], ALU.subtract,
+               X2ALL + ["CL" + s, "Z" + s], ["CD%s%d" % (s, x) for x in range(i, i + n)], 192 * n * GA_C)
+        for i, n in ABS:
+            n = min(n, L - i)
+            act(ab[:, 192 * i:192 * (i + n)], cd[:, 192 * i:192 * (i + n)], ACT.Abs, 128.0, 1.0,
+                ["CD%s%d" % (s, x) for x in range(i, i + n)], ["AB%s%d" % (s, x) for x in range(i, i + n)], 192 * n)
+        if k:
+            mm(pd[:, 0:192], T.PN[:], B("F", s)[:], True, False, ["PN", "F" + s], ["pD" + s], 192)
+        todo = [x for i in ORDER for x in (i, i + 1)] + [14] * t
+        for j, x in enumerate(todo):
+            mm(pd[:, 0:192], T.ZD[:, 15 - x:143 - x], ab[:, 192 * x:192 * x + 192], j == 0 and not k, j == L - 1,
+               ["ZD", "AB%s%d" % (s, x)], ["pD" + s], 192)
+        o = B("pK", s)
+        mm(o[:, 0:12, :], T.ZR[:], z[:, 0:192], True, False, ["ZR", "Z" + s], ["pK" + s], 192)
+        swap4(o, 0, swf, lambda u: T.GA3[:, 12 * st[s] + u:12 * st[s] + 12:2, :], "pK" + s, ["G3" + s, "SWF"], False, 1, 4)
+
+    def select(s, k, t):
+        L = 14 + t
+        last = k == 3
+        thr = 8 if t else 9
+        kt, sc, vi, vj = B("KT", s), B("SC", s), B("VI", s), B("VJ", s)
+        act(B("VAL", s)[:], B("pD", s)[:, 0:192], ACT.Sign, c(thr), -1.0, ["pD" + s, "C%d" % thr], ["VAL" + s], 192)
+        mm(B("pK", s)[:, 0:12, :], T.DW[:], B("VAL", s)[:], False, True, ["DW", "VAL" + s], ["pK" + s], 192)
+        tr(kt[:], B("pK", s)[:, 0:12, :], ["pK" + s], ["KT" + s], 192)
+        V(lambda v: v.tensor_tensor_scan(sc[:], T.R1[:, 0:192], kt[:], 0.0, ALU.mult, ALU.max), ["R1", "KT" + s], ["SC" + s], 192)
+        cp(vi[:], sc[:, 15:192:16], ["SC" + s], ["VI" + s])
+        ts(vj[:], vi[:], 4095, None, ALU.bitwise_and, None, ["VI" + s], ["VJ" + s])
+        cp(T.VL0[:, sl(s)], vj[:], ["VJ" + s], ["VL" + s])
+        vx_lists(s, lambda u: vj[:, u:12:2], "VJ" + s)
+        if last:
+            cp(T.VLF[:, sl(s)], vj[:], ["VJ" + s], ["VLF" + s])
+            ts(T.VXN[:, sl(s)], vj[:], 8.0, None, ALU.add, None, ["VJ" + s], ["VXN" + s])
+        else:
+            o = B("pD", s)[:, 192:384]
+            mm(o, T.TU[:], B("VAL", s)[:], True, k == 0, ["TU", "VAL" + s], ["pD" + s], 192)
+            if k:
+                mm(o, T.ID[:], B("F", s)[:], False, True, ["ID", "F" + s], ["pD" + s], 192)
+            act(B("F", s)[:], o, ACT.Relu, c(10), 1.0, ["pD" + s, "C10"], ["F" + s], 192)
+        if not (last and t):
+            agather(s, not last)
+        xgather(s)
+        zswap(s, False)
+        if last:
+            o = B("pS", s)
+            mm(o[:, 0:12, :], T.NI[:], B("Z", s)[:, 0:192], True, False, ["NI", "Z" + s], ["pS" + s], 192)
+            swap4(o, 0, swb, xv(s), "pS" + s, ["XV" + s, "SWB"], True)
+        zact(s, False, last)
+        if not last:
+            lists(s, L)
+
+    def votes(s, t):
+        act(B("GT", s)[:], B("pS", s)[:, 0:12, :], ACT.Sign, 127.5, 1.0, ["pS" + s], ["GT" + s], 192)
+        mm(B("pK", s)[:, 0:12, :], T.BK[:], B("GT", s)[:], True, True, ["BK", "GT" + s], ["pK" + s], 192)
+        o = B("pZ", s)
+        mm(o[:, 12:24, :], T.ZR[:], B("ZF", s)[:], True, False, ["ZR", "ZF" + s], ["pZ" + s], 192)
+        swap4(o, 12, swb, lambda u: B("ZF", s)[:, u:12:2, :], "pZ" + s, ["ZF" + s, "SWB"], True)
+        zn = "ZN%d" % t
+        act(T[zn][:, sw(s)], o[:, 12:24, :], ACT.Identity, 0.0, 1.0, ["pZ" + s], [zn + s], 192)
+        act(T.VF[:, sw(s)], T.IDT[:].indirect(T.VL0[:, sl(s)]), ACT.Identity, 0.0, 1.0, ["IDT", "VL" + s], ["VF" + s], 192 * GA_C)
+        tr(B("KT", s)[:], B("pK", s)[:, 0:12, :], ["pK" + s], ["KT" + s], 192)
+        ts(T.WT[:, sl(s)], B("KT", s)[:, 0:192:16], 1.0, EPS, ALU.is_lt, ALU.add, ["KT" + s], ["WT" + s])
+        for d in range(2):
+            cp(T.VB[:, 24 * d + 12 * st[s]:24 * d + 12 * st[s] + 12, :], T.VF[:, sw(s)], ["VF" + s], ["VB" + s], 192)
+        if s == "A":
+            cp(T.VB[:, 48:49, :], T.VF[:, 0:16], ["VFA"], ["VBA"])
+        trs = []
+        for q in range(4 * st[s], 4 * st[s] + 4):
+            if q == rank:
+                continue
+            dst = T.cores[q]
+            rid, pid, _e = topo.addr(dst)
+            j = 2 * len(trs)
+            mask = sum(1 << e for e in topo.engines(core, dst)[j:j + 2])
+            trs.append(RemoteDMATransfer(dst_ids=[DstId(rid=rid, pnc=pid)], dma_engine_mask=mask, remote_sem=T.sem["arr%d" % t],
+                                         src=T[zn][:, 48 * q:48 * q + 48], dst=T["RZ%d" % t][:, 48 * rank:48 * rank + 48]))
+        op("G", lambda q: q.remote_dma_fused(trs, local_sem=T.sem.lsem), [zn + s], [], 1.0, "lsem")
+
+    def flips(t):
+        rest, ear, gas, zn = T.pKA, T.pKB, ["GAA", "GAB"], "ZN%d" % t
+        act(T.XW[:], T.XO[:].indirect(T.VXN[:]), ACT.Identity, 0.0, 1.0, XOALL + ["VXNA", "VXNB"], ["XW"], 384 * GA_C)
+        act(T.DX[:], T.XW[:], ACT.Identity, c(13), c(12), ["XW", "C12", "C13"], ["DX"], 384)
+        mm(ear[:, 0:24, :], T.ZR[:], T[zn][:], True, False, ["ZR", zn + "A", zn + "B"], ["pKB"], 384)
+        for b in range(23, -1, -1):
+            e0 = 24 * b
+            ts(T.E[:, e0:e0 + 24, :], T.VB[:, b + 1:b + 25, :], T.VLF[:, b:b + 1], T.WT[:, b:b + 1], ALU.is_equal, ALU.mult,
+               ["VBA", "VBB", "VLFA", "VLFB", "WTA", "WTB"], ["E%d" % b], 192)
+            if b < 23:
+                mm(ear[:, b + 1:24, :], T.BK[:], T.E[:, e0:e0 + 23 - b, :], False, False, ["BK", "E%d" % b], ["pKB"], 368 - 16 * b)
+            mm(rest[:, 0:b + 1, :], T.BK[:], T.E[:, e0 + 23 - b:e0 + 24, :], b == 23, b == 0, ["BK", "E%d" % b], ["pKA"], 16 + 16 * b)
+        for h in (18, 12, 6, 0):
+            tt(T.DG[:, h:h + 6, :], T.E[:, 24 * h + 23:24 * h + 144:24, :], T.TRI[:, h:h + 6, :], ALU.mult,
+               ["E%d" % b for b in range(h, h + 6)] + ["TRI"], ["DG"], 192)
+        act(T.RS[:], rest[:, 0:24, :], ACT.Identity, 0.0, 1.0, ["pKA"], ["RS"], 384)
+        mm(ear[:, 0:24, :], T.BK[:], T.DG[:], False, True, ["BK", "DG"], ["pKB"], 384)
+        tt(T.S3[:], T.DWL[:], T.VLF[:], ALU.subtract, ["DWL", "VLFA", "VLFB"], ["S3"])
+        tt(T.DM[:], ear[:, 0:24, :], T.DIAG[:], ALU.mult, ["pKB", "DIAG"], ["DM"], 384)
+        tt(T.RT[:], ear[:, 0:24, :], T.RS[:], ALU.add, ["pKB", "RS"], ["RT"], 384)
+        V(lambda v: v.tensor_tensor_scan(T.SC2[:], T.R1[:], T.DM[:], 0.0, ALU.mult, ALU.add), ["R1", "DM"], ["SC2"], 384)
+        ts(T.pZA[:, 0:24, :], T.RT[:], 1.0, None, ALU.is_lt, None, ["RT"], ["pZA"], 384)
+        ts(T.S1[:], T.SC2[:, 15:384:16], 0.0, None, ALU.is_gt, None, ["SC2"], ["S1"])
+        tt(T.S2[:], T.S1[:], T.S3[:], ALU.mult, ["S1", "S3"], ["S2"])
+        tt(T.FX[:], T.pZA[:, 0:24, :], T.DX[:], ALU.mult, ["pZA", "DX"], ["FX"], 384)
+        tt(T.S4[:], T.S2[:], T.VLF[:], ALU.add, ["S2", "VLFA", "VLFB"], ["S4"])
+        ts(T.XOFF[:], T.S4[:], 8.0, None, ALU.add, None, ["S4"], ["XOFF"])
+        tt(T.XO[:].indirect(T.XOFF[:]), T.XW[:], T.FX[:], ALU.add, ["XW", "FX", "XOFF"], XOALL, 384 * SC_C)
+        if not t:
+            both("dd", T.XO[:, 8:2056], ["XOb"])
+            cp(T.AOFF[:], T.S4[:], ["S4"], ["AOFF"])
+            act(T.AT[:, 2048:2432], T.GA[:], ACT.Identity, c(14), c(6), gas + ["C6", "C14"], ["ATn"], 384)
+            tt(T.AT[:].indirect(T.AOFF[:]), T.GA[:], T.NEWL[:], ALU.add, gas + ["NEWL", "AOFF"], ["AT", "ATn"], 384 * SC_C)
+
+    def arrivals(t):
+        rz, zn = "RZ%d" % t, "ZN%d" % t
+        op("R", None, [zn + "A", zn + "B"], [rz], 8.0, "arr%d" % t)
+        for ph, pk in ((0, "pSA"), (1, "pSB"), (2, "pZB"))[2 * t:]:
+            for r in range(8):
+                d = (rank - r) % 8
+                if ph == 2:
+                    o = 512 + 128 - 16 * d
+                else:
+                    e = (ph - d) % 2
+                    o = 256 * e + 32 * ((((ph - d) % 8 - e) // 2) % 4)
+                src, keys = (T[zn], [zn + "A", zn + "B"]) if r == rank else (T[rz], [rz])
+                mm(T[pk][:, 3 * r:3 * r + 3, :], T.W3[:, o:o + 128], src[:, 48 * r:48 * r + 48], True, True, ["W3"] + keys, [pk], 64)
+            n = 8 + 2048
+            if t:
+                out, key = T.XM[:], "XM"
+            elif ph == 2:
+                out, key = T.XO[:, n:n + 384], "XOn"
+            else:
+                out, key = T.X2[:, ph * H + n:ph * H + n + 384], "X2n"
+            act(out, T[pk][:, 0:24, :], ACT.Identity, -128.0, 1.0, [pk], [key], 384)
+
+    for t in range(2):
+        for s in "AB":
+            begin(s, 14 + t)
+        for k in range(4):
+            for s in "AB":
+                ahead[0] = AHEAD if s == "A" else 0.0
+                bulk(s, k, t)
+                select(s, k, t)
+        ahead[0] = 0.0
+        for s in "AB":
+            votes(s, t)
+        if t:
+            dma("Y", T.yv[:, :], T.VF[0:128:16, :], "dv", ["VFA", "VFB"], [], 12)
+            arrivals(t)
+        flips(t)
+        if not t:
+            arrivals(t)
+    dma("Y", T.yx[:, 2432:2816], T.XM[:], "dv", ["XM"], [], 96)
+    dma("Y", T.yx[:, 0:2432], T.XO[:, 8:2440], "do", XOALL, [], 620)
+    emit(g, T, schedule(ops))

@@ -4,14 +4,19 @@ from concourse.mybir import AluOpType, ActivationFunctionType
 ALU = AluOpType
 ACT = ActivationFunctionType
 H = 8 + 2816
-NA = 2816 + 384
+NX = H + 2440
 EPS = 2.0 ** -9
-NB = 1
-ABS = ((2, 2), (4, 2), (6, 4), (10, 2), (12, 3))
-ORDER = (2, 4, 0, 6, 8, 10, 12)
-CY, FV, FS, FP, PE, WAKE = 0.83e-3, 0.06, 0.10, 0.04, 0.45e-3, 0.08
+LOW = -2048.0
+PLAN = ((("S", 12, 2), ("A", 2, 2), ("A", 4, 2), ("A", 6, 2), ("A", 8, 2), ("A", 10, 2), ("A", 0, 2)),
+        (("S", 12, 2), ("A", 2, 2), ("A", 4, 2), ("S", 14, 1), ("A", 6, 2), ("A", 8, 2), ("A", 10, 2), ("A", 0, 2)))
+NB = 0
+XE, ZE, GE = "S", "S", "S"
+SAME = 0.18
+CY, FV, FS, FP, PE, WAKE = 0.83e-3, 0.015, 0.04, 0.015, 0.42e-3, 0.19
 GA_C, SC_C = 1.5, 3.5
-AHEAD = 2.2
+AHEAD = 3.5
+BOOST = 6.0
+SLACK = {"V": 0.05, "S": 0.05, "P": 0.03, "G": 0.0, "Y": 0.0, "R": 0.0}
 LOADS = {"dw": 4e3, "dl": 3e3, "dx": 2e3, "dy": 1e3}
 
 SCRATCH = {}
@@ -22,22 +27,23 @@ def _decl(dtype, where="sbuf", **shapes):
         SCRATCH[n] = (where, [128] + sh, dtype)
 
 
-_decl("bfloat16", X2=[2 * H], XO=[8 + NA], XM=[384], W3=[768], ZD=[144], BK=[128], ID=[128], NI=[128], PN=[128], DW=[128],
-      TU=[128], ZR=[128], SWB=[512], R1=[384], DIAG=[24, 16], TRI=[24, 16], E=[576, 16], DG=[24, 16], DX=[384], FX=[384],
-      XV=[384], XW=[384], ZN0=[384], ZN1=[384], RZ0=[384], RZ1=[384])
-_decl("float32", AT=[NA], IDT=[2816], C=[32], Q=[144], QX=[24, 16], QX2=[128], QG=[128], T1=[128], T2=[128], SWF=[512],
-      NEWL=[384], DWL=[24], VLF=[24], WT=[24], VF=[384], DM=[384], SC2=[384], RS=[24, 16], RT=[384], S1=[24], S2=[24], S3=[24],
-      S4=[24], GA=[384], GA3=[24, 16])
-_decl("int32", ATI=[2048], W0I=[24], PI=[8], QW=[768])
-_decl("uint16", VL0=[24], VX0=[24], VXN=[24], VB=[49, 16], AOFF=[24], XOFF=[24])
+_decl("bfloat16", X2=[NX], XM=[384], ZD=[144], Z2=[144], ZN=[144], BK=[128], ID2=[256], NI=[128], TRI=[128], TRL=[128], SWB=[512],
+      BS=[512], LA=[2, 138], LB=[768], EV=[128], IDS=[128], D14=[128], T1=[128], T2=[128], T3=[128], T4=[128],
+      R1=[192], K8=[192], QX=[24, 16], QC=[24, 16], DIAG=[24, 16], UP=[12, 16], E=[576, 16], DG=[24, 16], FL=[384],
+      XN=[384], XV=[384], XW=[384], ZN0=[384], ZN1=[384], RZ0=[384], RZ1=[384])
+_decl("float16", GA=[384], GA3=[24, 16], VB=[24, 16])
+_decl("float32", C=[40], TH=[8], Q=[144], QP=[128], QG=[128], DW0=[384], CAP=[24, 16], VLF=[24], WT=[24],
+      VF=[384], DM=[384], SC2=[384], AS=[384])
+_decl("int32", ATI=[H], W0I=[24], PI=[8])
+_decl("uint16", XOFF=[24], VU=[24, 16])
 for _s in "AB":
-    _decl("bfloat16", **{"CD" + _s: [3072], "AB" + _s: [3072], "XG" + _s: [384], "Z" + _s: [384], "ZF" + _s: [12, 16],
-                         "VAL" + _s: [192], "F" + _s: [192], "GT" + _s: [192]})
-    _decl("float32", **{"LT" + _s: [192], "KT" + _s: [192], "SC" + _s: [192]})
-    _decl("int32", **{"VI" + _s: [12], "VJ" + _s: [12]})
-    _decl("uint16", **{"CL" + _s: [192]})
+    _decl("bfloat16", **{"CD" + _s: [2880], "AB" + _s: [2880], "XG" + _s: [384], "Z" + _s: [384], "ZF" + _s: [12, 16],
+                         "VAL" + _s: [192], "GT" + _s: [12, 16]})
+    _decl("float16", **{"LT" + _s: [192], "R" + _s: [48, 16]})
+    _decl("float32", **{"KT" + _s: [32], "KW" + _s: [32]})
+    _decl("uint16", **{"CL" + _s: [192], "VL" + _s: [24]})
     _decl("float32", "psum", **{"pD" + _s: [512], "pK" + _s: [32, 16], "pZ" + _s: [32, 16], "pS" + _s: [32, 16]})
-SEMAPHORES = ["sv", "ss", "sp", "sg", "dw", "dl", "dx", "dy", "dd", "do", "dv", "dgA", "dgB", "arr0", "arr1", "lsem"]
+SEMAPHORES = ["sv", "ss", "sp", "sg", "dw", "dl", "dx", "dy", "dd", "de", "do", "dv", "dgA", "dgB", "arr0", "arr1", "lsem"]
 
 
 def schedule(ops):
@@ -45,21 +51,23 @@ def schedule(ops):
     for j, o in enumerate(ops):
         p = {}
         for k in o["r"]:
-            if k in lastw:
-                p[lastw[k]] = 0 if k[0] == "p" and ops[lastw[k]]["e"] == o["e"] else 1
+            for x in lastw.get(k, ()):
+                p[x] = 0 if k[0] == "p" and ops[x]["e"] == o["e"] else 1
             if k[0] == "p":
                 for x in readers.get(k, ()):
                     p.setdefault(x, 0 if ops[x]["e"] == o["e"] else 1)
+        group = {}
         for k in o["w"]:
-            for x in ([lastw[k]] if k in lastw else []) + readers.get(k, []):
-                same = ops[x]["e"] == o["e"] or (o["sem"] and ops[x]["sem"] == o["sem"])
-                p.setdefault(x, 0 if same else 1)
+            group[k] = [x for x in lastw.get(k, ()) if o["sem"] and ops[x]["sem"] == o["sem"] and not readers.get(k)]
+            for x in lastw.get(k, []) + readers.get(k, []):
+                if x not in group[k]:
+                    p.setdefault(x, 0 if ops[x]["e"] == o["e"] and not ops[x]["sem"] else 1)
         p.pop(j, None)
         preds.append(p)
         for k in o["r"]:
             readers.setdefault(k, []).append(j)
         for k in o["w"]:
-            lastw[k] = j
+            lastw[k] = group[k] + [j]
             readers[k] = []
     n = len(ops)
     succ = [[] for _ in range(n)]
@@ -68,7 +76,11 @@ def schedule(ops):
             succ[i].append(j)
     bl = [0.0] * n
     for j in range(n - 1, -1, -1):
-        bl[j] = ops[j]["c"] + ops[j]["lat"] + max([bl[x] + WAKE for x in succ[j]] or [0.0])
+        bl[j] = ops[j]["c"] + ops[j]["lat"] + max([bl[x] + (SAME if ops[x]["e"] == ops[j]["e"] else WAKE) for x in succ[j]] or [0.0])
+    lev = [o["lev"] for o in ops]
+    for j in range(n - 1, -1, -1):
+        if lev[j] is None:
+            lev[j] = min([lev[x] for x in succ[j]] or [99])
     left = [len(preds[j]) for j in range(n)]
     base = [0.0] * n
     free, out = {}, []
@@ -76,8 +88,9 @@ def schedule(ops):
     dmaq = 0.0
     while ready:
         st = [max(base[j], free.get(ops[j]["e"], 0.0)) for j in ready]
-        t0 = min(st) + 0.03
-        j = max((bl[x] + ops[x]["first"], -x, x) for x, s in zip(ready, st) if s <= t0)[2]
+        t0 = min(st)
+        e0 = ops[ready[st.index(t0)]]["e"]
+        j = max((-lev[x], bl[x] + ops[x]["first"], -x, x) for x, s in zip(ready, st) if s <= t0 + SLACK[e0] and ops[x]["e"] == e0)[3]
         ready.remove(j)
         o = ops[j]
         s = max(base[j], free.get(o["e"], 0.0))
@@ -87,7 +100,8 @@ def schedule(ops):
             fin = max(dmaq, fin) + o["lat"]
         out.append(o)
         for x in succ[j]:
-            base[x] = max(base[x], fin + WAKE if preds[x][j] else s + o["c"])
+            lag = SAME if ops[x]["e"] == o["e"] and not o["lat"] else WAKE
+            base[x] = max(base[x], fin + lag if preds[x][j] else s + o["c"])
             left[x] -= 1
             if not left[x]:
                 ready.append(x)
@@ -110,11 +124,11 @@ def emit(g, T, ops):
                 need.extend((x, True) for x in readers.get(k, ()))
         for k in w:
             if k in lastw:
-                need.append((lastw[k], True))
-            need.extend((x, True) for x in readers.get(k, ()))
+                need.append((lastw[k], False))
+            need.extend((x, False) for x in readers.get(k, ()))
         mx = {}
-        for (s, c), anti in need:
-            if (s == e and (anti or e == "P")) or s == me:
+        for (s, c), both_read in need:
+            if (s == e and (both_read or e == "P")) or s == me:
                 continue
             if s not in eng:
                 c = cnt[s]
@@ -169,11 +183,11 @@ def rank_program(g, core, T, topo):
     if rank is None:
         return
     ops = []
-    ahead = [0.0]
+    ahead = [None]
 
     def op(e, fn, r, w, c, sem=None, lat=0.0, by=0.0):
         ops.append({"e": e, "fn": fn, "r": list(r), "w": list(w), "c": c, "sem": sem, "lat": lat, "by": by,
-                    "first": ahead[0] + LOADS.get(sem, 0.0)})
+                    "first": LOADS.get(sem, 0.0), "lev": -9 if sem in LOADS else ahead[0]})
 
     def V(fn, r, w, n):
         op("V", fn, r, w, FV + max(64, n) * CY)
@@ -193,9 +207,6 @@ def rank_program(g, core, T, topo):
     def tr(out, in_, r, w, n=64):
         V(lambda v: v.transpose(out, in_), r, w, n)
 
-    def ms(ap, x, w, n=64):
-        V(lambda v: v.memset(ap, x), [], w, n)
-
     def act(out, in_, f, bias, scale, r, w, n):
         op("S", lambda s: s.activation(out, in_, f, bias=bias, scale=scale), r, w, FS + n * CY)
 
@@ -205,236 +216,263 @@ def rank_program(g, core, T, topo):
     def dma(e, out, in_, sem, r, w, kb):
         op(e, lambda q: q.dma_start(out=out, in_=in_), r, w, 0.07, sem, 2.0, kb / 200.0)
 
-    B = lambda n, s: T[n + s]
-    st = {"A": 0, "B": 1}
-
-    dma("Y", T.W0I[:], T.w0[:], "dw", [], ["W0I"], 12)
-    for i in range(8):
-        dma("Y", T.ATI[16 * i:16 * i + 15, :], T.lk[16 * i:16 * i + 15, :], "dl", [], ["ATI"], 120)
-    dma("Y", T.ATI[15:128:16, :], T.nx[:, :], "dl", [], ["ATI"], 64)
-    dma("Y", T.XO[:, 8:2056], T.x0[:, :], "dx", [], ["XOb"], 512)
-
-    def both(sem, src, keys):
-        for i in range(8):
-            o, a = (i % 2) * H + 8, 32 * (i // 2)
-            for par in range(2):
-                dma("Y", T.X2[a + 16 * par:a + 16 * par + 16, o:o + 2048], src[16 * i:16 * i + 16, :], sem, keys, ["X2b"], 64)
-    both("dy", T.x0, [])
-
     def iota(out, pat, base, cm, key, n, flag=True):
         if flag:
             op("G", lambda q: q.iota(out, pat, base, cm, allow_small_or_imprecise_dtypes=True), [], [key], 0.13 + 2 * n * CY)
         else:
             op("G", lambda q: q.iota(out, pat, base, cm), [], [key], 0.13 + 2 * n * CY)
+
+    B = lambda n, s: T[n + s]
+    st = {"A": 0, "B": 1}
+
+    dma("S", T.W0I[:], T.w0[:], "dw", [], ["W0I"], 12)
+    dma("Y", T.ATI[15:128:16, 8:2056], T.nx[:, :], "dl", [], ["AT"], 64)
+    for i in range(8):
+        dma("YS"[i % 2], T.ATI[16 * i:16 * i + 15, 8:2056], T.lk[16 * i:16 * i + 15, :], "dl", [], ["AT"], 120)
+    dma("S", T.X2[:, 8:2056], T.x0[:, :], "dx", [], ["XO"], 512)
+    for i in range(8):
+        a = 16 * (i ^ 1)
+        dma("YS"[i % 2], T.X2[a:a + 16, H + 8:H + 2056], T.x0[16 * i:16 * i + 16, :], "dy", [], ["XT"], 64)
+
     iota(T.PI[:, 0:1], [[1, 1]], 0, 1, "PI", 1, False)
     iota(T.Q[:], [[1, 144]], 0, 0, "Q", 144)
     iota(T.QG[:], [[1, 8], [0, 16]], 0, 0, "QG", 128)
-    iota(T.QX2[:], [[0, 8], [1, 16]], 0, 0, "QX2", 128)
+    iota(T.QP[:], [[0, 8], [1, 16]], 1, 0, "QP", 128)
+    iota(T.QP[:, 15:128:16], [[0, 8]], 0, 0, "QP", 8)
+    iota(T.ATI[:, 0:8], [[0, 8]], 0, 0, "ATp", 8, False)
+    iota(T.X2[:, 0:8], [[0, 8]], 255, 0, "XOp", 8)
+    iota(T.X2[:, 2056:H + 8], [[0, 776]], 255, 0, "XOn", 776)
     iota(T.QX[:], [[0, 24], [1, 16]], 0, 0, "QX", 384)
-    iota(T.DWL[:], [[16, 24]], 2816, 0, "DWL", 24)
-    iota(T.QW[:, 0:256], [[32, 8], [0, 2], [1, 16]], 0, 0, "QW", 256, False)
-    iota(T.QW[:, 256:512], [[32, 8], [0, 2], [1, 16]], 16, 0, "QW", 256, False)
-    iota(T.QW[:, 512:768], [[1, 256]], 0, 0, "QW", 256, False)
-    iota(T.NEWL[:], [[1, 384]], 2049, 0, "NEWL", 384)
-    iota(T.IDT[:], [[1, 2816]], 0, 0, "IDT", 2816)
+    iota(T.QC[:], [[16, 24], [0, 16]], 0, 0, "QC", 384)
+    iota(T.DW0[:], [[1, 384]], 2440, 0, "DW0", 384)
+    iota(T.K8[:], [[0, 192]], 1032, 0, "K8", 192)
+    iota(T.ATI[:, 2440:H], [[0, 384]], 0, 0, "ATd", 384, False)
     c = lambda i: T.C[:, i:i + 1]
-    ms(T.ZR[:], 0.0, ["ZR"])
-    for ph in range(2):
-        ms(T.X2[:, ph * H:ph * H + 8], 255.0, ["X2n"])
-        ms(T.X2[:, ph * H + 2056:ph * H + H], 255.0, ["X2n"], 384)
-    ms(T.XO[:, 0:8], 0.0, ["XOn"])
-    ms(T.XO[:, 2056:8 + NA], 0.0, ["XOn"], 576)
     ts(T.PI[:, 1:2], T.PI[:, 0:1], 4, None, ALU.arith_shift_right, None, ["PI"], ["PI1"])
     ts(T.PI[:, 2:3], T.PI[:, 0:1], 15, None, ALU.bitwise_and, None, ["PI"], ["PI2"])
     ts(T.PI[:, 3:4], T.PI[:, 0:1], 4, 1, ALU.arith_shift_right, ALU.bitwise_and, ["PI"], ["PI3"])
     ts(T.PI[:, 4:5], T.PI[:, 0:1], 1, None, ALU.bitwise_and, None, ["PI"], ["PI4"])
     cp(T.C[:, 0:5], T.PI[:, 0:5], ["PI", "PI1", "PI2", "PI3", "PI4"], ["C0"])
-    for o, i, s1, s2, o0, o1, rr in [
-        (6, 2, 15.0, None, ALU.is_equal, None, []),
-        (7, 2, 14.0, None, ALU.is_equal, None, []),
-        (10, 2, 16.0, -209.0, ALU.mult, ALU.add, []),
-        (20, 4, -1.0, 1.0, ALU.mult, ALU.add, []),
-        (16, 3, 1000.0, c(0), ALU.mult, ALU.add, []),
-        (21, 3, -1000.0, 1000.0, ALU.mult, ALU.add, []),
-        (15, 2, -1.0, c(0), ALU.mult, ALU.add, []),
-        (8, 6, 1.0e6, 69.5, ALU.mult, ALU.add, [6]),
-        (22, 6, -16.0, c(2), ALU.mult, ALU.add, [6]),
-        (14, 6, 1.0, None, ALU.subtract, None, [6]),
-        (23, 6, -1.0, 1.0, ALU.mult, ALU.add, [6]),
-        (12, 20, -2.0, None, ALU.mult, None, [20]),
-        (13, 20, 15.0, None, ALU.mult, None, [20]),
-        (17, 16, 16.0, None, ALU.add, None, [16]),
-        (19, 21, c(0), None, ALU.add, None, [21]),
-        (24, 15, 15.0, None, ALU.add, None, [15]),
-        (9, 7, -1000.0, c(8), ALU.mult, ALU.add, [7, 8]),
-        (11, 22, 2.0, 4096.0, ALU.add, ALU.mult, [22]),
-        (18, 19, -16.0, None, ALU.add, None, [19]),
+    A_, M_, EQ = ALU.add, ALU.mult, ALU.is_equal
+    for o, i, s1, s2, o0, o1 in [
+        (5, 3, float(H), 1032.0, M_, A_),
+        (20, 3, float(-H), 1032.0 + H, M_, A_),
+        (6, 2, 15.0, None, EQ, None),
+        (7, 2, 14.0, None, EQ, None),
+        (15, 2, -1.0, 0, M_, A_),
+        (16, 3, 1000.0, 0, M_, A_),
+        (21, 3, -1000.0, 1000.0, M_, A_),
+        (17, 16, 16.0, None, A_, None),
+        (19, 21, 0, None, A_, None),
+        (18, 19, -16.0, None, A_, None),
+        (24, 15, 15.0, None, A_, None),
+        (23, 6, -1.0, 1.0, M_, A_),
+        (22, 2, 1.0, 23, A_, M_),
+        (10, 22, 2048.0 * (GE == "S"), -32768.0 if GE == "S" else -4096.0, M_, A_),
+        (27, 2, float(NB), 2048.0, ALU.is_lt, M_),
+        (28, 27, 69.5, None, A_, None),
+        (8, 6, 1.0e6, 28, M_, A_),
+        (9, 7, -1.0e6, 8, M_, A_),
+        (11, 2, 1.0, -2048.0, A_, M_),
+        (25, 3, -15.0, 15, M_, A_),
+        (26, 3, -10.0, 15, M_, A_),
+        (12, 4, 7.5, -7.5, M_, A_),
+        (13, 7, 2049.0, 1024.0, M_, A_),
+        (14, 6, 1025.0, -1.0, M_, A_),
+        (31, 3, 999.0, 1, M_, A_),
+        (32, 3, -1001.0, 1000.0, M_, A_),
+        (33, 32, 1, None, A_, None),
     ]:
-        ts(c(o), c(i), s1, s2, o0, o1, ["C0"] + ["C%d" % x for x in rr], ["C%d" % o])
-    cp(T.VL0[:], T.W0I[:], ["W0I"], ["VLA", "VLB"])
+        col = lambda x: c(x) if isinstance(x, int) else x
+        key = lambda x: "C%d" % (x if x > 4 else 0)
+        ts(c(o), c(i), col(s1), col(s2), o0, o1, [key(x) for x in (i, s1, s2) if isinstance(x, int)], [key(o)])
+    for t in range(2):
+        ts(T.TH[:, 4 * t:4 * t + 4], T.Q[:, 0:4], c(11), c(9 - t), M_, A_, ["Q", "C11", "C%d" % (9 - t)], ["TH%d" % t])
+    ID = T.ID2[:, 0:128]
+    Q = T.Q[:, 0:128]
     for j, col in enumerate((16, 17, 18, 19)):
-        ts(T.SWB[:, 128 * j:128 * j + 128], T.Q[:, 0:128], c(col), None, ALU.is_equal, None, ["Q", "C%d" % col], ["SWB"], 128)
+        ts(T.SWB[:, 128 * j:128 * j + 128], Q, c(col), None, EQ, None, ["Q", "C%d" % col], ["SW%d" % j], 128)
+    SW, BSK = ["SW%d" % j for j in range(4)], ["BS%d" % j for j in range(4)]
+    for j in range(4):
+        u, d = j // 2, j % 2
+        ts(T.BS[:, 128 * j:128 * j + 128], T.QG[:], float(-d), c(31 + 2 * u), A_, EQ, ["QG", "C%d" % (31 + 2 * u)], [BSK[j]], 128)
     swb = lambda s, d: T.SWB[:, 128 * (2 * s + d):128 * (2 * s + d) + 128]
-    swf = lambda s, d: T.SWF[:, 128 * (2 * s + d):128 * (2 * s + d) + 128]
-    ts(T.ID[:], T.Q[:, 0:128], c(0), None, ALU.is_equal, None, ["Q", "C0"], ["ID"], 128)
-    ts(T.NI[:], T.Q[:, 0:128], c(0), -1.0, ALU.is_equal, ALU.mult, ["Q", "C0"], ["NI"], 128)
-    ts(T.ZD[:], T.Q[:], c(24), None, ALU.is_equal, None, ["Q", "C24"], ["ZD"], 144)
-    cp(T.SWF[:], T.SWB[:], ["SWB"], ["SWF"], 512)
-    ts(T.DW[:], T.Q[:, 0:128], c(0), c(11), ALU.is_equal, ALU.mult, ["Q", "C0", "C11"], ["DW"], 128)
-    ts(T.PN[:], T.Q[:, 0:128], c(0), 128.0, ALU.is_equal, ALU.mult, ["Q", "C0"], ["PN"], 128)
-    ts(T.BK[:], T.QG[:], c(1), None, ALU.is_equal, None, ["QG", "C0"], ["BK"], 128)
-    ts(T.T1[:], T.QX2[:], c(2), -16.0, ALU.is_lt, ALU.mult, ["QX2", "C0"], ["T1"], 128)
-    ts(T.T2[:], T.T1[:], 1.0, c(23), ALU.add, ALU.mult, ["T1", "C23"], ["T2"], 128)
-    tt(T.TU[:], T.T2[:], T.BK[:], ALU.mult, ["T2", "BK"], ["TU"], 256)
-    ts(T.R1[:], T.QX[:], 0.0, None, ALU.is_gt, None, ["QX"], ["R1"], 384)
-    ms(T.AT[:, 2048:NA], -1.0, ["ATn"], 1152)
-    ts(T.DIAG[:], T.QX[:], c(2), None, ALU.is_equal, None, ["QX", "C0"], ["DIAG"], 384)
-    ts(T.TRI[:], T.QX[:], c(2), None, ALU.is_gt, None, ["QX", "C0"], ["TRI"], 384)
-    ts(T.NEWL[:], T.NEWL[:], c(7), None, ALU.mult, None, ["NEWL", "C7"], ["NEWL"], 384)
-    ts(T.DWL[:], T.DWL[:], c(2), None, ALU.add, None, ["DWL", "C0"], ["DWL"])
-    ts(T.QW[:], T.QW[:], 127, None, ALU.bitwise_and, None, ["QW"], ["QW"], 768)
-    ts(T.W3[:], T.QW[:], c(0), None, ALU.is_equal, None, ["QW", "C0"], ["W3"], 768)
+    bs = lambda s, d: T.BS[:, 128 * (2 * s + d):128 * (2 * s + d) + 128]
+    ts(ID, Q, c(0), None, EQ, None, ["Q", "C0"], ["ID"], 128)
+    act(T.ID2[:, 128:256], ID, ACT.Identity, 0.0, 1.0, ["ID"], ["ID2"], 128)
+    act(T.NI[:], ID, ACT.Identity, 0.0, -1.0, ["ID"], ["NI"], 128)
+    act(T.EV[:], ID, ACT.Identity, 0.0, c(12), ["ID", "C12"], ["EV"], 128)
+    act(T.IDS[:], ID, ACT.Identity, 0.0, 2.0 ** -23, ["ID"], ["IDS"], 128)
+    act(T.D14[:], ID, ACT.Identity, 0.0, c(7), ["ID", "C7"], ["D14"], 128)
+    ts(T.ZD[:], T.Q[:], c(24), None, EQ, None, ["Q", "C24"], ["ZD"], 144)
+    ts(T.BK[:], T.QG[:], c(1), None, EQ, None, ["QG", "C0"], ["BK"], 128)
+    act(T.Z2[:], T.ZD[:], ACT.Identity, 0.0, 2.0, ["ZD"], ["Z2"], 144)
+    act(T.ZN[:], T.ZD[:], ACT.Identity, 0.0, -1.0, ["ZD"], ["ZN"], 144)
+    big = 2048.0 if GE == "S" else 4096.0
+    ts(T.T1[:], T.QP[:], c(22), -big, ALU.is_lt, M_, ["QP", "C22"], ["T1"], 128)
+    act(T.T2[:], ID, ACT.Identity, 0.0, big, ["ID"], ["T2"], 128)
+    tt(T.T3[:], T.T1[:], T.BK[:], M_, ["T1", "BK"], ["T3"], 256)
+    tt(T.TRI[:], T.T3[:], T.T2[:], A_, ["T3", "T2"], ["TRI"], 256)
+    ts(T.T4[:], T.QP[:], c(22), c(23), ALU.is_ge, M_, ["QP", "C22", "C23"], ["T4"], 128)
+    tt(T.TRL[:], T.T4[:], T.BK[:], M_, ["T4", "BK"], ["TRL"], 256)
+    ts(T.LA[:, 0, :], T.Q[:, 0:138], -10.0, c(25), A_, EQ, ["Q", "C25"], ["LA0"], 138)
+    ts(T.LA[:, 1, :], T.Q[:, 0:138], -22.0, c(26), A_, EQ, ["Q", "C26"], ["LA1"], 138)
+    for b in range(6):
+        pk = "pD" + "AB"[b // 3]
+        for j in range(2):
+            o = 10 - (2 - j) * b
+            mm(T[pk][:, 128 * (b % 3):128 * (b % 3) + 128], ID, T.LA[:, j, o:o + 128], j == 0, j == 1, ["ID", "LA%d" % j], [pk], 128)
+    for j in range(2):
+        act(T.LB[:, 384 * j:384 * j + 384], T["pD" + "AB"[j]][:, 0:384], ACT.Identity, 0.0, 1.0, ["pD" + "AB"[j]], ["LB%d" % j], 384)
+    ts(T.R1[:], T.QX[:, 0:12, :], 0.0, None, ALU.is_gt, None, ["QX"], ["R1"], 96)
+    ts(T.DIAG[:], T.QX[:], c(2), 2.0 ** -23, EQ, M_, ["QX", "C0"], ["DIAG"], 192)
+    tt(T.CAP[:], T.DIAG[:], T.DW0[:], M_, ["DIAG", "DW0"], ["CAP"], 768)
+    ts(T.UP[:], T.QX[:, 0:12, :], c(2), None, ALU.is_gt, None, ["QX", "C0"], ["UP"], 96)
 
     sl = lambda s: slice(12 * st[s], 12 * st[s] + 12)
     sw = lambda s: slice(192 * st[s], 192 * st[s] + 192)
-    X2ALL, XOALL = ["X2b", "X2n"], ["XOb", "XOn"]
-
-    def vx_lists(s, src, key):
-        for u in range(2):
-            o = 12 * st[s] + 6 * u
-            ts(T.VX0[:, o:o + 6], src(u), 8.0, None, ALU.add, None, [key], ["VX" + s])
+    XOWN = ["XO", "XOp", "XOn"]
+    xall = lambda t: XOWN + ["XT"] + ["XTn"] * t
+    xwin = lambda t: T.X2[:, 0:H + 2056 + 384 * t]
+    xown = lambda t: T.X2[:, 0:2056 + 384 * t]
 
     for s in "AB":
-        vx_lists(s, lambda u: T.W0I[:, 12 * st[s] + u:12 * st[s] + 12:2], "W0I")
-    cp(T.AT[:, 0:2048], T.ATI[:], ["ATI"], ["AT"], 2048)
+        ts(B("VL", s)[:, 0:12], T.W0I[:, sl(s)], 8.0, None, A_, None, ["W0I"], ["VL" + s])
+        for u in range(2):
+            o = 12 * st[s] + u
+            ts(B("VL", s)[:, 12 + 6 * u:18 + 6 * u], T.W0I[:, o:o + 11:2], 8.0, None, A_, None, ["W0I"], ["VX%s%d" % (s, u)])
 
-    def agather(s, key=True):
-        act(T.GA[:, sw(s)], T.AT[:].indirect(T.VL0[:, sl(s)]), ACT.Identity, 0.0, 1.0, ["AT", "ATn", "VL" + s], ["GA" + s], 192 * GA_C)
+    def agather(s, t, key=True):
+        ts(T.GA[:, sw(s)], T.ATI[:, 0:2056 + 384 * t].indirect(B("VL", s)[:, 0:12]), -1024.0, None, A_, None,
+           ["AT", "ATp", "VL" + s] + ["ATn"] * t, ["GA" + s], 192 * GA_C)
         if key:
-            dma("Y", T.GA3[:, sl(s), :], T.GA[:, sw(s)], "dg" + s, ["GA" + s], ["G3" + s], 96)
+            dma("Y", T.GA3[:, sl(s), :], T.GA[:, sw(s)], "dg" + s, ["GA" + s], ["G3" + s], 48)
 
-    def xgather(s):
-        act(T.XV[:, sw(s)], T.XO[:].indirect(T.VX0[:, sl(s)]), ACT.Identity, 0.0, 1.0, XOALL + ["VX" + s], ["XV" + s], 192 * GA_C)
+    def xgather(s, t):
+        src, r = xown(t).indirect(B("VL", s)[:, 12:24]), XOWN[:2 + t] + ["VX%s0" % s, "VX%s1" % s]
+        if XE == "V":
+            cp(T.XV[:, sw(s)], src, r, ["XV" + s], 192 * GA_C)
+        else:
+            act(T.XV[:, sw(s)], src, ACT.Identity, 0.0, 1.0, r, ["XV" + s], 192 * GA_C)
 
-    def swap4(out, o0, mat, src, key, r, stop, n=1, f=1):
-        k = 0
-        for rep in range(n):
-            for u in range(2):
-                for v in range(2):
-                    k += 1
-                    mm(out[:, o0 + v:o0 + 12:2, :], mat(v, u), src(u), False, stop and k == 4 * n, r, [key], 96 * f)
+    def swap4(out, o0, mat, src, key, r, stop, start=False):
+        for u in range(2):
+            for v in range(2):
+                mm(out[:, o0 + v:o0 + 12:2, :], mat(v, u), src(u), start and u + v == 0, stop and u + v == 2, r, [key], 96)
 
     def xv(s):
         return lambda u: T.XV[:, 192 * st[s] + 96 * u:192 * st[s] + 96 * u + 96]
 
-    def zswap(s, first):
+    def zstep(s, first, final=False):
         o = B("pZ", s)
-        if first:
-            mm(o[:, 0:12, :], T.ZR[:], T.XV[:, sw(s)], True, False, ["ZR", "XV" + s], ["pZ" + s], 192)
-        else:
-            mm(o[:, 0:12, :], T.ID[:], B("Z", s)[:, 0:192], True, False, ["ID", "Z" + s], ["pZ" + s], 192)
-        swap4(o, 0, swb, xv(s), "pZ" + s, ["XV" + s, "SWB"], True, 2 if first else 1)
-
-    def zact(s, first, final=False):
-        bias = 127.75 if first else 63.75
-        src = B("pZ", s)[:, 0:12, :]
+        if not first:
+            mm(o[:, 0:12, :], ID, B("Z", s)[:, 0:192], True, False, ["ID", "Z%s0" % s], ["pZ" + s], 192)
+        swap4(o, 0, swb, xv(s), "pZ" + s, ["XV" + s] + SW, True, first)
         if final:
-            act(B("ZF", s)[:], src, ACT.Identity, bias, 0.5, ["pZ" + s], ["ZF" + s], 192)
-        else:
-            for d in range(2):
-                act(B("Z", s)[:, 192 * d:192 * d + 192], src, ACT.Identity, bias, 0.5, ["pZ" + s], ["Z" + s], 192)
+            q = B("pS", s)
+            mm(q[:, 0:12, :], T.NI[:], B("Z", s)[:, 0:192], True, False, ["NI", "Z%s0" % s], ["pS" + s], 192)
+            swap4(q, 0, swb, xv(s), "pS" + s, ["XV" + s] + SW, True)
+            act(B("ZF", s)[:], o[:, 0:12, :], ACT.Identity, 63.75, 0.5, ["pZ" + s], ["ZF" + s], 192)
+            return
+        bias, scale, z = 128.0 if first else 63.75, 1.0 if first else 0.5, B("Z", s)
+        if ZE == "V":
+            ts(z[:, 0:192], o[:, 0:12, :], scale, bias, M_, A_, ["pZ" + s], ["Z%s0" % s], 192)
+            cp(z[:, 192:384], z[:, 0:192], ["Z%s0" % s], ["Z%s1" % s], 96)
+            return
+        for d in range(2):
+            act(z[:, 192 * d:192 * d + 192], o[:, 0:12, :], ACT.Identity, bias, scale, ["pZ" + s], ["Z%s%d" % (s, d)], 192)
 
     def lists(s, L):
         lt, cl = B("LT", s), B("CL", s)
         for b in range(6):
             o = 192 * st[s] + 32 * b
-            tr(lt[:, b:192:6], T.GA[:, o:o + 32], ["GA" + s], ["LT" + s])
-        for g2 in range(2):
-            ts(cl[:, g2:12 * L:2], lt[:, 96 * g2:96 * g2 + 6 * L], 8.0 + H * g2, None, ALU.add, None, ["LT" + s], ["CL" + s], 90)
+            tr(lt[:, b:192:6], T.GA[:, o:o + 32], ["GA" + s], ["LT%s%d" % (s, b)])
+        for h in range(2):
+            ts(cl[:, h:12 * L:2], lt[:, 96 * h:96 * h + 6 * L], c(20 if h else 5), None, A_, None,
+               ["LT%s%d" % (s, b) for b in range(6)] + ["C20" if h else "C5"], ["CL%s%d" % (s, h)])
 
-    def begin(s, L):
-        agather(s)
-        xgather(s)
-        zswap(s, True)
-        zact(s, True)
-        lists(s, L)
+    def begin(s, t):
+        agather(s, t)
+        xgather(s, t)
+        zstep(s, True)
+        lists(s, 14 + t)
 
     def bulk(s, k, t):
         L = 14 + t
         pd, ab, cd, cl, z = B("pD", s), B("AB", s), B("CD", s), B("CL", s), B("Z", s)
-        for i in range(0, 2 * NB, 2):
-            act(B("XG", s)[:], T.X2[:].indirect(cl[:, 12 * i:12 * i + 24]), ACT.Identity, 0.0, 1.0, X2ALL + ["CL" + s], ["XG" + s], 384 * GA_C)
-            o = B("pS", s)[:, 0:24, :]
-            mm(o, T.ID[:], B("XG", s)[:], True, False, ["ID", "XG" + s], ["pS" + s], 384)
-            mm(o, T.NI[:], z[:], False, True, ["NI", "Z" + s], ["pS" + s], 384)
-            act(ab[:, 192 * i:192 * i + 384], o, ACT.Abs, 128.0, 1.0, ["pS" + s], ["AB%s%d" % (s, i), "AB%s%d" % (s, i + 1)], 384)
-        for i in range(2 * NB, L, 2):
-            n = min(2, L - i)
-            tt(cd[:, 192 * i:192 * (i + n)], T.X2[:].indirect(cl[:, 12 * i:12 * (i + n)]), z[:, 0:192 * n], ALU.subtract,
-               X2ALL + ["CL" + s, "Z" + s], ["CD%s%d" % (s, x) for x in range(i, i + n)], 192 * n * GA_C)
-        for i, n in ABS:
-            n = min(n, L - i)
-            act(ab[:, 192 * i:192 * (i + n)], cd[:, 192 * i:192 * (i + n)], ACT.Abs, 128.0, 1.0,
-                ["CD%s%d" % (s, x) for x in range(i, i + n)], ["AB%s%d" % (s, x) for x in range(i, i + n)], 192 * n)
-        if k:
-            mm(pd[:, 0:192], T.PN[:], B("F", s)[:], True, False, ["PN", "F" + s], ["pD" + s], 192)
-        todo = [x for i in ORDER for x in (i, i + 1)] + [14] * t
-        for j, x in enumerate(todo):
-            mm(pd[:, 0:192], T.ZD[:, 15 - x:143 - x], ab[:, 192 * x:192 * x + 192], j == 0 and not k, j == L - 1,
-               ["ZD", "AB%s%d" % (s, x)], ["pD" + s], 192)
+        zk = lambda n: ["Z%s%d" % (s, d) for d in range(n)]
+        abk = lambda i, n: ["AB%s%d" % (s, x) for x in range(i, i + n)]
+        cdk = lambda i, n: ["CD%s%d" % (s, x) for x in range(i, i + n)]
+        clk = ["CL%s0" % s, "CL%s1" % s]
+        sums = []
+        for mode, i, n in PLAN[t]:
+            if mode != "S":
+                for j in range(i, i + n, 2):
+                    tt(cd[:, 192 * j:192 * j + 384], xwin(t).indirect(cl[:, 12 * j:12 * j + 24]), z[:], ALU.subtract,
+                       xall(t) + clk + zk(2), cdk(j, 2), 384 * GA_C)
+            if mode == "A":
+                act(ab[:, 192 * i:192 * (i + n)], cd[:, 192 * i:192 * (i + n)], ACT.Abs, 128.0, 1.0, cdk(i, n), abk(i, n), 192 * n)
+            if mode == "B":
+                ts(ab[:, 192 * i:192 * (i + n)], cd[:, 192 * i:192 * (i + n)], 128.0, 0.0, A_, ALU.max, cdk(i, n), abk(i, n), 96 * n)
+                sums += [("ZN", cd, x, cdk(x, 1)) for x in range(i, i + n)] + [("Z2", ab, x, abk(x, 1)) for x in range(i, i + n)]
+            else:
+                sums += [("ZD", ab, x, abk(x, 1)) for x in range(i, i + n)]
+            if mode != "S":
+                continue
+            xg, o = B("XG", s)[:, 0:192 * n], B("pS", s)[:, 0:12 * n, :]
+            act(xg, xwin(t).indirect(cl[:, 12 * i:12 * (i + n)]), ACT.Identity, 0.0, 1.0, xall(t) + clk, ["XG" + s], 192 * n * GA_C)
+            mm(o, T.NI[:], z[:, 0:192 * n], True, False, ["NI"] + zk(n), ["pS" + s], 192 * n)
+            mm(o, ID, xg, False, True, ["ID", "XG" + s], ["pS" + s], 192 * n)
+            act(ab[:, 192 * i:192 * (i + n)], o, ACT.Abs, 128.0, 1.0, ["pS" + s], abk(i, n), 192 * n)
+        for j in range(k):
+            mm(pd[:, 0:192], T.TRL[:], B("R", s)[:, 12 * j:12 * j + 12, :], j == 0, False, ["TRL", "R%s%d" % (s, j)], ["pD" + s], 192)
+        for j, (mat, src, x, keys) in enumerate(sums):
+            mm(pd[:, 0:192], T[mat][:, 15 - x:143 - x], src[:, 192 * x:192 * x + 192], j == 0 and not k, j == len(sums) - 1,
+               [mat] + keys, ["pD" + s], 192)
         o = B("pK", s)
-        mm(o[:, 0:12, :], T.ZR[:], z[:, 0:192], True, False, ["ZR", "Z" + s], ["pK" + s], 192)
-        swap4(o, 0, swf, lambda u: T.GA3[:, 12 * st[s] + u:12 * st[s] + 12:2, :], "pK" + s, ["G3" + s, "SWF"], False, 1, 4)
+        swap4(o, 0, swb, lambda u: T.GA3[:, 12 * st[s] + u:12 * st[s] + 12:2, :], "pK" + s, ["G3" + s] + SW, False, True)
 
-    def select(s, k, t):
-        L = 14 + t
+    def turn(s, src, key, out, okey, col):
+        o = B("pD", s)[:, col:col + 32]
+        for b in range(6):
+            mm(o, T.LB[:, 128 * b:128 * b + 128], src[:, 2 * b:2 * b + 2, :], b == 0, b == 5, ["LB0", "LB1", key], ["pD" + s], 64)
+        tr(out[:], o, ["pD" + s], [okey])
+
+    def choose(s, k, t):
         last = k == 3
-        thr = 8 if t else 9
-        kt, sc, vi, vj = B("KT", s), B("SC", s), B("VI", s), B("VJ", s)
-        act(B("VAL", s)[:], B("pD", s)[:, 0:192], ACT.Sign, c(thr), -1.0, ["pD" + s, "C%d" % thr], ["VAL" + s], 192)
-        mm(B("pK", s)[:, 0:12, :], T.DW[:], B("VAL", s)[:], False, True, ["DW", "VAL" + s], ["pK" + s], 192)
-        tr(kt[:], B("pK", s)[:, 0:12, :], ["pK" + s], ["KT" + s], 192)
-        V(lambda v: v.tensor_tensor_scan(sc[:], T.R1[:, 0:192], kt[:], 0.0, ALU.mult, ALU.max), ["R1", "KT" + s], ["SC" + s], 192)
-        cp(vi[:], sc[:, 15:192:16], ["SC" + s], ["VI" + s])
-        ts(vj[:], vi[:], 4095, None, ALU.bitwise_and, None, ["VI" + s], ["VJ" + s])
-        cp(T.VL0[:, sl(s)], vj[:], ["VJ" + s], ["VL" + s])
-        vx_lists(s, lambda u: vj[:, u:12:2], "VJ" + s)
-        if last:
-            cp(T.VLF[:, sl(s)], vj[:], ["VJ" + s], ["VLF" + s])
-            ts(T.VXN[:, sl(s)], vj[:], 8.0, None, ALU.add, None, ["VJ" + s], ["VXN" + s])
+        r, rk, kt = B("R", s)[:, 12 * k:12 * k + 12, :], "R%s%d" % (s, k), B("KT", s)
+        th = T.TH[:, 4 * t + k:4 * t + k + 1]
+        if GE == "V":
+            ts(B("VAL", s)[:], B("pD", s)[:, 0:192], th, None, ALU.is_lt, None, ["pD" + s, "TH%d" % t], ["VAL" + s], 192)
         else:
-            o = B("pD", s)[:, 192:384]
-            mm(o, T.TU[:], B("VAL", s)[:], True, k == 0, ["TU", "VAL" + s], ["pD" + s], 192)
-            if k:
-                mm(o, T.ID[:], B("F", s)[:], False, True, ["ID", "F" + s], ["pD" + s], 192)
-            act(B("F", s)[:], o, ACT.Relu, c(10), 1.0, ["pD" + s, "C10"], ["F" + s], 192)
-        if not (last and t):
-            agather(s, not last)
-        xgather(s)
-        zswap(s, False)
+            act(B("VAL", s)[:], B("pD", s)[:, 0:192], ACT.Sign, th, -1.0, ["pD" + s, "TH%d" % t], ["VAL" + s], 192)
+        mm(B("pK", s)[:, 0:12, :], T.TRI[:], B("VAL", s)[:], False, True, ["TRI", "VAL" + s], ["pK" + s], 192)
+        ts(r, B("pK", s)[:, 0:12, :], c(10), LOW, A_, ALU.max, ["pK" + s, "C10"], [rk], 192)
+        turn(s, r, rk, kt, "KT" + s, 192)
+        ts(B("VL", s)[:], kt[:, 0:24], 31752.0, None, A_, None, ["KT" + s], ["VL" + s, "VX%s0" % s, "VX%s1" % s])
         if last:
-            o = B("pS", s)
-            mm(o[:, 0:12, :], T.NI[:], B("Z", s)[:, 0:192], True, False, ["NI", "Z" + s], ["pS" + s], 192)
-            swap4(o, 0, swb, xv(s), "pS" + s, ["XV" + s, "SWB"], True)
-        zact(s, False, last)
+            ts(T.VLF[:, sl(s)], kt[:, 0:12], 31744.0, None, A_, None, ["KT" + s], ["VLF" + s])
+            o = B("pK", s)
+            swap4(o, 0, bs, lambda u: r[:, u:12:2, :], "pK" + s, [rk] + BSK, True, True)
+            ts(T.VU[:, sl(s), :], o[:, 0:12, :], 31744.0, None, A_, None, ["pK" + s], ["VU" + s], 192)
+            act(T.VB[:, sl(s), :], o[:, 0:12, :], ACT.Identity, 30720.0, 1.0, ["pK" + s], ["VB" + s], 192)
+            if t:
+                act(T.VF[:, sw(s)], o[:, 0:12, :], ACT.Identity, 31744.0, 1.0, ["pK" + s], ["VF" + s], 192)
+        if not (last and t):
+            agather(s, t, not last)
+        xgather(s, t)
+        zstep(s, False, last)
         if not last:
-            lists(s, L)
+            lists(s, 14 + t)
 
     def votes(s, t):
         act(B("GT", s)[:], B("pS", s)[:, 0:12, :], ACT.Sign, 127.5, 1.0, ["pS" + s], ["GT" + s], 192)
-        mm(B("pK", s)[:, 0:12, :], T.BK[:], B("GT", s)[:], True, True, ["BK", "GT" + s], ["pK" + s], 192)
+        turn(s, B("GT", s), "GT" + s, B("KW", s), "KW" + s, 224)
+        ts(T.WT[:, sl(s)], B("KW", s)[:, 0:12], 1.0, EPS, ALU.is_lt, A_, ["KW" + s], ["WT" + s])
         o = B("pZ", s)
-        mm(o[:, 12:24, :], T.ZR[:], B("ZF", s)[:], True, False, ["ZR", "ZF" + s], ["pZ" + s], 192)
-        swap4(o, 12, swb, lambda u: B("ZF", s)[:, u:12:2, :], "pZ" + s, ["ZF" + s, "SWB"], True)
+        swap4(o, 12, swb, lambda u: B("ZF", s)[:, u:12:2, :], "pZ" + s, ["ZF" + s] + SW, True, True)
         zn = "ZN%d" % t
         act(T[zn][:, sw(s)], o[:, 12:24, :], ACT.Identity, 0.0, 1.0, ["pZ" + s], [zn + s], 192)
-        act(T.VF[:, sw(s)], T.IDT[:].indirect(T.VL0[:, sl(s)]), ACT.Identity, 0.0, 1.0, ["IDT", "VL" + s], ["VF" + s], 192 * GA_C)
-        tr(B("KT", s)[:], B("pK", s)[:, 0:12, :], ["pK" + s], ["KT" + s], 192)
-        ts(T.WT[:, sl(s)], B("KT", s)[:, 0:192:16], 1.0, EPS, ALU.is_lt, ALU.add, ["KT" + s], ["WT" + s])
-        for d in range(2):
-            cp(T.VB[:, 24 * d + 12 * st[s]:24 * d + 12 * st[s] + 12, :], T.VF[:, sw(s)], ["VF" + s], ["VB" + s], 192)
-        if s == "A":
-            cp(T.VB[:, 48:49, :], T.VF[:, 0:16], ["VFA"], ["VBA"])
         trs = []
         for q in range(4 * st[s], 4 * st[s] + 4):
             if q == rank:
@@ -448,78 +486,104 @@ def rank_program(g, core, T, topo):
         op("G", lambda q: q.remote_dma_fused(trs, local_sem=T.sem.lsem), [zn + s], [], 1.0, "lsem")
 
     def flips(t):
-        rest, ear, gas, zn = T.pKA, T.pKB, ["GAA", "GAB"], "ZN%d" % t
-        act(T.XW[:], T.XO[:].indirect(T.VXN[:]), ACT.Identity, 0.0, 1.0, XOALL + ["VXNA", "VXNB"], ["XW"], 384 * GA_C)
-        act(T.DX[:], T.XW[:], ACT.Identity, c(13), c(12), ["XW", "C12", "C13"], ["DX"], 384)
-        mm(ear[:, 0:24, :], T.ZR[:], T[zn][:], True, False, ["ZR", zn + "A", zn + "B"], ["pKB"], 384)
-        for b in range(23, -1, -1):
-            e0 = 24 * b
-            ts(T.E[:, e0:e0 + 24, :], T.VB[:, b + 1:b + 25, :], T.VLF[:, b:b + 1], T.WT[:, b:b + 1], ALU.is_equal, ALU.mult,
-               ["VBA", "VBB", "VLFA", "VLFB", "WTA", "WTB"], ["E%d" % b], 192)
-            if b < 23:
-                mm(ear[:, b + 1:24, :], T.BK[:], T.E[:, e0:e0 + 23 - b, :], False, False, ["BK", "E%d" % b], ["pKB"], 368 - 16 * b)
-            mm(rest[:, 0:b + 1, :], T.BK[:], T.E[:, e0 + 23 - b:e0 + 24, :], b == 23, b == 0, ["BK", "E%d" % b], ["pKA"], 16 + 16 * b)
-        for h in (18, 12, 6, 0):
-            tt(T.DG[:, h:h + 6, :], T.E[:, 24 * h + 23:24 * h + 144:24, :], T.TRI[:, h:h + 6, :], ALU.mult,
-               ["E%d" % b for b in range(h, h + 6)] + ["TRI"], ["DG"], 192)
-        act(T.RS[:], rest[:, 0:24, :], ACT.Identity, 0.0, 1.0, ["pKA"], ["RS"], 384)
-        mm(ear[:, 0:24, :], T.BK[:], T.DG[:], False, True, ["BK", "DG"], ["pKB"], 384)
-        tt(T.S3[:], T.DWL[:], T.VLF[:], ALU.subtract, ["DWL", "VLFA", "VLFB"], ["S3"])
-        tt(T.DM[:], ear[:, 0:24, :], T.DIAG[:], ALU.mult, ["pKB", "DIAG"], ["DM"], 384)
-        tt(T.RT[:], ear[:, 0:24, :], T.RS[:], ALU.add, ["pKB", "RS"], ["RT"], 384)
-        V(lambda v: v.tensor_tensor_scan(T.SC2[:], T.R1[:], T.DM[:], 0.0, ALU.mult, ALU.add), ["R1", "DM"], ["SC2"], 384)
-        ts(T.pZA[:, 0:24, :], T.RT[:], 1.0, None, ALU.is_lt, None, ["RT"], ["pZA"], 384)
-        ts(T.S1[:], T.SC2[:, 15:384:16], 0.0, None, ALU.is_gt, None, ["SC2"], ["S1"])
-        tt(T.S2[:], T.S1[:], T.S3[:], ALU.mult, ["S1", "S3"], ["S2"])
-        tt(T.FX[:], T.pZA[:, 0:24, :], T.DX[:], ALU.mult, ["pZA", "DX"], ["FX"], 384)
-        tt(T.S4[:], T.S2[:], T.VLF[:], ALU.add, ["S2", "VLFA", "VLFB"], ["S4"])
-        ts(T.XOFF[:], T.S4[:], 8.0, None, ALU.add, None, ["S4"], ["XOFF"])
-        tt(T.XO[:].indirect(T.XOFF[:]), T.XW[:], T.FX[:], ALU.add, ["XW", "FX", "XOFF"], XOALL, 384 * SC_C)
+        rest, ear, gas, vb = T.pKA, ("pSA", "pKB"), ["GAA", "GAB"], ["VBA", "VBB"]
+        for s in "AB":
+            act(T.XW[:, sw(s)], xown(t).indirect(B("VL", s)[:, 0:12]), ACT.Identity, 0.0, 1.0, XOWN[:2 + t] + ["VL" + s], ["XW" + s], 192 * GA_C)
         if not t:
-            both("dd", T.XO[:, 8:2056], ["XOb"])
-            cp(T.AOFF[:], T.S4[:], ["S4"], ["AOFF"])
-            act(T.AT[:, 2048:2432], T.GA[:], ACT.Identity, c(14), c(6), gas + ["C6", "C14"], ["ATn"], 384)
-            tt(T.AT[:].indirect(T.AOFF[:]), T.GA[:], T.NEWL[:], ALU.add, gas + ["NEWL", "AOFF"], ["AT", "ATn"], 384 * SC_C)
+            o = T.pDA[:, 0:384]
+            mm(o, ID, T.GA[:], True, False, ["ID"] + gas, ["pDA"], 384)
+            mm(o, T.D14[:], T.QC[:], False, False, ["D14", "QC"], ["pDA"], 384)
+            mm(o, T.D14[:], T.QX[:], False, True, ["D14", "QX"], ["pDA"], 384)
+            act(T.AS[:], o, ACT.Identity, c(13), 1.0, ["pDA", "C13"], ["AS"], 384)
+            ts(T.ATI[:, 2056:2440], T.GA[:], c(6), c(14), M_, A_, gas + ["C6", "C14"], ["ATn"], 384)
+
+        def compare(b, c0, c1):
+            e0, s = 24 * b, "AB"[b // 12]
+            key = "E%d.%d" % (b, c0)
+            ts(T.E[:, e0 + c0:e0 + c1, :], T.VU[:, c0:c1, :], T.VLF[:, b:b + 1], T.WT[:, b:b + 1], EQ, M_,
+               ["VU" + x for x in "AB"[c0 // 12:(c1 + 11) // 12]] + ["VLF" + s, "WT" + s], [key], 8 * (c1 - c0))
+            lo = max(c0, b + 1)
+            if lo < c1:
+                h = lo // 12
+                mm(T[ear[h]][:, lo - 12 * h:12, :], T.BK[:], T.E[:, e0 + lo:e0 + c1, :], False, False, ["BK", key], [ear[h]], 16 * (c1 - lo))
+            if c0 <= b:
+                mm(rest[:, 0:b + 1, :], T.BK[:], T.E[:, e0:e0 + b + 1, :], False, b == 23, ["BK", key], ["pKA"], 16 + 16 * b)
+
+        def lowest(h, parts):
+            o, w = T[ear[h]][:, 0:12, :], slice(192 * h, 192 * h + 192)
+            for b0, n in parts:
+                tt(T.DG[:, b0:b0 + n, :], T.E[:, 25 * b0:25 * (b0 + n - 1) + 1:25, :], T.UP[:, 0:n, :], M_,
+                   ["E%d.0" % b for b in range(b0, b0 + n)] + ["UP"], ["DG%d" % b0], 32 * n)
+            mm(o, T.BK[:], T.DG[:, 12 * h:12 * h + 12, :], False, True, ["BK"] + ["DG%d" % b0 for b0, n in parts], [ear[h]], 192)
+            tt(T.DM[:, w], o, T.CAP[:, 12 * h:12 * h + 12, :], ALU.min, [ear[h], "CAP"], ["DM%d" % h], 192)
+            V(lambda v: v.tensor_tensor_scan(T.SC2[:, w], T.R1[:], T.DM[:, w], 0.0, M_, A_), ["R1", "DM%d" % h], ["SC%d" % h], 192)
+            ts(T.XOFF[:, 12 * h:12 * h + 12], T.SC2[:, 192 * h + 15:192 * h + 192:16], 2.0 ** 23, None, M_, None, ["SC%d" % h], ["XOFF%d" % h])
+
+        for h in range(2):
+            o = T[ear[h]][:, 0:12, :]
+            mm(rest[:, 12 * h:12 * h + 12, :], T.IDS[:], T.K8[:], h == 0, False, ["IDS", "K8"], ["pKA"], 192)
+            mm(o, T.IDS[:], T.K8[:], True, False, ["IDS", "K8"], [ear[h]], 192)
+            mm(o, T.IDS[:], T.VB[:, 12 * h:12 * h + 12, :], False, False, ["IDS", vb[h]], [ear[h]], 192)
+        ahead[0] -= 0.5
+        for b in range(12):
+            compare(b, 0, 12)
+        lowest(0, ((0, 12),))
+        ahead[0] += 0.5
+        for b in range(12):
+            compare(b, 12, 24)
+        for b in range(12, 24):
+            compare(b, 0, 24)
+        lowest(1, ((12, 8), (20, 4)))
+        act(T.FL[:], rest[:, 0:24, :], ACT.Sign, 0.875, -1.0, ["pKA"], ["FL"], 384)
+        o = T.pZA[:, 0:24, :]
+        mm(o, ID, T.XW[:], True, False, ["ID", "XWA", "XWB"], ["pZA"], 384)
+        mm(o, T.EV[:], T.FL[:], False, True, ["EV", "FL"], ["pZA"], 384)
+        act(T.XN[:], o, ACT.Abs, c(12), 1.0, ["pZA", "C12"], ["XN"], 384)
+        cp(T.X2[:, 0:H].indirect(T.XOFF[:]), T.XN[:], ["XN", "XOFF0", "XOFF1"], XOWN, 384 * SC_C)
+        if not t:
+            for i in range(8):
+                a, o = 16 * i, 16 * (i ^ 1)
+                dma("YS"[i % 2], T.X2[o:o + 16:2, H + 8:H + 2056], T.X2[a:a + 16:2, 8:2056], "dd", ["XO"], ["XT"], 32)
+            cp(T.ATI[:].indirect(T.XOFF[:]), T.AS[:], ["AS", "XOFF0", "XOFF1"], ["AT", "ATp", "ATn", "ATd"], 384 * SC_C)
 
     def arrivals(t):
         rz, zn = "RZ%d" % t, "ZN%d" % t
-        op("R", None, [zn + "A", zn + "B"], [rz], 8.0, "arr%d" % t)
-        for ph, pk in ((0, "pSA"), (1, "pSB"), (2, "pZB"))[2 * t:]:
-            for r in range(8):
-                d = (rank - r) % 8
-                if ph == 2:
-                    o = 512 + 128 - 16 * d
-                else:
-                    e = (ph - d) % 2
-                    o = 256 * e + 32 * ((((ph - d) % 8 - e) // 2) % 4)
-                src, keys = (T[zn], [zn + "A", zn + "B"]) if r == rank else (T[rz], [rz])
-                mm(T[pk][:, 3 * r:3 * r + 3, :], T.W3[:, o:o + 128], src[:, 48 * r:48 * r + 48], True, True, ["W3"] + keys, [pk], 64)
-            n = 8 + 2048
-            if t:
-                out, key = T.XM[:], "XM"
-            elif ph == 2:
-                out, key = T.XO[:, n:n + 384], "XOn"
-            else:
-                out, key = T.X2[:, ph * H + n:ph * H + n + 384], "X2n"
-            act(out, T[pk][:, 0:24, :], ACT.Identity, -128.0, 1.0, [pk], [key], 384)
+        op("R", None, [zn + "A", zn + "B"], [rz], 6.0, "arr%d" % t)
+        for r in range(8):
+            o = 128 - 16 * ((rank - r) % 8)
+            src, keys = (T[zn], [zn + "A", zn + "B"]) if r == rank else (T[rz], [rz])
+            mm(T.pZB[:, 3 * r:3 * r + 3, :], T.ID2[:, o:o + 128], src[:, 48 * r:48 * r + 48], True, True, ["ID", "ID2"] + keys, ["pZB"], 64)
+        out, key = (T.XM[:], "XM") if t else (T.X2[:, 2056:2440], "XOn")
+        act(out, T.pZB[:, 0:24, :], ACT.Identity, -128.0, 1.0, ["pZB"], [key], 384)
+        if not t:
+            for u in range(2):
+                mm(T.pSB[:, 0:24, :], swb(u, 1 - u), out, u == 0, u == 1, SW + [key], ["pSB"], 384)
+            act(T.X2[:, H + 2056:H + 2440], T.pSB[:, 0:24, :], ACT.Identity, 0.0, 1.0, ["pSB"], ["XTn"], 384)
+
+    def store(first, sem, after=()):
+        dma("Y", T.yx[first:128:2, 0:2432], T.X2[first:128:2, 8:2440], sem, XOWN + list(after), [], 311)
 
     for t in range(2):
         for s in "AB":
-            begin(s, 14 + t)
+            ahead[0] = 10 * t + st[s] - 0.5
+            begin(s, t)
         for k in range(4):
             for s in "AB":
-                ahead[0] = AHEAD if s == "A" else 0.0
+                ahead[0] = 10 * t + 2 * k + st[s]
+                if (t, k, s) == (1, 1, "A"):
+                    store(1, "de", ["RA0"])
                 bulk(s, k, t)
-                select(s, k, t)
-        ahead[0] = 0.0
+                choose(s, k, t)
         for s in "AB":
+            ahead[0] = 10 * t + 6 + st[s]
             votes(s, t)
+        ahead[0] = 10 * t + 8
         if t:
             dma("Y", T.yv[:, :], T.VF[0:128:16, :], "dv", ["VFA", "VFB"], [], 12)
             arrivals(t)
+            dma("Y", T.yx[:, 2432:2816], T.XM[:], "dv", ["XM"], [], 96)
         flips(t)
         if not t:
             arrivals(t)
-    dma("Y", T.yx[:, 2432:2816], T.XM[:], "dv", ["XM"], [], 96)
-    dma("Y", T.yx[:, 0:2432], T.XO[:, 8:2440], "do", XOALL, [], 620)
+    store(0, "do")
     emit(g, T, schedule(ops))

@@ -7,17 +7,25 @@ H = 8 + 2816
 NX = H + 2440
 EPS = 2.0 ** -9
 LOW = -2048.0
-PLAN = ((("S", 12, 2), ("A", 2, 2), ("A", 4, 2), ("A", 6, 2), ("A", 8, 2), ("A", 10, 2), ("A", 0, 2)),
-        (("S", 12, 2), ("A", 2, 2), ("A", 4, 2), ("S", 14, 1), ("A", 6, 2), ("A", 8, 2), ("A", 10, 2), ("A", 0, 2)))
+SS = "ABC"
+NK = 12 // len(SS)
+CW, W = 2 * NK, 32 * NK
+GS = 3
+LP = True
+XB = True
+FLEV = (1.0, 0.0)
+FLAT = False
+PASSES = 4
+PLAN = ((("S", 11, 3), ("A", 0, 3), ("A", 3, 3), ("A", 6, 3), ("A", 9, 2)),
+        (("S", 12, 3), ("A", 0, 3), ("A", 3, 3), ("A", 6, 3), ("A", 9, 3)))
 NB = 0
-XE, ZE, GE = "S", "S", "S"
+XE, ZE, GE = "S", "SV", "S"
 SAME = 0.18
+NEAR = 0.04
 CY, FV, FS, FP, PE, WAKE = 0.83e-3, 0.015, 0.04, 0.015, 0.42e-3, 0.19
 GA_C, SC_C = 1.5, 3.5
-AHEAD = 3.5
-BOOST = 6.0
-SLACK = {"V": 0.05, "S": 0.05, "P": 0.03, "G": 0.0, "Y": 0.0, "R": 0.0}
-LOADS = {"dw": 4e3, "dl": 3e3, "dx": 2e3, "dy": 1e3}
+SLACK = {"V": 0.3, "S": 0.3, "P": 0.3, "G": 0.0, "Y": 0.0, "R": 0.0}
+LOADS = {"dw": 4e3, "dx": 3e3, "dl": 2e3, "dy": 1e3}
 
 SCRATCH = {}
 
@@ -28,22 +36,23 @@ def _decl(dtype, where="sbuf", **shapes):
 
 
 _decl("bfloat16", X2=[NX], XM=[384], ZD=[144], Z2=[144], ZN=[144], BK=[128], ID2=[256], NI=[128], TRI=[128], TRL=[128], SWB=[512],
-      BS=[512], LA=[2, 138], LB=[768], EV=[128], IDS=[128], D14=[128], T1=[128], T2=[128], T3=[128], T4=[128],
-      R1=[192], K8=[192], QX=[24, 16], QC=[24, 16], DIAG=[24, 16], UP=[12, 16], E=[576, 16], DG=[24, 16], FL=[384],
-      XN=[384], XV=[384], XW=[384], ZN0=[384], ZN1=[384], RZ0=[384], RZ1=[384])
+      BS=[512], LA=[2, 138], LB=[128 * NK], EV=[128], IDS=[128], D14=[128], T1=[128], T2=[128], T3=[128], T4=[128], SX=[128],
+      R1=[W], K8=[W], QX=[24, 16], QC=[24, 16], DIAG=[24, 16], UP=[CW, 16], E=[24 * CW, 16], DG=[24, 16], FL=[384], FP=[384],
+      XN=[384], XV=[384], XW=[384], ZN0=[384], ZN1=[384], RZ0=[384], RZ1=[384], OFFS=[W])
 _decl("float16", GA=[384], GA3=[24, 16], VB=[24, 16])
 _decl("float32", C=[40], TH=[8], Q=[144], QP=[128], QG=[128], DW0=[384], CAP=[24, 16], VLF=[24], WT=[24],
-      VF=[384], DM=[384], SC2=[384], AS=[384])
+      VF=[384], DM=[2, 384], SC2=[2, 384], AS=[384], OF0=[W])
 _decl("int32", ATI=[H], W0I=[24], PI=[8])
-_decl("uint16", XOFF=[24], VU=[24, 16])
-for _s in "AB":
-    _decl("bfloat16", **{"CD" + _s: [2880], "AB" + _s: [2880], "XG" + _s: [384], "Z" + _s: [384], "ZF" + _s: [12, 16],
-                         "VAL" + _s: [192], "GT" + _s: [12, 16]})
-    _decl("float16", **{"LT" + _s: [192], "R" + _s: [48, 16]})
+_decl("uint16", XOFF=[24], ROFF=[24], VU=[24, 16])
+for _s in SS:
+    _decl("bfloat16", **{"CD" + _s: [15 * W], "AB" + _s: [15 * W], "XG" + _s: [2, 4 * W], "Z" + _s: [4 * W], "ZF" + _s: [CW, 16],
+                         "VAL" + _s: [W], "GT" + _s: [CW, 16]})
+    _decl("float16", **{"LT" + _s: [W], "R" + _s: [4 * CW, 16]})
     _decl("float32", **{"KT" + _s: [32], "KW" + _s: [32]})
-    _decl("uint16", **{"CL" + _s: [192], "VL" + _s: [24]})
-    _decl("float32", "psum", **{"pD" + _s: [512], "pK" + _s: [32, 16], "pZ" + _s: [32, 16], "pS" + _s: [32, 16]})
-SEMAPHORES = ["sv", "ss", "sp", "sg", "dw", "dl", "dx", "dy", "dd", "de", "do", "dv", "dgA", "dgB", "arr0", "arr1", "lsem"]
+    _decl("uint16", **{"CL" + _s: [W], "VL" + _s: [2 * CW]})
+    _decl("float32", "psum", **{"pD" + _s: [512], "pK" + _s: [32, 16]})
+_decl("float32", "psum", pS0=[32, 16], pS1=[32, 16])
+SEMAPHORES = ["sv", "ss", "sp", "sg", "dw", "dl", "dx", "dy", "dd", "de", "do", "dv", "arr0", "arr1", "lsem"] + ["dg" + _s for _s in SS]
 
 
 def schedule(ops):
@@ -81,31 +90,45 @@ def schedule(ops):
     for j in range(n - 1, -1, -1):
         if lev[j] is None:
             lev[j] = min([lev[x] for x in succ[j]] or [99])
-    left = [len(preds[j]) for j in range(n)]
-    base = [0.0] * n
-    free, out = {}, []
-    ready = [j for j in range(n) if not left[j]]
-    dmaq = 0.0
-    while ready:
-        st = [max(base[j], free.get(ops[j]["e"], 0.0)) for j in ready]
-        t0 = min(st)
-        e0 = ops[ready[st.index(t0)]]["e"]
-        j = max((-lev[x], bl[x] + ops[x]["first"], -x, x) for x, s in zip(ready, st) if s <= t0 + SLACK[e0] and ops[x]["e"] == e0)[3]
-        ready.remove(j)
-        o = ops[j]
-        s = max(base[j], free.get(o["e"], 0.0))
-        fin = free[o["e"]] = s + o["c"]
-        if o["lat"]:
-            dmaq = max(dmaq, fin) + o["by"]
-            fin = max(dmaq, fin) + o["lat"]
-        out.append(o)
-        for x in succ[j]:
-            lag = SAME if ops[x]["e"] == o["e"] and not o["lat"] else WAKE
-            base[x] = max(base[x], fin + lag if preds[x][j] else s + o["c"])
-            left[x] -= 1
-            if not left[x]:
-                ready.append(x)
-    return out
+    lag = lambda i, j: (SAME if ops[i]["e"] == ops[j]["e"] and not ops[i]["lat"] else WAKE) if preds[j][i] else 0.0
+
+    def place(rank, back):
+        after, left = (preds, [len(x) for x in succ]) if back else (succ, [len(x) for x in preds])
+        base, end, free, out, dmaq = [0.0] * n, [0.0] * n, {}, [], 0.0
+        ready = [j for j in range(n) if not left[j]]
+        while ready:
+            st = [max(base[j], free.get(ops[j]["e"], 0.0)) for j in ready]
+            t0 = min(st)
+            e0 = ops[ready[st.index(t0)]]["e"]
+            mine = [(x, s) for x, s in zip(ready, st) if ops[x]["e"] == e0]
+            j = max((x for x, s in mine if s <= t0 + NEAR), key=rank)
+            soon = [(x, s) for x, s in mine if rank(x) > rank(j) and s < t0 + SLACK[e0] * ops[j]["c"]]
+            if soon:
+                k, sk = max(soon, key=lambda a: rank(a[0]))
+                fits = [x for x, s in mine if s + ops[x]["c"] <= sk + NEAR]
+                j = max(fits, key=rank) if fits else k
+            ready.remove(j)
+            o = ops[j]
+            fin = end[j] = free[o["e"]] = max(base[j], free.get(o["e"], 0.0)) + o["c"]
+            if o["lat"] and not back:
+                dmaq = max(dmaq, fin) + o["by"]
+                fin = end[j] = dmaq + o["lat"]
+            out.append(j)
+            for x in after[j]:
+                base[x] = max(base[x], fin + (lag(x, j) + ops[x]["lat"] + ops[x]["by"] if back else lag(j, x)))
+                left[x] -= 1
+                if not left[x]:
+                    base[x] = max(base[x], 0.0)
+                    ready.append(x)
+        return out, end, max(end)
+
+    best = now = place(lambda x: (-lev[x], bl[x] + ops[x]["first"], -x), False)
+    for _ in range(PASSES):
+        fin = now[1]
+        late = place(lambda x: (fin[x], x), True)[1]
+        now = place(lambda x: (late[x] + ops[x]["first"], -x), False)
+        best = min(best, now, key=lambda r: r[2])
+    return [ops[j] for j in best[0]]
 
 
 def emit(g, T, ops):
@@ -183,11 +206,11 @@ def rank_program(g, core, T, topo):
     if rank is None:
         return
     ops = []
-    ahead = [None]
+    level = [None]
 
     def op(e, fn, r, w, c, sem=None, lat=0.0, by=0.0):
         ops.append({"e": e, "fn": fn, "r": list(r), "w": list(w), "c": c, "sem": sem, "lat": lat, "by": by,
-                    "first": LOADS.get(sem, 0.0), "lev": -9 if sem in LOADS else ahead[0]})
+                    "first": LOADS.get(sem, 0.0), "lev": -9 if sem in LOADS else level[0]})
 
     def V(fn, r, w, n):
         op("V", fn, r, w, FV + max(64, n) * CY)
@@ -214,7 +237,7 @@ def rank_program(g, core, T, topo):
         op("P", lambda t: t.matmul(out, lhsT, rhs, start, stop), r, w, FP + max(64, n) * PE)
 
     def dma(e, out, in_, sem, r, w, kb):
-        op(e, lambda q: q.dma_start(out=out, in_=in_), r, w, 0.07, sem, 2.0, kb / 200.0)
+        op(e, lambda q: q.dma_start(out=out, in_=in_), r, w, 0.07, sem, 2.0, kb / 230.0)
 
     def iota(out, pat, base, cm, key, n, flag=True):
         if flag:
@@ -223,16 +246,22 @@ def rank_program(g, core, T, topo):
             op("G", lambda q: q.iota(out, pat, base, cm), [], [key], 0.13 + 2 * n * CY)
 
     B = lambda n, s: T[n + s]
-    st = {"A": 0, "B": 1}
+    st = {s: i for i, s in enumerate(SS)}
+    NS = len(SS)
+    gat = lambda n: 40 + n * GA_C
+    each = lambda k: [k + s for s in SS]
 
     dma("S", T.W0I[:], T.w0[:], "dw", [], ["W0I"], 12)
+    if XB:
+        dma("Y", T.X2[:, 8:2056], T.x0[:, :], "dx", [], ["XO"], 512)
     dma("Y", T.ATI[15:128:16, 8:2056], T.nx[:, :], "dl", [], ["AT"], 64)
     for i in range(8):
-        dma("YS"[i % 2], T.ATI[16 * i:16 * i + 15, 8:2056], T.lk[16 * i:16 * i + 15, :], "dl", [], ["AT"], 120)
-    dma("S", T.X2[:, 8:2056], T.x0[:, :], "dx", [], ["XO"], 512)
-    for i in range(8):
-        a = 16 * (i ^ 1)
-        dma("YS"[i % 2], T.X2[a:a + 16, H + 8:H + 2056], T.x0[16 * i:16 * i + 16, :], "dy", [], ["XT"], 64)
+        dma("SY"[i % 2], T.ATI[16 * i:16 * i + 15, 8:2056], T.lk[16 * i:16 * i + 15, :], "dl", [], ["AT"], 120)
+    if not XB:
+        dma("S", T.X2[:, 8:2056], T.x0[:, :], "dy", [], ["XO"], 512)
+        for i in range(8):
+            a = 16 * (i ^ 1)
+            dma("YS"[i % 2], T.X2[a:a + 16, H + 8:H + 2056], T.x0[16 * i:16 * i + 16, :], "dy", [], ["XT"], 64)
 
     iota(T.PI[:, 0:1], [[1, 1]], 0, 1, "PI", 1, False)
     iota(T.Q[:], [[1, 144]], 0, 0, "Q", 144)
@@ -245,7 +274,7 @@ def rank_program(g, core, T, topo):
     iota(T.QX[:], [[0, 24], [1, 16]], 0, 0, "QX", 384)
     iota(T.QC[:], [[16, 24], [0, 16]], 0, 0, "QC", 384)
     iota(T.DW0[:], [[1, 384]], 2440, 0, "DW0", 384)
-    iota(T.K8[:], [[0, 192]], 1032, 0, "K8", 192)
+    iota(T.K8[:], [[0, W]], 1032, 0, "K8", W)
     iota(T.ATI[:, 2440:H], [[0, 384]], 0, 0, "ATd", 384, False)
     c = lambda i: T.C[:, i:i + 1]
     ts(T.PI[:, 1:2], T.PI[:, 0:1], 4, None, ALU.arith_shift_right, None, ["PI"], ["PI1"])
@@ -275,13 +304,14 @@ def rank_program(g, core, T, topo):
         (9, 7, -1.0e6, 8, M_, A_),
         (11, 2, 1.0, -2048.0, A_, M_),
         (25, 3, -15.0, 15, M_, A_),
-        (26, 3, -10.0, 15, M_, A_),
+        (26, 3, NK - 16.0, 15, M_, A_),
         (12, 4, 7.5, -7.5, M_, A_),
         (13, 7, 2049.0, 1024.0, M_, A_),
         (14, 6, 1025.0, -1.0, M_, A_),
         (31, 3, 999.0, 1, M_, A_),
         (32, 3, -1001.0, 1000.0, M_, A_),
         (33, 32, 1, None, A_, None),
+        (34, 3, -2.0 * H, float(H), M_, A_),
     ]:
         col = lambda x: c(x) if isinstance(x, int) else x
         key = lambda x: "C%d" % (x if x > 4 else 0)
@@ -298,6 +328,7 @@ def rank_program(g, core, T, topo):
         ts(T.BS[:, 128 * j:128 * j + 128], T.QG[:], float(-d), c(31 + 2 * u), A_, EQ, ["QG", "C%d" % (31 + 2 * u)], [BSK[j]], 128)
     swb = lambda s, d: T.SWB[:, 128 * (2 * s + d):128 * (2 * s + d) + 128]
     bs = lambda s, d: T.BS[:, 128 * (2 * s + d):128 * (2 * s + d) + 128]
+    tt(T.SX[:], swb(0, 1), swb(1, 0), A_, SW, ["SX"], 256)
     ts(ID, Q, c(0), None, EQ, None, ["Q", "C0"], ["ID"], 128)
     act(T.ID2[:, 128:256], ID, ACT.Identity, 0.0, 1.0, ["ID"], ["ID2"], 128)
     act(T.NI[:], ID, ACT.Identity, 0.0, -1.0, ["ID"], ["NI"], 128)
@@ -306,8 +337,9 @@ def rank_program(g, core, T, topo):
     act(T.D14[:], ID, ACT.Identity, 0.0, c(7), ["ID", "C7"], ["D14"], 128)
     ts(T.ZD[:], T.Q[:], c(24), None, EQ, None, ["Q", "C24"], ["ZD"], 144)
     ts(T.BK[:], T.QG[:], c(1), None, EQ, None, ["QG", "C0"], ["BK"], 128)
-    act(T.Z2[:], T.ZD[:], ACT.Identity, 0.0, 2.0, ["ZD"], ["Z2"], 144)
-    act(T.ZN[:], T.ZD[:], ACT.Identity, 0.0, -1.0, ["ZD"], ["ZN"], 144)
+    if NB:
+        act(T.Z2[:], T.ZD[:], ACT.Identity, 0.0, 2.0, ["ZD"], ["Z2"], 144)
+        act(T.ZN[:], T.ZD[:], ACT.Identity, 0.0, -1.0, ["ZD"], ["ZN"], 144)
     big = 2048.0 if GE == "S" else 4096.0
     ts(T.T1[:], T.QP[:], c(22), -big, ALU.is_lt, M_, ["QP", "C22"], ["T1"], 128)
     act(T.T2[:], ID, ACT.Identity, 0.0, big, ["ID"], ["T2"], 128)
@@ -316,80 +348,106 @@ def rank_program(g, core, T, topo):
     ts(T.T4[:], T.QP[:], c(22), c(23), ALU.is_ge, M_, ["QP", "C22", "C23"], ["T4"], 128)
     tt(T.TRL[:], T.T4[:], T.BK[:], M_, ["T4", "BK"], ["TRL"], 256)
     ts(T.LA[:, 0, :], T.Q[:, 0:138], -10.0, c(25), A_, EQ, ["Q", "C25"], ["LA0"], 138)
-    ts(T.LA[:, 1, :], T.Q[:, 0:138], -22.0, c(26), A_, EQ, ["Q", "C26"], ["LA1"], 138)
-    for b in range(6):
-        pk = "pD" + "AB"[b // 3]
+    ts(T.LA[:, 1, :], T.Q[:, 0:138], -10.0 - CW, c(26), A_, EQ, ["Q", "C26"], ["LA1"], 138)
+    hk = NK // 2
+    for b in range(NK):
+        pk = "pD" + SS[b // hk]
         for j in range(2):
             o = 10 - (2 - j) * b
-            mm(T[pk][:, 128 * (b % 3):128 * (b % 3) + 128], ID, T.LA[:, j, o:o + 128], j == 0, j == 1, ["ID", "LA%d" % j], [pk], 128)
+            mm(T[pk][:, 128 * (b % hk):128 * (b % hk) + 128], ID, T.LA[:, j, o:o + 128], j == 0, j == 1, ["ID", "LA%d" % j], [pk], 128)
     for j in range(2):
-        act(T.LB[:, 384 * j:384 * j + 384], T["pD" + "AB"[j]][:, 0:384], ACT.Identity, 0.0, 1.0, ["pD" + "AB"[j]], ["LB%d" % j], 384)
-    ts(T.R1[:], T.QX[:, 0:12, :], 0.0, None, ALU.is_gt, None, ["QX"], ["R1"], 96)
+        act(T.LB[:, 128 * hk * j:128 * hk * (j + 1)], T["pD" + SS[j]][:, 0:128 * hk], ACT.Identity, 0.0, 1.0, ["pD" + SS[j]], ["LB%d" % j], 128 * hk)
+    if LP:
+        iota(T.OF0[:], [[0, W // 2], [1, 2]], 0, 0, "OF0", W)
+        ts(T.OFFS[:], T.OF0[:], c(34), c(5), M_, A_, ["OF0", "C34", "C5"], ["OFFS"], W)
+    ts(T.R1[:], T.QX[:, 0:CW, :], 0.0, None, ALU.is_gt, None, ["QX"], ["R1"], W // 2)
     ts(T.DIAG[:], T.QX[:], c(2), 2.0 ** -23, EQ, M_, ["QX", "C0"], ["DIAG"], 192)
     tt(T.CAP[:], T.DIAG[:], T.DW0[:], M_, ["DIAG", "DW0"], ["CAP"], 768)
-    ts(T.UP[:], T.QX[:, 0:12, :], c(2), None, ALU.is_gt, None, ["QX", "C0"], ["UP"], 96)
+    ts(T.UP[:], T.QX[:, 0:CW, :], c(2), None, ALU.is_gt, None, ["QX", "C0"], ["UP"], W // 2)
+    XT = ["XT"]
+    if XB:
+        XT = ["XT%d" % j for j in range(4)]
+        for j in range(4):
+            pk = "pS%d" % (j % 2)
+            mm(T[pk][:], T.SX[:], T.X2[:, 8 + 512 * j:520 + 512 * j], True, True, ["SX", "XO"], [pk], 512)
+            act(T.X2[:, H + 8 + 512 * j:H + 520 + 512 * j], T[pk][:], ACT.Identity, 0.0, 1.0, [pk], [XT[j]], 512)
 
-    sl = lambda s: slice(12 * st[s], 12 * st[s] + 12)
-    sw = lambda s: slice(192 * st[s], 192 * st[s] + 192)
+    sl = lambda s: slice(CW * st[s], CW * st[s] + CW)
+    sw = lambda s: slice(W * st[s], W * st[s] + W)
     XOWN = ["XO", "XOp", "XOn"]
-    xall = lambda t: XOWN + ["XT"] + ["XTn"] * t
+    xall = lambda t: XOWN + XT + ["XTn"] * t
     xwin = lambda t: T.X2[:, 0:H + 2056 + 384 * t]
     xown = lambda t: T.X2[:, 0:2056 + 384 * t]
+    turns = [0]
 
-    for s in "AB":
-        ts(B("VL", s)[:, 0:12], T.W0I[:, sl(s)], 8.0, None, A_, None, ["W0I"], ["VL" + s])
+    def bank():
+        turns[0] += 1
+        return "pS%d" % (turns[0] % 2)
+
+    for s in SS:
+        ts(B("VL", s)[:, 0:CW], T.W0I[:, sl(s)], 8.0, None, A_, None, ["W0I"], ["VL" + s])
         for u in range(2):
-            o = 12 * st[s] + u
-            ts(B("VL", s)[:, 12 + 6 * u:18 + 6 * u], T.W0I[:, o:o + 11:2], 8.0, None, A_, None, ["W0I"], ["VX%s%d" % (s, u)])
+            o = CW * st[s] + u
+            ts(B("VL", s)[:, CW + NK * u:CW + NK * u + NK], T.W0I[:, o:o + CW - 1:2], 8.0, None, A_, None, ["W0I"], ["VX%s%d" % (s, u)])
 
     def agather(s, t, key=True):
-        ts(T.GA[:, sw(s)], T.ATI[:, 0:2056 + 384 * t].indirect(B("VL", s)[:, 0:12]), -1024.0, None, A_, None,
-           ["AT", "ATp", "VL" + s] + ["ATn"] * t, ["GA" + s], 192 * GA_C)
+        ts(T.GA[:, sw(s)], T.ATI[:, 0:2056 + 384 * t].indirect(B("VL", s)[:, 0:CW]), -1024.0, None, A_, None,
+           ["AT", "ATp", "VL" + s] + ["ATn"] * t, ["GA" + s], gat(W))
         if key:
-            dma("Y", T.GA3[:, sl(s), :], T.GA[:, sw(s)], "dg" + s, ["GA" + s], ["G3" + s], 48)
+            dma("Y", T.GA3[:, sl(s), :], T.GA[:, sw(s)], "dg" + s, ["GA" + s], ["G3" + s], W // 4)
 
     def xgather(s, t):
-        src, r = xown(t).indirect(B("VL", s)[:, 12:24]), XOWN[:2 + t] + ["VX%s0" % s, "VX%s1" % s]
+        src, r = xown(t).indirect(B("VL", s)[:, CW:2 * CW]), XOWN[:2 + t] + ["VX%s0" % s, "VX%s1" % s]
         if XE == "V":
-            cp(T.XV[:, sw(s)], src, r, ["XV" + s], 192 * GA_C)
+            cp(T.XV[:, sw(s)], src, r, ["XV" + s], gat(W))
         else:
-            act(T.XV[:, sw(s)], src, ACT.Identity, 0.0, 1.0, r, ["XV" + s], 192 * GA_C)
+            act(T.XV[:, sw(s)], src, ACT.Identity, 0.0, 1.0, r, ["XV" + s], gat(W))
 
     def swap4(out, o0, mat, src, key, r, stop, start=False):
         for u in range(2):
             for v in range(2):
-                mm(out[:, o0 + v:o0 + 12:2, :], mat(v, u), src(u), start and u + v == 0, stop and u + v == 2, r, [key], 96)
+                mm(out[:, o0 + v:o0 + CW:2, :], mat(v, u), src(u), start and u + v == 0, stop and u + v == 2, r, [key], W // 2)
 
     def xv(s):
-        return lambda u: T.XV[:, 192 * st[s] + 96 * u:192 * st[s] + 96 * u + 96]
+        return lambda u: T.XV[:, W * st[s] + W // 2 * u:W * st[s] + W // 2 * (u + 1)]
 
     def zstep(s, first, final=False):
-        o = B("pZ", s)
+        pk, z = "pK" + s, B("Z", s)
+        o = T[pk][:, CW:2 * CW, :]
         if not first:
-            mm(o[:, 0:12, :], ID, B("Z", s)[:, 0:192], True, False, ["ID", "Z%s0" % s], ["pZ" + s], 192)
-        swap4(o, 0, swb, xv(s), "pZ" + s, ["XV" + s] + SW, True, first)
+            mm(o, ID, z[:, 0:W], True, False, ["ID", "Z%s0" % s], [pk], W)
+        swap4(T[pk], CW, swb, xv(s), pk, ["XV" + s] + SW, True, first)
         if final:
-            q = B("pS", s)
-            mm(q[:, 0:12, :], T.NI[:], B("Z", s)[:, 0:192], True, False, ["NI", "Z%s0" % s], ["pS" + s], 192)
-            swap4(q, 0, swb, xv(s), "pS" + s, ["XV" + s] + SW, True)
-            act(B("ZF", s)[:], o[:, 0:12, :], ACT.Identity, 63.75, 0.5, ["pZ" + s], ["ZF" + s], 192)
+            mm(T[pk][:, 0:CW, :], T.NI[:], z[:, 0:W], True, False, ["NI", "Z%s0" % s], [pk], W)
+            swap4(T[pk], 0, swb, xv(s), pk, ["XV" + s] + SW, True)
+            act(B("GT", s)[:], T[pk][:, 0:CW, :], ACT.Sign, 127.5, 1.0, [pk], ["GT" + s], W)
+            act(B("ZF", s)[:], o, ACT.Identity, 63.75, 0.5, [pk], ["ZF" + s], W)
             return
-        bias, scale, z = 128.0 if first else 63.75, 1.0 if first else 0.5, B("Z", s)
-        if ZE == "V":
-            ts(z[:, 0:192], o[:, 0:12, :], scale, bias, M_, A_, ["pZ" + s], ["Z%s0" % s], 192)
-            cp(z[:, 192:384], z[:, 0:192], ["Z%s0" % s], ["Z%s1" % s], 96)
-            return
-        for d in range(2):
-            act(z[:, 192 * d:192 * d + 192], o[:, 0:12, :], ACT.Identity, bias, scale, ["pZ" + s], ["Z%s%d" % (s, d)], 192)
+        bias, scale = 128.0 if first else 63.75, 1.0 if first else 0.5
+        for d in range(GS):
+            if ZE[min(d, len(ZE) - 1)] == "S":
+                act(z[:, W * d:W * d + W], o, ACT.Identity, bias, scale, [pk], ["Z%s%d" % (s, d)], W)
+            elif d:
+                cp(z[:, W * d:W * d + W], z[:, 0:W], ["Z%s0" % s], ["Z%s%d" % (s, d)], W // 2)
+            else:
+                ts(z[:, 0:W], o, scale, bias, M_, A_, [pk], ["Z%s0" % s], W)
 
     def lists(s, L):
         lt, cl = B("LT", s), B("CL", s)
-        for b in range(6):
-            o = 192 * st[s] + 32 * b
-            tr(lt[:, b:192:6], T.GA[:, o:o + 32], ["GA" + s], ["LT%s%d" % (s, b)])
+        if LP:
+            o = B("pD", s)
+            tr(lt[:], T.GA[:, sw(s)], ["GA" + s], ["LT" + s], W)
+            mm(o[:, 256:256 + CW * L], ID, T.OFFS[:, 0:CW * L], True, False, ["ID", "OFFS"], ["pD" + s], CW * L)
+            for j in range(CW):
+                mm(o[:, 256 + j:256 + CW * L:CW], ID, lt[:, 16 * j:16 * j + L], False, j == CW - 1, ["ID", "LT" + s], ["pD" + s], 64)
+            cp(cl[:, 0:CW * L], o[:, 256:256 + CW * L], ["pD" + s], ["CL%s0" % s, "CL%s1" % s], CW * L)
+            return
+        for b in range(NK):
+            o = W * st[s] + 32 * b
+            tr(lt[:, b:W:NK], T.GA[:, o:o + 32], ["GA" + s], ["LT%s%d" % (s, b)])
         for h in range(2):
-            ts(cl[:, h:12 * L:2], lt[:, 96 * h:96 * h + 6 * L], c(20 if h else 5), None, A_, None,
-               ["LT%s%d" % (s, b) for b in range(6)] + ["C20" if h else "C5"], ["CL%s%d" % (s, h)])
+            ts(cl[:, h:CW * L:2], lt[:, W // 2 * h:W // 2 * h + NK * L], c(20 if h else 5), None, A_, None,
+               ["LT%s%d" % (s, b) for b in range(NK)] + ["C20" if h else "C5"], ["CL%s%d" % (s, h)], NK * L)
 
     def begin(s, t):
         agather(s, t)
@@ -398,66 +456,66 @@ def rank_program(g, core, T, topo):
         lists(s, 14 + t)
 
     def bulk(s, k, t):
-        L = 14 + t
         pd, ab, cd, cl, z = B("pD", s), B("AB", s), B("CD", s), B("CL", s), B("Z", s)
         zk = lambda n: ["Z%s%d" % (s, d) for d in range(n)]
         abk = lambda i, n: ["AB%s%d" % (s, x) for x in range(i, i + n)]
         cdk = lambda i, n: ["CD%s%d" % (s, x) for x in range(i, i + n)]
         clk = ["CL%s0" % s, "CL%s1" % s]
-        sums = []
+        sums, ns = [], 0
         for mode, i, n in PLAN[t]:
+            part = slice(W * i, W * (i + n))
             if mode != "S":
-                for j in range(i, i + n, 2):
-                    tt(cd[:, 192 * j:192 * j + 384], xwin(t).indirect(cl[:, 12 * j:12 * j + 24]), z[:], ALU.subtract,
-                       xall(t) + clk + zk(2), cdk(j, 2), 384 * GA_C)
+                for j in range(i, i + n, GS):
+                    m = min(GS, i + n - j)
+                    tt(cd[:, W * j:W * (j + m)], xwin(t).indirect(cl[:, CW * j:CW * (j + m)]), z[:, 0:W * m], ALU.subtract,
+                       xall(t) + clk + zk(m), cdk(j, m), gat(W * m))
             if mode == "A":
-                act(ab[:, 192 * i:192 * (i + n)], cd[:, 192 * i:192 * (i + n)], ACT.Abs, 128.0, 1.0, cdk(i, n), abk(i, n), 192 * n)
+                act(ab[:, part], cd[:, part], ACT.Abs, 128.0, 1.0, cdk(i, n), abk(i, n), W * n)
             if mode == "B":
-                ts(ab[:, 192 * i:192 * (i + n)], cd[:, 192 * i:192 * (i + n)], 128.0, 0.0, A_, ALU.max, cdk(i, n), abk(i, n), 96 * n)
+                ts(ab[:, part], cd[:, part], 128.0, 0.0, A_, ALU.max, cdk(i, n), abk(i, n), W * n // 2)
                 sums += [("ZN", cd, x, cdk(x, 1)) for x in range(i, i + n)] + [("Z2", ab, x, abk(x, 1)) for x in range(i, i + n)]
             else:
                 sums += [("ZD", ab, x, abk(x, 1)) for x in range(i, i + n)]
-            if mode != "S":
-                continue
-            xg, o = B("XG", s)[:, 0:192 * n], B("pS", s)[:, 0:12 * n, :]
-            act(xg, xwin(t).indirect(cl[:, 12 * i:12 * (i + n)]), ACT.Identity, 0.0, 1.0, xall(t) + clk, ["XG" + s], 192 * n * GA_C)
-            mm(o, T.NI[:], z[:, 0:192 * n], True, False, ["NI"] + zk(n), ["pS" + s], 192 * n)
-            mm(o, ID, xg, False, True, ["ID", "XG" + s], ["pS" + s], 192 * n)
-            act(ab[:, 192 * i:192 * (i + n)], o, ACT.Abs, 128.0, 1.0, ["pS" + s], abk(i, n), 192 * n)
+            if mode == "S":
+                q, xk = bank(), "XG%s%d" % (s, ns % 2)
+                xg, o = B("XG", s)[:, ns % 2, 0:W * n], T[q][:, 0:CW * n, :]
+                ns += 1
+                act(xg, xwin(t).indirect(cl[:, CW * i:CW * (i + n)]), ACT.Identity, 0.0, 1.0, xall(t) + clk, [xk], gat(W * n))
+                mm(o, T.NI[:], z[:, 0:W * n], True, False, ["NI"] + zk(n), [q], W * n)
+                mm(o, ID, xg, False, True, ["ID", xk], [q], W * n)
+                act(ab[:, part], o, ACT.Abs, 128.0, 1.0, [q], abk(i, n), W * n)
         for j in range(k):
-            mm(pd[:, 0:192], T.TRL[:], B("R", s)[:, 12 * j:12 * j + 12, :], j == 0, False, ["TRL", "R%s%d" % (s, j)], ["pD" + s], 192)
+            mm(pd[:, 0:W], T.TRL[:], B("R", s)[:, CW * j:CW * j + CW, :], j == 0, False, ["TRL", "R%s%d" % (s, j)], ["pD" + s], W)
         for j, (mat, src, x, keys) in enumerate(sums):
-            mm(pd[:, 0:192], T[mat][:, 15 - x:143 - x], src[:, 192 * x:192 * x + 192], j == 0 and not k, j == len(sums) - 1,
-               [mat] + keys, ["pD" + s], 192)
-        o = B("pK", s)
-        swap4(o, 0, swb, lambda u: T.GA3[:, 12 * st[s] + u:12 * st[s] + 12:2, :], "pK" + s, ["G3" + s] + SW, False, True)
+            mm(pd[:, 0:W], T[mat][:, 15 - x:143 - x], src[:, W * x:W * x + W], j == 0 and not k, j == len(sums) - 1,
+               [mat] + keys, ["pD" + s], W)
+        swap4(B("pK", s), 0, swb, lambda u: T.GA3[:, CW * st[s] + u:CW * st[s] + CW:2, :], "pK" + s, ["G3" + s] + SW, False, True)
 
     def turn(s, src, key, out, okey, col):
         o = B("pD", s)[:, col:col + 32]
-        for b in range(6):
-            mm(o, T.LB[:, 128 * b:128 * b + 128], src[:, 2 * b:2 * b + 2, :], b == 0, b == 5, ["LB0", "LB1", key], ["pD" + s], 64)
+        for b in range(NK):
+            mm(o, T.LB[:, 128 * b:128 * b + 128], src[:, 2 * b:2 * b + 2, :], b == 0, b == NK - 1, ["LB0", "LB1", key], ["pD" + s], 64)
         tr(out[:], o, ["pD" + s], [okey])
 
     def choose(s, k, t):
         last = k == 3
-        r, rk, kt = B("R", s)[:, 12 * k:12 * k + 12, :], "R%s%d" % (s, k), B("KT", s)
-        th = T.TH[:, 4 * t + k:4 * t + k + 1]
+        r, rk, kt, pk = B("R", s)[:, CW * k:CW * k + CW, :], "R%s%d" % (s, k), B("KT", s), "pK" + s
+        th, o = T.TH[:, 4 * t + k:4 * t + k + 1], T[pk][:, 0:CW, :]
         if GE == "V":
-            ts(B("VAL", s)[:], B("pD", s)[:, 0:192], th, None, ALU.is_lt, None, ["pD" + s, "TH%d" % t], ["VAL" + s], 192)
+            ts(B("VAL", s)[:], B("pD", s)[:, 0:W], th, None, ALU.is_lt, None, ["pD" + s, "TH%d" % t], ["VAL" + s], W)
         else:
-            act(B("VAL", s)[:], B("pD", s)[:, 0:192], ACT.Sign, th, -1.0, ["pD" + s, "TH%d" % t], ["VAL" + s], 192)
-        mm(B("pK", s)[:, 0:12, :], T.TRI[:], B("VAL", s)[:], False, True, ["TRI", "VAL" + s], ["pK" + s], 192)
-        ts(r, B("pK", s)[:, 0:12, :], c(10), LOW, A_, ALU.max, ["pK" + s, "C10"], [rk], 192)
+            act(B("VAL", s)[:], B("pD", s)[:, 0:W], ACT.Sign, th, -1.0, ["pD" + s, "TH%d" % t], ["VAL" + s], W)
+        mm(o, T.TRI[:], B("VAL", s)[:], False, True, ["TRI", "VAL" + s], [pk], W)
+        ts(r, o, c(10), LOW, A_, ALU.max, [pk, "C10"], [rk], W)
         turn(s, r, rk, kt, "KT" + s, 192)
-        ts(B("VL", s)[:], kt[:, 0:24], 31752.0, None, A_, None, ["KT" + s], ["VL" + s, "VX%s0" % s, "VX%s1" % s])
+        ts(B("VL", s)[:], kt[:, 0:2 * CW], 31752.0, None, A_, None, ["KT" + s], ["VL" + s, "VX%s0" % s, "VX%s1" % s])
         if last:
-            ts(T.VLF[:, sl(s)], kt[:, 0:12], 31744.0, None, A_, None, ["KT" + s], ["VLF" + s])
-            o = B("pK", s)
-            swap4(o, 0, bs, lambda u: r[:, u:12:2, :], "pK" + s, [rk] + BSK, True, True)
-            ts(T.VU[:, sl(s), :], o[:, 0:12, :], 31744.0, None, A_, None, ["pK" + s], ["VU" + s], 192)
-            act(T.VB[:, sl(s), :], o[:, 0:12, :], ACT.Identity, 30720.0, 1.0, ["pK" + s], ["VB" + s], 192)
+            ts(T.VLF[:, sl(s)], kt[:, 0:CW], 31744.0, None, A_, None, ["KT" + s], ["VLF" + s])
+            swap4(T[pk], 0, bs, lambda u: r[:, u:CW:2, :], pk, [rk] + BSK, True, True)
+            act(T.VB[:, sl(s), :], o, ACT.Identity, 30720.0, 1.0, [pk], ["VB" + s], W)
+            ts(T.VU[:, sl(s), :], T.VB[:, sl(s), :], 1024.0, None, A_, None, ["VB" + s], ["VU" + s], W)
             if t:
-                act(T.VF[:, sw(s)], o[:, 0:12, :], ACT.Identity, 31744.0, 1.0, ["pK" + s], ["VF" + s], 192)
+                act(T.VF[:, sw(s)], T.VB[:, sl(s), :], ACT.Identity, 1024.0, 1.0, ["VB" + s], ["VF" + s], W)
         if not (last and t):
             agather(s, t, not last)
         xgather(s, t)
@@ -466,16 +524,14 @@ def rank_program(g, core, T, topo):
             lists(s, 14 + t)
 
     def votes(s, t):
-        act(B("GT", s)[:], B("pS", s)[:, 0:12, :], ACT.Sign, 127.5, 1.0, ["pS" + s], ["GT" + s], 192)
         turn(s, B("GT", s), "GT" + s, B("KW", s), "KW" + s, 224)
-        ts(T.WT[:, sl(s)], B("KW", s)[:, 0:12], 1.0, EPS, ALU.is_lt, A_, ["KW" + s], ["WT" + s])
-        o = B("pZ", s)
-        swap4(o, 12, swb, lambda u: B("ZF", s)[:, u:12:2, :], "pZ" + s, ["ZF" + s] + SW, True, True)
-        zn = "ZN%d" % t
-        act(T[zn][:, sw(s)], o[:, 12:24, :], ACT.Identity, 0.0, 1.0, ["pZ" + s], [zn + s], 192)
+        ts(T.WT[:, sl(s)], B("KW", s)[:, 0:CW], 1.0, EPS, ALU.is_lt, A_, ["KW" + s], ["WT" + s])
+        pk, zn = "pK" + s, "ZN%d" % t
+        swap4(T[pk], 0, swb, lambda u: B("ZF", s)[:, u:CW:2, :], pk, ["ZF" + s] + SW, True, True)
+        act(T[zn][:, sw(s)], T[pk][:, 0:CW, :], ACT.Identity, 0.0, 1.0, [pk], [zn + s], W)
         trs = []
-        for q in range(4 * st[s], 4 * st[s] + 4):
-            if q == rank:
+        for q in range(8):
+            if q == rank or (48 * q + 47) // W != st[s]:
                 continue
             dst = T.cores[q]
             rid, pid, _e = topo.addr(dst)
@@ -483,103 +539,101 @@ def rank_program(g, core, T, topo):
             mask = sum(1 << e for e in topo.engines(core, dst)[j:j + 2])
             trs.append(RemoteDMATransfer(dst_ids=[DstId(rid=rid, pnc=pid)], dma_engine_mask=mask, remote_sem=T.sem["arr%d" % t],
                                          src=T[zn][:, 48 * q:48 * q + 48], dst=T["RZ%d" % t][:, 48 * rank:48 * rank + 48]))
-        op("G", lambda q: q.remote_dma_fused(trs, local_sem=T.sem.lsem), [zn + s], [], 1.0, "lsem")
+        op("G", lambda q: q.remote_dma_fused(trs, local_sem=T.sem.lsem), [zn + x for x in SS[:st[s] + 1]], [], 1.0, "lsem")
 
     def flips(t):
-        rest, ear, gas, vb = T.pKA, ("pSA", "pKB"), ["GAA", "GAB"], ["VBA", "VBB"]
-        for s in "AB":
-            act(T.XW[:, sw(s)], xown(t).indirect(B("VL", s)[:, 0:12]), ACT.Identity, 0.0, 1.0, XOWN[:2 + t] + ["VL" + s], ["XW" + s], 192 * GA_C)
+        top = level[0]
+        for s in SS:
+            act(T.XW[:, sw(s)], xown(t).indirect(B("VL", s)[:, 0:CW]), ACT.Identity, 0.0, 1.0, XOWN[:2 + t] + ["VL" + s], ["XW" + s], gat(W))
         if not t:
-            o = T.pDA[:, 0:384]
-            mm(o, ID, T.GA[:], True, False, ["ID"] + gas, ["pDA"], 384)
-            mm(o, T.D14[:], T.QC[:], False, False, ["D14", "QC"], ["pDA"], 384)
-            mm(o, T.D14[:], T.QX[:], False, True, ["D14", "QX"], ["pDA"], 384)
-            act(T.AS[:], o, ACT.Identity, c(13), 1.0, ["pDA", "C13"], ["AS"], 384)
-            ts(T.ATI[:, 2056:2440], T.GA[:], c(6), c(14), M_, A_, gas + ["C6", "C14"], ["ATn"], 384)
+            o = T.pS1[:, 0:24, :]
+            mm(o, T.D14[:], T.QC[:], True, False, ["D14", "QC"], ["pS1"], 384)
+            mm(o, T.D14[:], T.QX[:], False, False, ["D14", "QX"], ["pS1"], 384)
+            mm(o, ID, T.GA[:], False, True, ["ID"] + each("GA"), ["pS1"], 384)
+            act(T.AS[:], o, ACT.Identity, c(13), 1.0, ["pS1", "C13"], ["AS"], 384)
+            ts(T.ATI[:, 2056:2440], T.GA[:], c(6), c(14), M_, A_, each("GA") + ["C6", "C14"], ["ATn"], 384)
 
-        def compare(b, c0, c1):
-            e0, s = 24 * b, "AB"[b // 12]
-            key = "E%d.%d" % (b, c0)
-            ts(T.E[:, e0 + c0:e0 + c1, :], T.VU[:, c0:c1, :], T.VLF[:, b:b + 1], T.WT[:, b:b + 1], EQ, M_,
-               ["VU" + x for x in "AB"[c0 // 12:(c1 + 11) // 12]] + ["VLF" + s, "WT" + s], [key], 8 * (c1 - c0))
-            lo = max(c0, b + 1)
-            if lo < c1:
-                h = lo // 12
-                mm(T[ear[h]][:, lo - 12 * h:12, :], T.BK[:], T.E[:, e0 + lo:e0 + c1, :], False, False, ["BK", key], [ear[h]], 16 * (c1 - lo))
-            if c0 <= b:
-                mm(rest[:, 0:b + 1, :], T.BK[:], T.E[:, e0:e0 + b + 1, :], False, b == 23, ["BK", key], ["pKA"], 16 + 16 * b)
+        def listed(s, j, out, key):
+            w, pd, dm, sc = sw(s), "pD" + s, T.DM[:, j, sw(s)], T.SC2[:, j, sw(s)]
+            tt(dm, T[pd][:, 256 + W * j:256 + W * j + W], T.CAP[:, sl(s), :], ALU.min, [pd, "CAP"], ["DM" + key + s], W)
+            V(lambda v: v.tensor_tensor_scan(sc, T.R1[:], dm, 0.0, M_, A_), ["R1", "DM" + key + s], ["SC" + key + s], W)
+            ts(out[:, sl(s)], T.SC2[:, j, w.start + 15:w.stop:16], 2.0 ** 23, None, M_, None, ["SC" + key + s], [key + s])
 
-        def lowest(h, parts):
-            o, w = T[ear[h]][:, 0:12, :], slice(192 * h, 192 * h + 192)
-            for b0, n in parts:
-                tt(T.DG[:, b0:b0 + n, :], T.E[:, 25 * b0:25 * (b0 + n - 1) + 1:25, :], T.UP[:, 0:n, :], M_,
-                   ["E%d.0" % b for b in range(b0, b0 + n)] + ["UP"], ["DG%d" % b0], 32 * n)
-            mm(o, T.BK[:], T.DG[:, 12 * h:12 * h + 12, :], False, True, ["BK"] + ["DG%d" % b0 for b0, n in parts], [ear[h]], 192)
-            tt(T.DM[:, w], o, T.CAP[:, 12 * h:12 * h + 12, :], ALU.min, [ear[h], "CAP"], ["DM%d" % h], 192)
-            V(lambda v: v.tensor_tensor_scan(T.SC2[:, w], T.R1[:], T.DM[:, w], 0.0, M_, A_), ["R1", "DM%d" % h], ["SC%d" % h], 192)
-            ts(T.XOFF[:, 12 * h:12 * h + 12], T.SC2[:, 192 * h + 15:192 * h + 192:16], 2.0 ** 23, None, M_, None, ["SC%d" % h], ["XOFF%d" % h])
-
-        for h in range(2):
-            o = T[ear[h]][:, 0:12, :]
-            mm(rest[:, 12 * h:12 * h + 12, :], T.IDS[:], T.K8[:], h == 0, False, ["IDS", "K8"], ["pKA"], 192)
-            mm(o, T.IDS[:], T.K8[:], True, False, ["IDS", "K8"], [ear[h]], 192)
-            mm(o, T.IDS[:], T.VB[:, 12 * h:12 * h + 12, :], False, False, ["IDS", vb[h]], [ear[h]], 192)
-        ahead[0] -= 0.5
-        for b in range(12):
-            compare(b, 0, 12)
-        lowest(0, ((0, 12),))
-        ahead[0] += 0.5
-        for b in range(12):
-            compare(b, 12, 24)
-        for b in range(12, 24):
-            compare(b, 0, 24)
-        lowest(1, ((12, 8), (20, 4)))
-        act(T.FL[:], rest[:, 0:24, :], ACT.Sign, 0.875, -1.0, ["pKA"], ["FL"], 384)
-        o = T.pZA[:, 0:24, :]
-        mm(o, ID, T.XW[:], True, False, ["ID", "XWA", "XWB"], ["pZA"], 384)
-        mm(o, T.EV[:], T.FL[:], False, True, ["EV", "FL"], ["pZA"], 384)
-        act(T.XN[:], o, ACT.Abs, c(12), 1.0, ["pZA", "C12"], ["XN"], 384)
-        cp(T.X2[:, 0:H].indirect(T.XOFF[:]), T.XN[:], ["XN", "XOFF0", "XOFF1"], XOWN, 384 * SC_C)
+        for h, s in enumerate(SS):
+            level[0] = top - FLEV[0] + FLEV[1] * h
+            pd, pk, w, bl = "pD" + s, "pK" + s, sw(s), sl(s)
+            two = h < NS - 1
+            ears, rest, e0 = [T[pd][:, 256 + W * j:256 + W * j + W] for j in range(1 + two)], T[pk][:, 2 * CW:3 * CW, :], CW * CW * h
+            for j, ear in enumerate(ears):
+                mm(ear, T.IDS[:], T.K8[:], j == 0, False, ["IDS", "K8"], [pd], W)
+                mm(ear, T.IDS[:], T.VB[:, bl, :], False, False, ["IDS", "VB" + s], [pd], W)
+            for b in range(CW - 1, -1, -1):
+                e, key, n = e0 + CW * b, "E%s%d" % (s, b), CW * h + b
+                ts(T.E[:, e:e + CW, :], T.VU[:, bl, :], T.VLF[:, n:n + 1], T.WT[:, n:n + 1], EQ, M_, ["VU" + s, "VLF" + s, "WT" + s], [key], W // 2)
+                mm(rest[:, 0:b + 1, :], T.BK[:], T.E[:, e:e + b + 1, :], b == CW - 1, b == 0, ["BK", key], [pk], 16 + 16 * b)
+                for ear in ears if b < CW - 1 else ():
+                    mm(ear[:, 16 * b + 16:W], T.BK[:], T.E[:, e + b + 1:e + CW, :], False, False, ["BK", key], [pd], W - 16 - 16 * b)
+            tt(T.DG[:, bl, :], T.E[:, e0:e0 + CW * CW:CW + 1, :], T.UP[:], M_, ["E%s%d" % (s, b) for b in range(CW)] + ["UP"], ["DG" + s], 2 * W)
+            act(T.FL[:, w], rest, ACT.Sign, 0.875, -1.0, [pk], ["FL" + s], W)
+            if two:
+                act(T.FP[:, w], rest, ACT.Relu, 0.875, -1.0, [pk], ["FP" + s], W)
+                mm(ears[1], ID, T.FP[:, w], False, False, ["ID", "FP" + s], [pd], W)
+            for j, ear in enumerate(ears):
+                mm(ear, T.BK[:], T.DG[:, bl, :], False, j == two, ["BK", "DG" + s], [pd], W)
+            listed(s, 0, T.XOFF, "XOFF")
+            if two:
+                listed(s, 1, T.ROFF, "ROFF")
+            o = T[pk][:, 3 * CW:4 * CW, :]
+            mm(o, ID, T.XW[:, w], True, False, ["ID", "XW" + s], [pk], W)
+            mm(o, T.EV[:], T.FL[:, w], False, True, ["EV", "FL" + s], [pk], W)
+            act(T.XN[:, w], o, ACT.Abs, c(12), 1.0, [pk, "C12"], ["XN" + s], W)
+        for h, s in enumerate(SS):
+            level[0] = top - FLEV[0] + FLEV[1] * h
+            cp(T.X2[:, 0:H].indirect(T.XOFF[:, sl(s)]), T.XN[:, sw(s)], ["XN" + s, "XOFF" + s], XOWN, 40 + W * SC_C)
+        for s in SS[:-1]:
+            cp(T.X2[:, 0:H].indirect(T.ROFF[:, sl(s)]), T.XW[:, sw(s)], ["XW" + s, "ROFF" + s], XOWN, 40 + W * SC_C)
+        level[0] = top
         if not t:
             for i in range(8):
                 a, o = 16 * i, 16 * (i ^ 1)
-                dma("YS"[i % 2], T.X2[o:o + 16:2, H + 8:H + 2056], T.X2[a:a + 16:2, 8:2056], "dd", ["XO"], ["XT"], 32)
-            cp(T.ATI[:].indirect(T.XOFF[:]), T.AS[:], ["AS", "XOFF0", "XOFF1"], ["AT", "ATp", "ATn", "ATd"], 384 * SC_C)
+                dma("YS"[i % 2], T.X2[o:o + 16:2, H + 8:H + 2056], T.X2[a:a + 16:2, 8:2056], "dd", ["XO"], XT, 32)
+            for s in SS[::-1]:
+                cp(T.ATI[:].indirect(T.XOFF[:, sl(s)]), T.AS[:, sw(s)], ["AS", "XO", "XOFF" + s], ["AT", "ATp", "ATn", "ATd"], 40 + W * SC_C)
 
     def arrivals(t):
-        rz, zn = "RZ%d" % t, "ZN%d" % t
-        op("R", None, [zn + "A", zn + "B"], [rz], 6.0, "arr%d" % t)
+        rz, zn, pk = "RZ%d" % t, "ZN%d" % t, "pS0"
+        op("R", None, each(zn), [rz], 4.0, "arr%d" % t)
         for r in range(8):
             o = 128 - 16 * ((rank - r) % 8)
-            src, keys = (T[zn], [zn + "A", zn + "B"]) if r == rank else (T[rz], [rz])
-            mm(T.pZB[:, 3 * r:3 * r + 3, :], T.ID2[:, o:o + 128], src[:, 48 * r:48 * r + 48], True, True, ["ID", "ID2"] + keys, ["pZB"], 64)
+            src, keys = (T[zn], each(zn)) if r == rank else (T[rz], [rz])
+            mm(T[pk][:, 3 * r:3 * r + 3, :], T.ID2[:, o:o + 128], src[:, 48 * r:48 * r + 48], True, True, ["ID", "ID2"] + keys, [pk], 64)
         out, key = (T.XM[:], "XM") if t else (T.X2[:, 2056:2440], "XOn")
-        act(out, T.pZB[:, 0:24, :], ACT.Identity, -128.0, 1.0, ["pZB"], [key], 384)
+        act(out, T[pk][:, 0:24, :], ACT.Identity, -128.0, 1.0, [pk], [key], 384)
         if not t:
-            for u in range(2):
-                mm(T.pSB[:, 0:24, :], swb(u, 1 - u), out, u == 0, u == 1, SW + [key], ["pSB"], 384)
-            act(T.X2[:, H + 2056:H + 2440], T.pSB[:, 0:24, :], ACT.Identity, 0.0, 1.0, ["pSB"], ["XTn"], 384)
+            mm(T.pS1[:, 0:24, :], T.SX[:], out, True, True, ["SX", key], ["pS1"], 384)
+            act(T.X2[:, H + 2056:H + 2440], T.pS1[:, 0:24, :], ACT.Identity, 0.0, 1.0, ["pS1"], ["XTn"], 384)
 
     def store(first, sem, after=()):
         dma("Y", T.yx[first:128:2, 0:2432], T.X2[first:128:2, 8:2440], sem, XOWN + list(after), [], 311)
 
     for t in range(2):
-        for s in "AB":
-            ahead[0] = 10 * t + st[s] - 0.5
+        for s in SS:
+            level[0] = 20 * t + st[s] - 0.5
             begin(s, t)
         for k in range(4):
-            for s in "AB":
-                ahead[0] = 10 * t + 2 * k + st[s]
-                if (t, k, s) == (1, 1, "A"):
-                    store(1, "de", ["RA0"])
+            for s in SS:
+                level[0] = 20 * t + NS * k + st[s]
+                if (t, k, s) == (1, 1, SS[0]):
+                    store(1, "de", ["R%s0" % s])
                 bulk(s, k, t)
+                if k == 3 and FLAT:
+                    level[0] = 20 * t + 4 * NS - 1
                 choose(s, k, t)
-        for s in "AB":
-            ahead[0] = 10 * t + 6 + st[s]
-            votes(s, t)
-        ahead[0] = 10 * t + 8
+                if k == 3:
+                    votes(s, t)
+        level[0] = 20 * t + 4 * NS
         if t:
-            dma("Y", T.yv[:, :], T.VF[0:128:16, :], "dv", ["VFA", "VFB"], [], 12)
+            dma("Y", T.yv[:, :], T.VF[0:128:16, :], "dv", each("VF"), [], 12)
             arrivals(t)
             dma("Y", T.yx[:, 2432:2816], T.XM[:], "dv", ["XM"], [], 96)
         flips(t)

@@ -1,10 +1,15 @@
+import numpy as np
 from concourse.bass import DstId, RemoteDMATransfer
 from concourse.mybir import AluOpType, ActivationFunctionType
 
 ALU = AluOpType
 ACT = ActivationFunctionType
-H = 8 + 2816
-NX = H + 2440
+P0 = 272
+N0 = P0 + 2048
+H = N0 + 384
+NX = 2 * H
+RE = ((2, 2, 2), (8, 4, 4))
+EARLY = ""
 EPS = 2.0 ** -9
 LOW = -2048.0
 SS = "ABC"
@@ -16,16 +21,39 @@ XB = True
 FLEV = (1.0, 0.0)
 FLAT = False
 PASSES = 4
+XPE = 0
+RLAT = 3.0
+HEAVY = ()
+XE2 = "V"
+DLAT = 2.0
+BW = 300.0
+OE = "VSVS"
+BE = "VSSSVV"
+OTHER = "ABC"
+COPY = "P"
+POLISH = 4000
+HEAT = 0.0
+SETTINGS = ((1.0, 1.5, 3.5, 0.18, 0.19, 0.8, 1.0), (1.2, 1.15, 2.5, 0.12, 0.15, 0.6, 0.8), (1.3, 1.9, 5.0, 0.2, 0.3, 1.0, 1.2))
+ORDER = {}
 PLAN = ((("S", 11, 3), ("A", 0, 3), ("A", 3, 3), ("A", 6, 3), ("A", 9, 2)),
         (("S", 12, 3), ("A", 0, 3), ("A", 3, 3), ("A", 6, 3), ("A", 9, 3)))
 NB = 0
-XE, ZE, GE = "S", "SV", "S"
+ZE = "SGG"
+GE = ("V", "S")
 SAME = 0.18
 NEAR = 0.04
 CY, FV, FS, FP, PE, WAKE = 0.83e-3, 0.015, 0.04, 0.015, 0.42e-3, 0.19
 GA_C, SC_C = 1.5, 3.5
 SLACK = {"V": 0.3, "S": 0.3, "P": 0.3, "G": 0.0, "Y": 0.0, "R": 0.0}
-LOADS = {"dw": 4e3, "dx": 3e3, "dl": 2e3, "dy": 1e3}
+NXL = 1
+Z2E = "V"
+KWB = True
+OFF2 = False
+LB_ = "S"
+GF = ""
+FTN = 400
+XFIRST = 3e3
+LOADS = {"dw": 4e3, "dl": 2e3, "dx0": XFIRST, "dx1": XFIRST - 100, "dx2": XFIRST - 200, "dx3": XFIRST - 300}
 
 SCRATCH = {}
 
@@ -36,26 +64,28 @@ def _decl(dtype, where="sbuf", **shapes):
 
 
 _decl("bfloat16", X2=[NX], XM=[384], ZD=[144], Z2=[144], ZN=[144], BK=[128], ID2=[256], NI=[128], TRI=[128], TRL=[128], SWB=[512],
-      BS=[512], LA=[2, 138], LB=[128 * NK], EV=[128], IDS=[128], D14=[128], T1=[128], T2=[128], T3=[128], T4=[128], SX=[128],
-      R1=[W], K8=[W], QX=[24, 16], QC=[24, 16], DIAG=[24, 16], UP=[CW, 16], E=[24 * CW, 16], DG=[24, 16], FL=[384], FP=[384],
-      XN=[384], XV=[384], XW=[384], ZN0=[384], ZN1=[384], RZ0=[384], RZ1=[384], OFFS=[W])
-_decl("float16", GA=[384], GA3=[24, 16], VB=[24, 16])
-_decl("float32", C=[40], TH=[8], Q=[144], QP=[128], QG=[128], DW0=[384], CAP=[24, 16], VLF=[24], WT=[24],
-      VF=[384], DM=[2, 384], SC2=[2, 384], AS=[384], OF0=[W])
-_decl("int32", ATI=[H], W0I=[24], PI=[8])
-_decl("uint16", XOFF=[24], ROFF=[24], VU=[24, 16])
+      BS=[512], LA=[2, 138], LB=[128 * NK], EV=[128], IDS=[128], D14=[128], T1=[128], T2=[128], Q=[144], QG=[128], SX=[128],
+      QX=[24, 16], QC=[24, 16], DIAG=[W], QX8=[W], E=[48 * CW, 16], FL=[384], TRS=[128], EVX=[128], K30=[32], UZ=[64],
+      XN=[3, 2 * W], XV=[384], XW=[384], FG=[384], ZN0=[384], ZN1=[384], RZ0=[384], RZ1=[384], B14=[128], FT1=[H])
+_decl("float16", LG=[384], GA=[384], GA3=[24, 16], VB=[384], QW=[384], KD=[W], OFFS=[W], DMX=[CW, 16], SC=[384])
+_decl("float32", C=[40], TH=[8], DW0=[W], DMF=[W], WT=[24],
+      VF=[384], DM=[384], AS=[384], OF0=[W])
+_decl("int32", FT0=[N0], IDT=[H], ATI=[H], W0I=[24], PI=[8])
+_decl("uint16", XOFF=[24], XOF2=[24], VL=[3, 2 * CW])
 for _s in SS:
     _decl("bfloat16", **{"CD" + _s: [15 * W], "AB" + _s: [15 * W], "XG" + _s: [2, 4 * W], "Z" + _s: [4 * W], "ZF" + _s: [CW, 16],
                          "VAL" + _s: [W], "GT" + _s: [CW, 16]})
     _decl("float16", **{"LT" + _s: [W], "R" + _s: [4 * CW, 16]})
-    _decl("float32", **{"KT" + _s: [32], "KW" + _s: [32]})
-    _decl("uint16", **{"CL" + _s: [W], "VL" + _s: [2 * CW]})
+    _decl("float32", **{"KT" + _s: [32], "KW" + _s: [W]})
+    _decl("uint16", **{"CL" + _s: [W]})
     _decl("float32", "psum", **{"pD" + _s: [512], "pK" + _s: [32, 16]})
 _decl("float32", "psum", pS0=[32, 16], pS1=[32, 16])
-SEMAPHORES = ["sv", "ss", "sp", "sg", "dw", "dl", "dx", "dy", "dd", "de", "do", "dv", "arr0", "arr1", "lsem"] + ["dg" + _s for _s in SS]
+SEMAPHORES = ["sv", "ss", "sp", "sg", "dw", "dl", "dx0", "dx1", "dx2", "dx3", "dd", "da", "de0", "de1", "do", "dv", "arr0", "arr1", "lsem"] + ["dg" + _s for _s in SS]
 
 
 def schedule(ops):
+    if len(ops) in ORDER:
+        return [ops[j] for j in ORDER[len(ops)]]
     preds, lastw, readers = [], {}, {}
     for j, o in enumerate(ops):
         p = {}
@@ -70,7 +100,7 @@ def schedule(ops):
             group[k] = [x for x in lastw.get(k, ()) if o["sem"] and ops[x]["sem"] == o["sem"] and not readers.get(k)]
             for x in lastw.get(k, []) + readers.get(k, []):
                 if x not in group[k]:
-                    p.setdefault(x, 0 if ops[x]["e"] == o["e"] and not ops[x]["sem"] else 1)
+                    p.setdefault(x, 0 if ops[x]["e"] == o["e"] == "P" else 1)
         p.pop(j, None)
         preds.append(p)
         for k in o["r"]:
@@ -128,10 +158,72 @@ def schedule(ops):
         late = place(lambda x: (fin[x], x), True)[1]
         now = place(lambda x: (late[x] + ops[x]["first"], -x), False)
         best = min(best, now, key=lambda r: r[2])
-    return [ops[j] for j in best[0]]
+    ORDER[n] = polish(ops, preds, succ, best[0])
+    return [ops[j] for j in ORDER[n]]
 
 
-def emit(g, T, ops):
+def polish(ops, preds, succ, order):
+    n = len(ops)
+    eng = [o["e"] for o in ops]
+    sets = []
+    for f, ga, sc, same, wake, dl, bw in SETTINGS:
+        cost = [o["c"] if o["sem"] else f * (o["c"] + CY * (o["ng"] * (ga - GA_C) + o["ns"] * (sc - SC_C))) for o in ops]
+        pl = [[(i, (same if eng[i] == eng[j] and not ops[i]["lat"] else wake) if k else 0.0) for i, k in preds[j].items()] for j in range(n)]
+        sets.append((cost, pl, [o["lat"] * dl for o in ops], [o["by"] * bw for o in ops]))
+
+    def run(seq, st):
+        cost, pl, lat, by = st
+        end, why, free, last, dmaq = [0.0] * n, [-1] * n, {}, {}, 0.0
+        for j in seq:
+            e = eng[j]
+            t, w = free.get(e, 0.0), last.get(e, -1)
+            for i, g in pl[j]:
+                if end[i] + g > t:
+                    t, w = end[i] + g, i
+            t += cost[j]
+            free[e], last[e], why[j] = t, j, w
+            if lat[j]:
+                dmaq = max(dmaq, t) + by[j]
+                t = dmaq + lat[j]
+            end[j] = t
+        return max(end), end, why
+
+    rng = np.random.default_rng(1)
+    base = [run(order, st)[0] for st in sets]
+    score = lambda rs: sum(r[0] / b for r, b in zip(rs, base))
+    now = [run(order, st) for st in sets]
+    best, keep, pairs = score(now), order, None
+    for it in range(POLISH):
+        if pairs is None:
+            pos = {j: p for p, j in enumerate(order)}
+            pairs = []
+            for r in now:
+                j = r[1].index(r[0])
+                while r[2][j] >= 0:
+                    i = r[2][j]
+                    if eng[i] == eng[j] and i not in preds[j]:
+                        pairs.append((i, j))
+                    j = i
+        u, v = pairs[int(rng.integers(len(pairs)))]
+        a, b = pos[u], pos[v]
+        mid = order[a + 1:b]
+        up, down = {v}, {u}
+        for x in reversed(mid):
+            if any(y in up for y in succ[x]) or (eng[x] != eng[v] and any(eng[y] == eng[x] for y in up)):
+                up.add(x)
+        if any(y in up for y in succ[u]):
+            continue
+        new = order[:a] + [x for x in mid if x in up] + [v, u] + [x for x in mid if x not in up] + order[b + 1:]
+        res = [run(new, st) for st in sets]
+        s = score(res)
+        if s < score(now) + HEAT * (1.0 - it / POLISH) * rng.random():
+            order, now, pairs = new, res, None
+            if s < best:
+                best, keep = s, new
+    return keep
+
+
+def emit(g, T, ops, sent):
     eng = {"V": g.vector, "S": g.scalar, "P": g.tensor, "G": g, "Y": g.sync}
     sem = {"V": "sv", "S": "ss", "P": "sp", "G": "sg"}
     cnt = {}
@@ -171,9 +263,9 @@ def emit(g, T, ops):
     for o in ops:
         e, r, w = o["e"], o["r"], o["w"]
         if e == "R":
-            cnt[o["sem"]] = 14
+            cnt[o["sem"]] = o["fn"]
             for k in w:
-                lastw[k] = (o["sem"], 14)
+                lastw[k] = (o["sem"], o["fn"])
             continue
         wait_for(e, r, w, o["sem"])
         if o["sem"] == "lsem":
@@ -198,18 +290,19 @@ def emit(g, T, ops):
     for s, c in sorted(cnt.items()):
         if know["G"].get(s, 0) < c:
             g.wait_ge(T.sem[sem.get(s, s)], c)
-    g.wait_ge(T.sem.lsem, 28)
+    g.wait_ge(T.sem.lsem, sent)
 
 
 def rank_program(g, core, T, topo):
     rank = T.rank_of(core)
     if rank is None:
         return
-    ops = []
+    ops, moved = [], {}
     level = [None]
 
     def op(e, fn, r, w, c, sem=None, lat=0.0, by=0.0):
         ops.append({"e": e, "fn": fn, "r": list(r), "w": list(w), "c": c, "sem": sem, "lat": lat, "by": by,
+                    "ng": moved.pop("g", 0), "ns": moved.pop("s", 0),
                     "first": LOADS.get(sem, 0.0), "lev": -9 if sem in LOADS else level[0]})
 
     def V(fn, r, w, n):
@@ -237,45 +330,56 @@ def rank_program(g, core, T, topo):
         op("P", lambda t: t.matmul(out, lhsT, rhs, start, stop), r, w, FP + max(64, n) * PE)
 
     def dma(e, out, in_, sem, r, w, kb):
-        op(e, lambda q: q.dma_start(out=out, in_=in_), r, w, 0.07, sem, 2.0, kb / 230.0)
+        op(e, lambda q: q.dma_start(out=out, in_=in_), r, w, 0.07, sem, DLAT, kb / BW)
 
-    def iota(out, pat, base, cm, key, n, flag=True):
+    def iota(out, pat, base, cm, key, n, flag=True, after=()):
         if flag:
-            op("G", lambda q: q.iota(out, pat, base, cm, allow_small_or_imprecise_dtypes=True), [], [key], 0.13 + 2 * n * CY)
+            op("G", lambda q: q.iota(out, pat, base, cm, allow_small_or_imprecise_dtypes=True), after, [key], 0.13 + 2 * n * CY)
         else:
-            op("G", lambda q: q.iota(out, pat, base, cm), [], [key], 0.13 + 2 * n * CY)
+            op("G", lambda q: q.iota(out, pat, base, cm), after, [key], 0.13 + 2 * n * CY)
 
     B = lambda n, s: T[n + s]
     st = {s: i for i, s in enumerate(SS)}
     NS = len(SS)
-    gat = lambda n: 40 + n * GA_C
+    gat = lambda n: 40 + moved.setdefault("g", n) * GA_C
+    sca = lambda: 40 + moved.setdefault("s", W) * SC_C
     each = lambda k: [k + s for s in SS]
 
     dma("S", T.W0I[:], T.w0[:], "dw", [], ["W0I"], 12)
-    if XB:
-        dma("Y", T.X2[:, 8:2056], T.x0[:, :], "dx", [], ["XO"], 512)
-    dma("Y", T.ATI[15:128:16, 8:2056], T.nx[:, :], "dl", [], ["AT"], 64)
-    for i in range(8):
-        dma("SY"[i % 2], T.ATI[16 * i:16 * i + 15, 8:2056], T.lk[16 * i:16 * i + 15, :], "dl", [], ["AT"], 120)
-    if not XB:
-        dma("S", T.X2[:, 8:2056], T.x0[:, :], "dy", [], ["XO"], 512)
-        for i in range(8):
-            a = 16 * (i ^ 1)
-            dma("YS"[i % 2], T.X2[a:a + 16, H + 8:H + 2056], T.x0[16 * i:16 * i + 16, :], "dy", [], ["XT"], 64)
+    XO = ["XO%d" % j for j in range(4)]
+    for j in range(NXL):
+        n = 2048 // NXL
+        dma("YS"[j % 2], T.X2[:, P0 + n * j:P0 + n * j + n], T.x0[:, n * j:n * j + n], "dx%d" % j, [], XO[4 * j // NXL:4 * (j + 1) // NXL], n // 4)
+    dma("Y", T.ATI[15:128:16, P0:N0], T.nx[:, :], "dl", [], ["AT"], 64)
+    for i in range(4):
+        a = slice(2 ** i - 1, 128, 2 ** (i + 1))
+        dma("SY"[i % 2], T.ATI[a, P0:N0], T.lk[a, :], "dl", [], ["AT"], 512 >> i)
 
     iota(T.PI[:, 0:1], [[1, 1]], 0, 1, "PI", 1, False)
     iota(T.Q[:], [[1, 144]], 0, 0, "Q", 144)
     iota(T.QG[:], [[1, 8], [0, 16]], 0, 0, "QG", 128)
-    iota(T.QP[:], [[0, 8], [1, 16]], 1, 0, "QP", 128)
-    iota(T.QP[:, 15:128:16], [[0, 8]], 0, 0, "QP", 8)
-    iota(T.ATI[:, 0:8], [[0, 8]], 0, 0, "ATp", 8, False)
-    iota(T.X2[:, 0:8], [[0, 8]], 255, 0, "XOp", 8)
-    iota(T.X2[:, 2056:H + 8], [[0, 776]], 255, 0, "XOn", 776)
-    iota(T.QX[:], [[0, 24], [1, 16]], 0, 0, "QX", 384)
-    iota(T.QC[:], [[16, 24], [0, 16]], 0, 0, "QC", 384)
-    iota(T.DW0[:], [[1, 384]], 2440, 0, "DW0", 384)
-    iota(T.K8[:], [[0, W]], 1032, 0, "K8", W)
-    iota(T.ATI[:, 2440:H], [[0, 384]], 0, 0, "ATd", 384, False)
+    V(lambda v: v.memset(T.ATI[:, 0:P0], 0), [], ["ATp"], P0)
+    V(lambda v: v.memset(T.X2[:, 0:P0], 255.0), [], ["XOp"], P0 // 2)
+    V(lambda v: v.memset(T.X2[:, N0:H + P0], 255.0), [], ["XOn", "XTp"], (384 + P0) // 2)
+    V(lambda v: v.memset(T.DMF[:], 4096.0), [], ["DMF"], W)
+    iota(T.QX8[:], [[0, CW], [1, 16]], 0, 0, "QX8", W)
+    iota(T.DW0[:], [[2, W]], 2178 + P0, 0, "DW0", W)
+    if XPE:
+        iota(T.UZ[:], [[0, 64]], 0, 0, "UZ", 64)
+    iota(T.K30[:], [[0, 32]], 30720, 0, "K30", 32)
+    FTK = [[], [], []]
+
+    def late(t):
+        after = ["G3" + SS[0]]
+        if not t:
+            FTK[2].append("IDT")
+            iota(T.IDT[:], [[1, H]], -P0 - 1024, 0, "IDT", H, False, ["TRI", "TRL", "TRS", "B14"])
+            op("G", lambda q: q.affine_select(T.QW[:], T.IDT[:, P0 + 1024:P0 + 1408], [[0, 384]], ALU.is_ge, 0.0, 0, 0), after + ["IDT"], ["QW"], 0.17 + 768 * CY)
+        for a in range(0, N0 + 384 * t, FTN):
+            n = min(FTN, N0 + 384 * t - a)
+            FTK[t].append("FT%d%d" % (t, a))
+            iota(T["FT%d" % t][:, a:a + n], [[0, n]], 2 * t - 1, 0, FTK[t][-1], n, t == 1, after)
+
     c = lambda i: T.C[:, i:i + 1]
     ts(T.PI[:, 1:2], T.PI[:, 0:1], 4, None, ALU.arith_shift_right, None, ["PI"], ["PI1"])
     ts(T.PI[:, 2:3], T.PI[:, 0:1], 15, None, ALU.bitwise_and, None, ["PI"], ["PI2"])
@@ -284,34 +388,30 @@ def rank_program(g, core, T, topo):
     cp(T.C[:, 0:5], T.PI[:, 0:5], ["PI", "PI1", "PI2", "PI3", "PI4"], ["C0"])
     A_, M_, EQ = ALU.add, ALU.mult, ALU.is_equal
     for o, i, s1, s2, o0, o1 in [
-        (5, 3, float(H), 1032.0, M_, A_),
-        (20, 3, float(-H), 1032.0 + H, M_, A_),
+        (5, 3, float(H), 1024.0 + P0, M_, A_),
         (6, 2, 15.0, None, EQ, None),
         (7, 2, 14.0, None, EQ, None),
         (15, 2, -1.0, 0, M_, A_),
         (16, 3, 1000.0, 0, M_, A_),
-        (21, 3, -1000.0, 1000.0, M_, A_),
-        (17, 16, 16.0, None, A_, None),
-        (19, 21, 0, None, A_, None),
-        (18, 19, -16.0, None, A_, None),
-        (24, 15, 15.0, None, A_, None),
-        (23, 6, -1.0, 1.0, M_, A_),
+        (19, 3, -1000.0, 0, M_, A_),
+        (17, 3, -32.0, 0, M_, A_),
+        (23, 6, 2048.0, -2048.0, M_, A_),
         (22, 2, 1.0, 23, A_, M_),
-        (10, 22, 2048.0 * (GE == "S"), -32768.0 if GE == "S" else -4096.0, M_, A_),
-        (27, 2, float(NB), 2048.0, ALU.is_lt, M_),
-        (28, 27, 69.5, None, A_, None),
-        (8, 6, 1.0e6, 28, M_, A_),
+        (10, 22, -1.0, -32768.0, M_, A_),
+        (8, 6, 1.0e6, 69.5, M_, A_),
         (9, 7, -1.0e6, 8, M_, A_),
         (11, 2, 1.0, -2048.0, A_, M_),
         (25, 3, -15.0, 15, M_, A_),
         (26, 3, NK - 16.0, 15, M_, A_),
         (12, 4, 7.5, -7.5, M_, A_),
-        (13, 7, 2049.0, 1024.0, M_, A_),
+        (20, 12, -128.0, None, A_, None),
+        (13, 7, 2048.0, None, M_, None),
+        (36, 7, 1025.0, None, M_, None),
+        (21, 7, -1.0, 1.0, M_, A_),
         (14, 6, 1025.0, -1.0, M_, A_),
-        (31, 3, 999.0, 1, M_, A_),
-        (32, 3, -1001.0, 1000.0, M_, A_),
-        (33, 32, 1, None, A_, None),
         (34, 3, -2.0 * H, float(H), M_, A_),
+        (35, 3, float(-H), 1024.0 + P0 + H, M_, A_),
+        (39, 2, -2.0, 254.0 - 1024 - P0, M_, A_),
     ]:
         col = lambda x: c(x) if isinstance(x, int) else x
         key = lambda x: "C%d" % (x if x > 4 else 0)
@@ -320,35 +420,39 @@ def rank_program(g, core, T, topo):
         ts(T.TH[:, 4 * t:4 * t + 4], T.Q[:, 0:4], c(11), c(9 - t), M_, A_, ["Q", "C11", "C%d" % (9 - t)], ["TH%d" % t])
     ID = T.ID2[:, 0:128]
     Q = T.Q[:, 0:128]
-    for j, col in enumerate((16, 17, 18, 19)):
-        ts(T.SWB[:, 128 * j:128 * j + 128], Q, c(col), None, EQ, None, ["Q", "C%d" % col], ["SW%d" % j], 128)
     SW, BSK = ["SW%d" % j for j in range(4)], ["BS%d" % j for j in range(4)]
     for j in range(4):
         u, d = j // 2, j % 2
-        ts(T.BS[:, 128 * j:128 * j + 128], T.QG[:], float(-d), c(31 + 2 * u), A_, EQ, ["QG", "C%d" % (31 + 2 * u)], [BSK[j]], 128)
+        ts(T.SWB[:, 128 * j:128 * j + 128], Q, 16.0 * (u - d) - 1000.0 * u, c(16 + 3 * u), A_, EQ, ["Q", "C%d" % (16 + 3 * u)], [SW[j]])
     swb = lambda s, d: T.SWB[:, 128 * (2 * s + d):128 * (2 * s + d) + 128]
     bs = lambda s, d: T.BS[:, 128 * (2 * s + d):128 * (2 * s + d) + 128]
-    tt(T.SX[:], swb(0, 1), swb(1, 0), A_, SW, ["SX"], 256)
-    ts(ID, Q, c(0), None, EQ, None, ["Q", "C0"], ["ID"], 128)
+    ts(T.SX[:], Q, -16.0, c(17), A_, EQ, ["Q", "C17"], ["SX"])
+    ts(ID, Q, c(0), None, EQ, None, ["Q", "C0"], ["ID"])
     act(T.ID2[:, 128:256], ID, ACT.Identity, 0.0, 1.0, ["ID"], ["ID2"], 128)
     act(T.NI[:], ID, ACT.Identity, 0.0, -1.0, ["ID"], ["NI"], 128)
     act(T.EV[:], ID, ACT.Identity, 0.0, c(12), ["ID", "C12"], ["EV"], 128)
-    act(T.IDS[:], ID, ACT.Identity, 0.0, 2.0 ** -23, ["ID"], ["IDS"], 128)
+    act(T.EVX[:], T.SX[:], ACT.Identity, 0.0, c(12), ["SX", "C12"], ["EVX"], 128)
+    for m in ("EV", "EVX"):
+        act(T[m][:, 14:128:16], T[m][:, 12:128:16], ACT.Identity, 0.0, 1.0, [m], [m], 8)
+    act(T.IDS[:], ID, ACT.Identity, 0.0, -2.0 ** -23, ["ID"], ["IDS"], 128)
     act(T.D14[:], ID, ACT.Identity, 0.0, c(7), ["ID", "C7"], ["D14"], 128)
-    ts(T.ZD[:], T.Q[:], c(24), None, EQ, None, ["Q", "C24"], ["ZD"], 144)
-    ts(T.BK[:], T.QG[:], c(1), None, EQ, None, ["QG", "C0"], ["BK"], 128)
-    if NB:
-        act(T.Z2[:], T.ZD[:], ACT.Identity, 0.0, 2.0, ["ZD"], ["Z2"], 144)
-        act(T.ZN[:], T.ZD[:], ACT.Identity, 0.0, -1.0, ["ZD"], ["ZN"], 144)
-    big = 2048.0 if GE == "S" else 4096.0
-    ts(T.T1[:], T.QP[:], c(22), -big, ALU.is_lt, M_, ["QP", "C22"], ["T1"], 128)
-    act(T.T2[:], ID, ACT.Identity, 0.0, big, ["ID"], ["T2"], 128)
-    tt(T.T3[:], T.T1[:], T.BK[:], M_, ["T1", "BK"], ["T3"], 256)
-    tt(T.TRI[:], T.T3[:], T.T2[:], A_, ["T3", "T2"], ["TRI"], 256)
-    ts(T.T4[:], T.QP[:], c(22), c(23), ALU.is_ge, M_, ["QP", "C22", "C23"], ["T4"], 128)
-    tt(T.TRL[:], T.T4[:], T.BK[:], M_, ["T4", "BK"], ["TRL"], 256)
-    ts(T.LA[:, 0, :], T.Q[:, 0:138], -10.0, c(25), A_, EQ, ["Q", "C25"], ["LA0"], 138)
-    ts(T.LA[:, 1, :], T.Q[:, 0:138], -10.0 - CW, c(26), A_, EQ, ["Q", "C26"], ["LA1"], 138)
+    ts(T.ZD[:], T.Q[:], -15.0, c(15), A_, EQ, ["Q", "C15"], ["ZD"], 72)
+    ts(T.BK[:], T.QG[:], c(1), None, EQ, None, ["QG", "C0"], ["BK"])
+
+    def select(out, in_, cmp, fill, sign, r, w):
+        op("G", lambda q: q.affine_select(out, in_, [[sign, 128]], cmp, fill, 0, -sign), r, w, 0.17 + 256 * CY)
+
+    act(T.T1[:], T.BK[:], ACT.Identity, 0.0, c(23), ["BK", "C23"], ["T1"], 128)
+    select(T.T2[:], T.T1[:], ALU.is_gt, 0.0, -1, ["T1"], ["T2"])
+    act(T.T2[:, 15:128:16], T.T1[:, 15:128:16], ACT.Identity, 0.0, 1.0, ["T1"], ["T2"], 8)
+    select(T.TRI[:], T.T2[:], ALU.not_equal, 2048.0, 1, ["T2"], ["TRI"])
+    select(T.TRL[:], T.BK[:], ALU.is_ge, 0.0, 1, ["BK"], ["TRL"])
+    iota(T.TRL[:, 15:128:16], [[0, 8]], 0, 0, "TRL", 8)
+    select(T.TRS[:], T.BK[:], ALU.is_gt, 0.0, 1, ["BK"], ["TRS"])
+    select(T.B14[:], T.BK[:], ALU.is_ge, 0.0, 0, ["BK"], ["B14"])
+    iota(T.B14[:, 14:128:16], [[0, 8]], 0, 0, "B14", 8)
+    ts(T.LA[:, 0, :], T.Q[:, 0:138], -10.0, c(25), A_, EQ, ["Q", "C25"], ["LA0"], 69)
+    ts(T.LA[:, 1, :], T.Q[:, 0:138], -10.0 - CW, c(26), A_, EQ, ["Q", "C26"], ["LA1"], 69)
     hk = NK // 2
     for b in range(NK):
         pk = "pD" + SS[b // hk]
@@ -357,51 +461,56 @@ def rank_program(g, core, T, topo):
             mm(T[pk][:, 128 * (b % hk):128 * (b % hk) + 128], ID, T.LA[:, j, o:o + 128], j == 0, j == 1, ["ID", "LA%d" % j], [pk], 128)
     for j in range(2):
         act(T.LB[:, 128 * hk * j:128 * hk * (j + 1)], T["pD" + SS[j]][:, 0:128 * hk], ACT.Identity, 0.0, 1.0, ["pD" + SS[j]], ["LB%d" % j], 128 * hk)
-    if LP:
-        iota(T.OF0[:], [[0, W // 2], [1, 2]], 0, 0, "OF0", W)
-        ts(T.OFFS[:], T.OF0[:], c(34), c(5), M_, A_, ["OF0", "C34", "C5"], ["OFFS"], W)
-    ts(T.R1[:], T.QX[:, 0:CW, :], 0.0, None, ALU.is_gt, None, ["QX"], ["R1"], W // 2)
-    ts(T.DIAG[:], T.QX[:], c(2), 2.0 ** -23, EQ, M_, ["QX", "C0"], ["DIAG"], 192)
-    tt(T.CAP[:], T.DIAG[:], T.DW0[:], M_, ["DIAG", "DW0"], ["CAP"], 768)
-    ts(T.UP[:], T.QX[:, 0:CW, :], c(2), None, ALU.is_gt, None, ["QX", "C0"], ["UP"], W // 2)
-    XT = ["XT"]
-    if XB:
-        XT = ["XT%d" % j for j in range(4)]
+    iota(T.OF0[:], [[0, W // 2], [1, 2]], 0, 0, "OF0", W)
+    ts(T.OFFS[:], T.OF0[:], c(34), c(5), M_, A_, ["OF0", "C34", "C5"], ["OFFS"], W)
+    ts(T.DIAG[:], T.QX8[:], c(2), None, EQ, None, ["QX8", "C0"], ["DIAG"], W // 2)
+    tt(T.KD[:], T.DIAG[:], T.DW0[:], M_, ["DIAG", "DW0"], ["KD"], 2 * W)
+    ts(T.DMF[:, 0:W:16], T.Q[:, 0:W:16], -2.0, c(39), M_, A_, ["Q", "C39"], ["DMF"])
+    XT = ["XT%d" % j for j in range(4)]
+
+    def other():
         for j in range(4):
             pk = "pS%d" % (j % 2)
-            mm(T[pk][:], T.SX[:], T.X2[:, 8 + 512 * j:520 + 512 * j], True, True, ["SX", "XO"], [pk], 512)
-            act(T.X2[:, H + 8 + 512 * j:H + 520 + 512 * j], T[pk][:], ACT.Identity, 0.0, 1.0, [pk], [XT[j]], 512)
+            mm(T[pk][:], T.SX[:], T.X2[:, P0 + 512 * j:P0 + 512 * j + 512], True, True, ["SX", XO[j]], [pk], 512)
+            o = T.X2[:, H + P0 + 512 * j:H + P0 + 512 * j + 512]
+            if OE[j] == "V":
+                cp(o, T[pk][:], [pk], [XT[j]], 512)
+            else:
+                act(o, T[pk][:], ACT.Identity, 0.0, 1.0, [pk], [XT[j]], 512)
 
-    sl = lambda s: slice(CW * st[s], CW * st[s] + CW)
-    sw = lambda s: slice(W * st[s], W * st[s] + W)
-    XOWN = ["XO", "XOp", "XOn"]
+    other()
+    XT = XT + ["XTp"]
+
+    ix = {s: NS - 1 - st[s] for s in SS}
+    sl = lambda s: slice(CW * ix[s], CW * ix[s] + CW)
+    sw = lambda s: slice(W * ix[s], W * ix[s] + W)
+    XOWN = XO + ["XOp", "XOn"]
     xall = lambda t: XOWN + XT + ["XTn"] * t
-    xwin = lambda t: T.X2[:, 0:H + 2056 + 384 * t]
-    xown = lambda t: T.X2[:, 0:2056 + 384 * t]
-    turns = [0]
+    xwin = lambda t: T.X2[:, 0:H + N0 + 384 * t]
+    xown = lambda t: T.X2[:, 0:N0 + 384 * t]
+    turns, sent = [0], [0]
 
     def bank():
         turns[0] += 1
         return "pS%d" % (turns[0] % 2)
 
-    for s in SS:
-        ts(B("VL", s)[:, 0:CW], T.W0I[:, sl(s)], 8.0, None, A_, None, ["W0I"], ["VL" + s])
-        for u in range(2):
-            o = CW * st[s] + u
-            ts(B("VL", s)[:, CW + NK * u:CW + NK * u + NK], T.W0I[:, o:o + CW - 1:2], 8.0, None, A_, None, ["W0I"], ["VX%s%d" % (s, u)])
+    ts(T.VL[:, :, 0:CW], T.W0I[:], float(P0), None, A_, None, ["W0I"], each("VL"))
+    for u in range(2):
+        ts(T.VL[:, :, CW + NK * u:CW + NK * u + NK], T.W0I[:, u:24:2], float(P0), None, A_, None, ["W0I"], ["VX%s%d" % (s, u) for s in SS])
+    vl = lambda s, a, b: T.VL[:, ix[s], a:b]
 
-    def agather(s, t, key=True):
-        ts(T.GA[:, sw(s)], T.ATI[:, 0:2056 + 384 * t].indirect(B("VL", s)[:, 0:CW]), -1024.0, None, A_, None,
-           ["AT", "ATp", "VL" + s] + ["ATn"] * t, ["GA" + s], gat(W))
+    def agather(s, t, key=True, e="V"):
+        src, r = T.ATI[:, 0:N0 + 384 * t].indirect(vl(s, 0, CW)), ["AT", "ATp", "VL" + s] + ["ATn"] * t
+        if e == "V":
+            ts(T.GA[:, sw(s)], src, -1024.0, None, A_, None, r, ["GA" + s], gat(W))
+        else:
+            act(T.GA[:, sw(s)], src, ACT.Identity, -1024.0, 1.0, r, ["GA" + s], gat(W))
         if key:
             dma("Y", T.GA3[:, sl(s), :], T.GA[:, sw(s)], "dg" + s, ["GA" + s], ["G3" + s], W // 4)
 
-    def xgather(s, t):
-        src, r = xown(t).indirect(B("VL", s)[:, CW:2 * CW]), XOWN[:2 + t] + ["VX%s0" % s, "VX%s1" % s]
-        if XE == "V":
-            cp(T.XV[:, sw(s)], src, r, ["XV" + s], gat(W))
-        else:
-            act(T.XV[:, sw(s)], src, ACT.Identity, 0.0, 1.0, r, ["XV" + s], gat(W))
+    def xgather(s, t, bias=0.0):
+        src, r = xown(t).indirect(vl(s, CW, 2 * CW)), XOWN[:5 + t] + ["VX%s0" % s, "VX%s1" % s]
+        act(T.XV[:, sw(s)], src, ACT.Identity, bias, 1.0, r, ["XV" + s], gat(W))
 
     def swap4(out, o0, mat, src, key, r, stop, start=False):
         for u in range(2):
@@ -409,7 +518,7 @@ def rank_program(g, core, T, topo):
                 mm(out[:, o0 + v:o0 + CW:2, :], mat(v, u), src(u), start and u + v == 0, stop and u + v == 2, r, [key], W // 2)
 
     def xv(s):
-        return lambda u: T.XV[:, W * st[s] + W // 2 * u:W * st[s] + W // 2 * (u + 1)]
+        return lambda u: T.XV[:, W * ix[s] + W // 2 * u:W * ix[s] + W // 2 * (u + 1)]
 
     def zstep(s, first, final=False):
         pk, z = "pK" + s, B("Z", s)
@@ -418,57 +527,80 @@ def rank_program(g, core, T, topo):
             mm(o, ID, z[:, 0:W], True, False, ["ID", "Z%s0" % s], [pk], W)
         swap4(T[pk], CW, swb, xv(s), pk, ["XV" + s] + SW, True, first)
         if final:
-            mm(T[pk][:, 0:CW, :], T.NI[:], z[:, 0:W], True, False, ["NI", "Z%s0" % s], [pk], W)
-            swap4(T[pk], 0, swb, xv(s), pk, ["XV" + s] + SW, True)
-            act(B("GT", s)[:], T[pk][:, 0:CW, :], ACT.Sign, 127.5, 1.0, [pk], ["GT" + s], W)
-            act(B("ZF", s)[:], o, ACT.Identity, 63.75, 0.5, [pk], ["ZF" + s], W)
+            if Z2E == "S":
+                act(z[:, 3 * W:4 * W], z[:, 0:W], ACT.Identity, 0.0, 2.0, ["Z%s0" % s], ["Z%s3" % s], W)
+            else:
+                ts(z[:, 3 * W:4 * W], z[:, 0:W], 2.0, None, M_, None, ["Z%s0" % s], ["Z%s3" % s])
+            select(B("ZF", s)[:], z[:, 0:W], ALU.is_ge, 0.0, 0, ["Z%s0" % s], ["ZF" + s])
+            tt(B("GT", s)[:], o, z[:, 3 * W:4 * W], ALU.is_gt, [pk, "Z%s3" % s], ["GT" + s], W)
             return
         bias, scale = 128.0 if first else 63.75, 1.0 if first else 0.5
         for d in range(GS):
             if ZE[min(d, len(ZE) - 1)] == "S":
                 act(z[:, W * d:W * d + W], o, ACT.Identity, bias, scale, [pk], ["Z%s%d" % (s, d)], W)
+            elif ZE[min(d, len(ZE) - 1)] == "G" and (not first or s in GF):
+                select(z[:, W * d:W * d + W], z[:, 0:W], ALU.is_ge, 0.0, 0, ["Z%s0" % s], ["Z%s%d" % (s, d)])
             elif d:
                 cp(z[:, W * d:W * d + W], z[:, 0:W], ["Z%s0" % s], ["Z%s%d" % (s, d)], W // 2)
             else:
                 ts(z[:, 0:W], o, scale, bias, M_, A_, [pk], ["Z%s0" % s], W)
 
-    def lists(s, L):
-        lt, cl = B("LT", s), B("CL", s)
-        if LP:
-            o = B("pD", s)
-            tr(lt[:], T.GA[:, sw(s)], ["GA" + s], ["LT" + s], W)
-            mm(o[:, 256:256 + CW * L], ID, T.OFFS[:, 0:CW * L], True, False, ["ID", "OFFS"], ["pD" + s], CW * L)
-            for j in range(CW):
-                mm(o[:, 256 + j:256 + CW * L:CW], ID, lt[:, 16 * j:16 * j + L], False, j == CW - 1, ["ID", "LT" + s], ["pD" + s], 64)
-            cp(cl[:, 0:CW * L], o[:, 256:256 + CW * L], ["pD" + s], ["CL%s0" % s, "CL%s1" % s], CW * L)
-            return
-        for b in range(NK):
-            o = W * st[s] + 32 * b
-            tr(lt[:, b:W:NK], T.GA[:, o:o + 32], ["GA" + s], ["LT%s%d" % (s, b)])
-        for h in range(2):
-            ts(cl[:, h:CW * L:2], lt[:, W // 2 * h:W // 2 * h + NK * L], c(20 if h else 5), None, A_, None,
-               ["LT%s%d" % (s, b) for b in range(NK)] + ["C20" if h else "C5"], ["CL%s%d" % (s, h)], NK * L)
+    def lists(s, L, e="V", shared=False):
+        lt, cl, pd = B("LT", s), B("CL", s), (bank() if LB_ == "S" else "pK" + s) if shared else "pD" + s
+        o = T[pd][:, 24:24 + L // 2, :] if shared else T[pd][:, 256:256 + CW * L]
+        col = lambda j: o[:, :, j:16:CW] if shared else o[:, j:CW * L:CW]
+        keys = ["CL%s%d" % (s, x) for x in range(L - 13)]
+        tr(lt[:], T.GA[:, sw(s)], ["GA" + s], ["LT" + s], W // 2)
+        two = OFF2 and not shared
+        if not two:
+            mm(o, ID, T.OFFS[:, 0:CW * L], True, False, ["ID", "OFFS"], [pd], CW * L)
+        for j in range(CW):
+            mm(col(j), ID, lt[:, 16 * j:16 * j + L], two and not j, j == CW - 1, ["ID", "LT" + s], [pd], 64)
+        if two:
+            for h in range(2):
+                ts(cl[:, h:CW * L:2], o[:, h:CW * L:2], c(5 + 30 * h), None, A_, None, [pd, "C5", "C35"], [k + "ab"[h] for k in keys], CW * L // 2)
+        elif e == "V":
+            cp(cl[:, 0:CW * L], o, [pd], [k + x for k in keys for x in "ab"], CW * L)
+        else:
+            act(cl[:, 0:CW * L], o, ACT.Identity, 0.0, 1.0, [pd], [k + x for k in keys for x in "ab"], CW * L)
 
     def begin(s, t):
-        agather(s, t)
-        xgather(s, t)
+        if t:
+            w, lt, pd = sw(s), B("LT", s), "pD" + s
+            act(T.LG[:, w], T.FT0[:].indirect(vl(s, 0, CW)), ACT.Identity, -1024.0, 1.0, FTK[0] + ["VL" + s], ["LG" + s], gat(W))
+            tr(lt[:], T.LG[:, w], ["LG" + s], ["LT" + s], W // 2)
+            for h in range(2):
+                o, i, k = B("CL", s)[:, 14 * CW + h:15 * CW:2], lt[:, 16 * h + 14:W:32], "C%d" % (5 + 30 * h)
+                if BE[0] == "V":
+                    ts(o, i, c(5 + 30 * h), None, A_, None, ["LT" + s, k], ["CL%s1%s" % (s, "ab"[h])])
+                else:
+                    act(o, i, ACT.Identity, c(5 + 30 * h), 1.0, ["LT" + s, k], ["CL%s1%s" % (s, "ab"[h])], NK)
+            mm(T[pd][:, 0:W], ID, T.GA[:, w], True, False, ["ID", "GA" + s], [pd], W)
+            mm(T[pd][:, 0:W], T.D14[:], T.LG[:, w], False, True, ["D14", "LG" + s], [pd], W)
+            act(T.GA3[:, sl(s), :], T[pd][:, 0:W], ACT.Identity, c(36), 1.0, [pd, "C36"], ["G3" + s], W)
+        else:
+            agather(s, 0)
+            lists(s, 14)
+        xgather(s, 0)
         zstep(s, True)
-        lists(s, 14 + t)
 
     def bulk(s, k, t):
         pd, ab, cd, cl, z = B("pD", s), B("AB", s), B("CD", s), B("CL", s), B("Z", s)
         zk = lambda n: ["Z%s%d" % (s, d) for d in range(n)]
         abk = lambda i, n: ["AB%s%d" % (s, x) for x in range(i, i + n)]
         cdk = lambda i, n: ["CD%s%d" % (s, x) for x in range(i, i + n)]
-        clk = ["CL%s0" % s, "CL%s1" % s]
+        clk = lambda i, n: ["CL%s%d%s" % (s, x, y) for x in range(1 + (i + n > 14)) for y in "ab"]
         sums, ns = [], 0
-        for mode, i, n in PLAN[t]:
+        plan = PLAN[t]
+        if (t, k, s) in HEAVY:
+            plan = (plan[0], ("S", 0, 3)) + plan[2:]
+        for mode, i, n in plan:
             part = slice(W * i, W * (i + n))
             if mode != "S":
                 for j in range(i, i + n, GS):
                     m = min(GS, i + n - j)
                     tt(cd[:, W * j:W * (j + m)], xwin(t).indirect(cl[:, CW * j:CW * (j + m)]), z[:, 0:W * m], ALU.subtract,
-                       xall(t) + clk + zk(m), cdk(j, m), gat(W * m))
+                       xall(t) + clk(j, m) + zk(m), cdk(j, m), gat(W * m))
             if mode == "A":
                 act(ab[:, part], cd[:, part], ACT.Abs, 128.0, 1.0, cdk(i, n), abk(i, n), W * n)
             if mode == "B":
@@ -480,164 +612,199 @@ def rank_program(g, core, T, topo):
                 q, xk = bank(), "XG%s%d" % (s, ns % 2)
                 xg, o = B("XG", s)[:, ns % 2, 0:W * n], T[q][:, 0:CW * n, :]
                 ns += 1
-                act(xg, xwin(t).indirect(cl[:, CW * i:CW * (i + n)]), ACT.Identity, 0.0, 1.0, xall(t) + clk, [xk], gat(W * n))
+                act(xg, xwin(t).indirect(cl[:, CW * i:CW * (i + n)]), ACT.Identity, 0.0, 1.0, xall(t) + clk(i, n), [xk], gat(W * n))
                 mm(o, T.NI[:], z[:, 0:W * n], True, False, ["NI"] + zk(n), [q], W * n)
                 mm(o, ID, xg, False, True, ["ID", xk], [q], W * n)
                 act(ab[:, part], o, ACT.Abs, 128.0, 1.0, [q], abk(i, n), W * n)
+        for j in range(XPE):
+            mm(pd[:, 384:512], T.D14[:], T.BK[:], True, True, ["D14", "BK"], ["pD" + s], 128)
         for j in range(k):
             mm(pd[:, 0:W], T.TRL[:], B("R", s)[:, CW * j:CW * j + CW, :], j == 0, False, ["TRL", "R%s%d" % (s, j)], ["pD" + s], W)
         for j, (mat, src, x, keys) in enumerate(sums):
             mm(pd[:, 0:W], T[mat][:, 15 - x:143 - x], src[:, W * x:W * x + W], j == 0 and not k, j == len(sums) - 1,
                [mat] + keys, ["pD" + s], W)
-        swap4(B("pK", s), 0, swb, lambda u: T.GA3[:, CW * st[s] + u:CW * st[s] + CW:2, :], "pK" + s, ["G3" + s] + SW, False, True)
+        swap4(B("pK", s), 0, swb, lambda u: T.GA3[:, CW * ix[s] + u:CW * ix[s] + CW:2, :], "pK" + s, ["G3" + s] + SW, False, True)
 
-    def turn(s, src, key, out, okey, col):
-        o = B("pD", s)[:, col:col + 32]
+    def turn(s, src, key, out, okey, col, add=False):
+        pd = "pD" + s if col else "pS0"
+        o = T[pd][:, col:col + 32] if col else T[pd][:, 0:2, :]
+        if add:
+            mm(o, ID, T.K30[:], True, False, ["ID", "K30"], [pd], 64)
         for b in range(NK):
-            mm(o, T.LB[:, 128 * b:128 * b + 128], src[:, 2 * b:2 * b + 2, :], b == 0, b == NK - 1, ["LB0", "LB1", key], ["pD" + s], 64)
-        tr(out[:], o, ["pD" + s], [okey])
+            mm(o, T.LB[:, 128 * b:128 * b + 128], src[:, 2 * b:2 * b + 2, :], b == 0 and not add, b == NK - 1, ["LB0", "LB1", key], [pd], 64)
+        tr(out[:], o, [pd], [okey])
 
     def choose(s, k, t):
         last = k == 3
         r, rk, kt, pk = B("R", s)[:, CW * k:CW * k + CW, :], "R%s%d" % (s, k), B("KT", s), "pK" + s
         th, o = T.TH[:, 4 * t + k:4 * t + k + 1], T[pk][:, 0:CW, :]
-        if GE == "V":
-            ts(B("VAL", s)[:], B("pD", s)[:, 0:W], th, None, ALU.is_lt, None, ["pD" + s, "TH%d" % t], ["VAL" + s], W)
+        ge = GE[t][(NS * k + st[s]) % len(GE[t])]
+        if ge == "V":
+            ts(B("VAL", s)[:], B("pD", s)[:, 0:W], th, 2.0, ALU.is_lt, M_, ["pD" + s, "TH%d" % t], ["VAL" + s], W)
         else:
             act(B("VAL", s)[:], B("pD", s)[:, 0:W], ACT.Sign, th, -1.0, ["pD" + s, "TH%d" % t], ["VAL" + s], W)
         mm(o, T.TRI[:], B("VAL", s)[:], False, True, ["TRI", "VAL" + s], [pk], W)
-        ts(r, o, c(10), LOW, A_, ALU.max, [pk, "C10"], [rk], W)
-        turn(s, r, rk, kt, "KT" + s, 192)
-        ts(B("VL", s)[:], kt[:, 0:2 * CW], 31752.0, None, A_, None, ["KT" + s], ["VL" + s, "VX%s0" % s, "VX%s1" % s])
+        ts(r, o, -4096.0 if ge == "V" else c(10), LOW, A_, ALU.max, [pk, "C10"], [rk], W)
+        turn(s, r, rk, kt, "KT" + s, 192, last)
+        ts(vl(s, 0, 2 * CW), kt[:, 0:2 * CW], (1024.0 if last else 31744.0) + P0, None, A_, None, ["KT" + s], ["VL" + s, "VX%s0" % s, "VX%s1" % s])
         if last:
-            ts(T.VLF[:, sl(s)], kt[:, 0:CW], 31744.0, None, A_, None, ["KT" + s], ["VLF" + s])
-            swap4(T[pk], 0, bs, lambda u: r[:, u:CW:2, :], pk, [rk] + BSK, True, True)
-            act(T.VB[:, sl(s), :], o, ACT.Identity, 30720.0, 1.0, [pk], ["VB" + s], W)
-            ts(T.VU[:, sl(s), :], T.VB[:, sl(s), :], 1024.0, None, A_, None, ["VB" + s], ["VU" + s], W)
-            if t:
-                act(T.VF[:, sw(s)], T.VB[:, sl(s), :], ACT.Identity, 1024.0, 1.0, ["VB" + s], ["VF" + s], W)
+            act(T.VB[:, sw(s)], T.IDT[:].indirect(vl(s, 0, CW)), ACT.Identity, 0.0, 1.0, FTK[2] + ["VL" + s], ["VB" + s], gat(W))
         if not (last and t):
-            agather(s, t, not last)
-        xgather(s, t)
+            agather(s, t, not last, BE[2] if last else BE[4])
+        xgather(s, t, 128.0 * last)
         zstep(s, False, last)
         if not last:
-            lists(s, 14 + t)
+            lists(s, 14 + t, BE[5])
+        elif not t and LB_ != "L":
+            lists(s, 14, BE[1], True)
 
     def votes(s, t):
-        turn(s, B("GT", s), "GT" + s, B("KW", s), "KW" + s, 224)
-        ts(T.WT[:, sl(s)], B("KW", s)[:, 0:CW], 1.0, EPS, ALU.is_lt, A_, ["KW" + s], ["WT" + s])
-        pk, zn = "pK" + s, "ZN%d" % t
-        swap4(T[pk], 0, swb, lambda u: B("ZF", s)[:, u:CW:2, :], pk, ["ZF" + s] + SW, True, True)
-        act(T[zn][:, sw(s)], T[pk][:, 0:CW, :], ACT.Identity, 0.0, 1.0, [pk], [zn + s], W)
+        pd, zn, pk = "pD" + s, "ZN%d" % t, "pK" + s
+        if KWB:
+            mm(T[pd][:, 0:W], T.BK[:], B("GT", s)[:], True, True, ["BK", "GT" + s], [pd], W)
+            tr(B("KW", s)[:], T[pd][:, 0:W], [pd], ["KW" + s], W)
+            ts(T.WT[:, sl(s)], B("KW", s)[:, 0:W:16], 8.5, EPS, ALU.is_lt, A_, ["KW" + s], ["WT" + s])
+        else:
+            turn(s, B("GT", s), "GT" + s, B("KW", s)[:, 0:32], "KW" + s, 224)
+            ts(T.WT[:, sl(s)], B("KW", s)[:, 0:CW], 8.5, EPS, ALU.is_lt, A_, ["KW" + s], ["WT" + s])
+        swap4(T[pk], 0, swb, lambda u: B("ZF", s)[:, u:CW:2, :], pk, ["ZF" + s] + SW, False, True)
+        for u in range(2):
+            mm(T[pk][:, u:CW:2, :], ID, xv(s)(u), False, u == 1, ["ID", "XV" + s], [pk], W // 2)
+        act(T[zn][:, sw(s)], T[pk][:, 0:CW, :], ACT.Identity, -0.25, 0.5, [pk], [zn + s], W)
         trs = []
         for q in range(8):
-            if q == rank or (48 * q + 47) // W != st[s]:
+            if q == rank or 48 * q // W != ix[s]:
                 continue
             dst = T.cores[q]
             rid, pid, _e = topo.addr(dst)
-            j = 2 * len(trs)
-            mask = sum(1 << e for e in topo.engines(core, dst)[j:j + 2])
+            n = RE[t][st[s]]
+            sent[0] += n
+            mask = sum(1 << e for e in topo.engines(core, dst)[n * len(trs):n * len(trs) + n])
             trs.append(RemoteDMATransfer(dst_ids=[DstId(rid=rid, pnc=pid)], dma_engine_mask=mask, remote_sem=T.sem["arr%d" % t],
                                          src=T[zn][:, 48 * q:48 * q + 48], dst=T["RZ%d" % t][:, 48 * rank:48 * rank + 48]))
         op("G", lambda q: q.remote_dma_fused(trs, local_sem=T.sem.lsem), [zn + x for x in SS[:st[s] + 1]], [], 1.0, "lsem")
 
     def flips(t):
         top = level[0]
-        for s in SS:
-            act(T.XW[:, sw(s)], xown(t).indirect(B("VL", s)[:, 0:CW]), ACT.Identity, 0.0, 1.0, XOWN[:2 + t] + ["VL" + s], ["XW" + s], gat(W))
         if not t:
-            o = T.pS1[:, 0:24, :]
-            mm(o, T.D14[:], T.QC[:], True, False, ["D14", "QC"], ["pS1"], 384)
-            mm(o, T.D14[:], T.QX[:], False, False, ["D14", "QX"], ["pS1"], 384)
-            mm(o, ID, T.GA[:], False, True, ["ID"] + each("GA"), ["pS1"], 384)
-            act(T.AS[:], o, ACT.Identity, c(13), 1.0, ["pS1", "C13"], ["AS"], 384)
-            ts(T.ATI[:, 2056:2440], T.GA[:], c(6), c(14), M_, A_, each("GA") + ["C6", "C14"], ["ATn"], 384)
-
-        def listed(s, j, out, key):
-            w, pd, dm, sc = sw(s), "pD" + s, T.DM[:, j, sw(s)], T.SC2[:, j, sw(s)]
-            tt(dm, T[pd][:, 256 + W * j:256 + W * j + W], T.CAP[:, sl(s), :], ALU.min, [pd, "CAP"], ["DM" + key + s], W)
-            V(lambda v: v.tensor_tensor_scan(sc, T.R1[:], dm, 0.0, M_, A_), ["R1", "DM" + key + s], ["SC" + key + s], W)
-            ts(out[:, sl(s)], T.SC2[:, j, w.start + 15:w.stop:16], 2.0 ** 23, None, M_, None, ["SC" + key + s], [key + s])
+            if BE[3] == "V":
+                ts(T.ATI[:, N0:H], T.GA[:], c(6), c(14), M_, A_, each("GA") + ["C6", "C14"], ["ATn"], 384)
+            else:
+                act(T.ATI[:, N0:H], T.GA[:], ACT.Identity, c(14), c(6), each("GA") + ["C6", "C14"], ["ATn"], 384)
 
         for h, s in enumerate(SS):
             level[0] = top - FLEV[0] + FLEV[1] * h
             pd, pk, w, bl = "pD" + s, "pK" + s, sw(s), sl(s)
-            two = h < NS - 1
-            ears, rest, e0 = [T[pd][:, 256 + W * j:256 + W * j + W] for j in range(1 + two)], T[pk][:, 2 * CW:3 * CW, :], CW * CW * h
-            for j, ear in enumerate(ears):
-                mm(ear, T.IDS[:], T.K8[:], j == 0, False, ["IDS", "K8"], [pd], W)
-                mm(ear, T.IDS[:], T.VB[:, bl, :], False, False, ["IDS", "VB" + s], [pd], W)
-            for b in range(CW - 1, -1, -1):
-                e, key, n = e0 + CW * b, "E%s%d" % (s, b), CW * h + b
-                ts(T.E[:, e:e + CW, :], T.VU[:, bl, :], T.VLF[:, n:n + 1], T.WT[:, n:n + 1], EQ, M_, ["VU" + s, "VLF" + s, "WT" + s], [key], W // 2)
-                mm(rest[:, 0:b + 1, :], T.BK[:], T.E[:, e:e + b + 1, :], b == CW - 1, b == 0, ["BK", key], [pk], 16 + 16 * b)
-                for ear in ears if b < CW - 1 else ():
-                    mm(ear[:, 16 * b + 16:W], T.BK[:], T.E[:, e + b + 1:e + CW, :], False, False, ["BK", key], [pd], W - 16 - 16 * b)
-            tt(T.DG[:, bl, :], T.E[:, e0:e0 + CW * CW:CW + 1, :], T.UP[:], M_, ["E%s%d" % (s, b) for b in range(CW)] + ["UP"], ["DG" + s], 2 * W)
+            ear, rest, ft = T[pd][:, 256:256 + W], T[pk][:, 2 * CW:3 * CW, :], "FT%d" % t
+            early, two = s in EARLY, not t and s in OTHER
+
+            def compare(e0, name, s2, o2, r, sums):
+                for b in range(CW - 1, -1, -1):
+                    e, key = e0 + CW * b, "%s%s%d" % (name, s, b)
+                    ts(T.E[:, e:e + CW, :], T.VB[:, w], B("KT", s)[:, b:b + 1], s2(b), EQ, o2, ["VB" + s, "KT" + s] + r, [key], W // 2)
+                    if "r" in sums:
+                        mm(rest[:, 0:b + 1, :], T.B14[:], T.E[:, e:e + b + 1, :], b == CW - 1 and t == 1, b == 0 and not h, ["B14", key], [pk], 16 + 16 * b)
+                    if "e" in sums and b < CW - 1:
+                        mm(ear[:, 16 * b + 16:W], T.BK[:], T.E[:, e + b + 1:e + CW, :], False, False, ["BK", key], [pd], W - 16 - 16 * b)
+                if "e" in sums:
+                    mm(ear, T.TRS[:], T.E[:, e0:e0 + CW * CW:CW + 1, :], False, True, ["TRS"] + ["%s%s%d" % (name, s, b) for b in range(CW)], [pd], W)
+
+            def listed():
+                act(T.DM[:, w], ear, ACT.Relu, -1408.0, -2.0 ** 23, [pd], ["DM" + s], W)
+                V(lambda v, w=w: v.tensor_tensor_scan(T.SC[:, w], T.DMF[:], T.DM[:, w], 4096.0, ALU.min, A_), ["DMF", "DM" + s], ["SC" + s], W)
+                sc = T.SC[:, w.start + 15:w.stop:16]
+                if XE2 == "V":
+                    ts(T.XOFF[:, bl], sc, 1024.0 + P0, None, A_, None, ["SC" + s], ["XOFF" + s])
+                else:
+                    act(T.XOFF[:, bl], sc, ACT.Identity, 1024.0 + P0, 1.0, ["SC" + s], ["XOFF" + s], CW)
+                if two:
+                    mm(T[pd][:, 0:CW], T.SX[:], sc, True, True, ["SX", "SC" + s], [pd], 64)
+                    if BE[1] == "V":
+                        ts(T.XOF2[:, bl], T[pd][:, 0:CW], 1024.0 + P0, None, A_, None, [pd], ["XOF2" + s])
+                    else:
+                        act(T.XOF2[:, bl], T[pd][:, 0:CW], ACT.Identity, 1024.0 + P0, 1.0, [pd], ["XOF2" + s], CW)
+
+            mm(ear, T.IDS[:], T.KD[:], True, False, ["IDS", "KD"], [pd], W)
+            mm(ear, T.IDS[:], T.VB[:, w], False, False, ["IDS", "VB" + s], [pd], W)
+            if not t:
+                mm(rest, T.D14[:], T.QW[:, w], True, False, ["D14", "QW"], [pk], W)
+            if early:
+                compare(CW * CW * h, "E", lambda b: 1.0, M_, [], "e")
+            else:
+                compare(CW * CW * h, "E", lambda b: T.WT[:, bl.start + b:bl.start + b + 1], M_, ["WT" + s], "re")
+            listed()
+            if early:
+                compare(CW * CW * (3 + h), "N", lambda b: T.WT[:, bl.start + b:bl.start + b + 1], M_, ["WT" + s], "r")
+            if h:
+                f, bias, scale = (ACT.Identity, 0.5, -0.5) if t else (ACT.Relu, 0.0, c(21))
+                act(T.FG[:, w], T[ft][:].indirect(vl(s, 0, CW)), f, bias, scale, FTK[t] + ["VL" + s, "C21"], ["FG" + s], gat(W))
+                mm(rest, ID, T.FG[:, w], False, True, ["ID", "FG" + s], [pk], W)
+            if not t:
+                act(T.AS[:, w], rest, ACT.Identity, c(13), 1.0, [pk, "C13"], ["AS" + s], W)
+                cp(T[ft][:].indirect(T.XOFF[:, bl]), T.AS[:, w], ["AS" + s, "XOFF" + s], FTK[t], sca())
             act(T.FL[:, w], rest, ACT.Sign, 0.875, -1.0, [pk], ["FL" + s], W)
+            if t and h < NS - 1:
+                cp(T[ft][:].indirect(T.XOFF[:, bl]), T.FL[:, w], ["FL" + s, "XOFF" + s], FTK[t], sca())
+            for j, (a, b) in enumerate((("ID2", "EV"), ("SX", "EVX"))[:1 + two]):
+                o = T[pk][:, j * CW:j * CW + CW, :]
+                for u in range(2):
+                    mm(o[:, u:CW:2, :], T[a][:, 0:128], xv(s)(u), u == 0, False, ["ID", a, "XV" + s], [pk], W // 2)
+                mm(o, T[b][:], T.FL[:, w], False, True, [b, "FL" + s], [pk], W)
+            act(T.XN[:, h, 0:W * (1 + two)], T[pk][:, 0:CW * (1 + two), :], ACT.Abs, c(20), 1.0, [pk, "C20"], ["XN" + s], W * (1 + two))
+            cp(xown(t).indirect(T.XOFF[:, bl]), T.XN[:, h, 0:W], ["XN" + s, "XOFF" + s], XOWN[:5 + t], sca())
             if two:
-                act(T.FP[:, w], rest, ACT.Relu, 0.875, -1.0, [pk], ["FP" + s], W)
-                mm(ears[1], ID, T.FP[:, w], False, False, ["ID", "FP" + s], [pd], W)
-            for j, ear in enumerate(ears):
-                mm(ear, T.BK[:], T.DG[:, bl, :], False, j == two, ["BK", "DG" + s], [pd], W)
-            listed(s, 0, T.XOFF, "XOFF")
-            if two:
-                listed(s, 1, T.ROFF, "ROFF")
-            o = T[pk][:, 3 * CW:4 * CW, :]
-            mm(o, ID, T.XW[:, w], True, False, ["ID", "XW" + s], [pk], W)
-            mm(o, T.EV[:], T.FL[:, w], False, True, ["EV", "FL" + s], [pk], W)
-            act(T.XN[:, w], o, ACT.Abs, c(12), 1.0, [pk, "C12"], ["XN" + s], W)
-        for h, s in enumerate(SS):
-            level[0] = top - FLEV[0] + FLEV[1] * h
-            cp(T.X2[:, 0:H].indirect(T.XOFF[:, sl(s)]), T.XN[:, sw(s)], ["XN" + s, "XOFF" + s], XOWN, 40 + W * SC_C)
-        for s in SS[:-1]:
-            cp(T.X2[:, 0:H].indirect(T.ROFF[:, sl(s)]), T.XW[:, sw(s)], ["XW" + s, "ROFF" + s], XOWN, 40 + W * SC_C)
+                cp(T.X2[:, H:H + N0].indirect(T.XOF2[:, bl]), T.XN[:, h, W:2 * W], ["XN" + s, "XOF2" + s], XT, sca())
+            elif not t and (h == NS - 1 or SS[h + 1] in OTHER):
+                if COPY == "P":
+                    other()
+                else:
+                    for i in range(8):
+                        a, o = 16 * i, 16 * (i ^ 1)
+                        dma("YS"[i % 2], T.X2[o:o + 16:2, H + P0:H + N0], T.X2[a:a + 16:2, P0:N0], "dd", XO, XT, 32)
         level[0] = top
         if not t:
-            for i in range(8):
-                a, o = 16 * i, 16 * (i ^ 1)
-                dma("YS"[i % 2], T.X2[o:o + 16:2, H + 8:H + 2056], T.X2[a:a + 16:2, 8:2056], "dd", ["XO"], XT, 32)
-            for s in SS[::-1]:
-                cp(T.ATI[:].indirect(T.XOFF[:, sl(s)]), T.AS[:, sw(s)], ["AS", "XO", "XOFF" + s], ["AT", "ATp", "ATn", "ATd"], 40 + W * SC_C)
+            dma("Y", T.ATI[14:128:16, P0:N0], T.FT0[14:128:16, P0:N0], "da", FTK[0], ["AT"], 64)
 
     def arrivals(t):
         rz, zn, pk = "RZ%d" % t, "ZN%d" % t, "pS0"
-        op("R", None, each(zn), [rz], 4.0, "arr%d" % t)
+        op("R", 7 * RE[t][NS - 1 - 48 * rank // W], each(zn), [rz], RLAT, "arr%d" % t)
         for r in range(8):
             o = 128 - 16 * ((rank - r) % 8)
-            src, keys = (T[zn], each(zn)) if r == rank else (T[rz], [rz])
-            mm(T[pk][:, 3 * r:3 * r + 3, :], T.ID2[:, o:o + 128], src[:, 48 * r:48 * r + 48], True, True, ["ID", "ID2"] + keys, [pk], 64)
-        out, key = (T.XM[:], "XM") if t else (T.X2[:, 2056:2440], "XOn")
+            src = T[zn if r == rank else rz]
+            mm(T[pk][:, 3 * r:3 * r + 3, :], T.ID2[:, o:o + 128], src[:, 48 * r:48 * r + 48], True, True, ["ID", "ID2", rz] + each(zn), [pk], 64)
+        out, key = (T.XM[:], "XM") if t else (T.X2[:, N0:H], "XOn")
         act(out, T[pk][:, 0:24, :], ACT.Identity, -128.0, 1.0, [pk], [key], 384)
         if not t:
             mm(T.pS1[:, 0:24, :], T.SX[:], out, True, True, ["SX", key], ["pS1"], 384)
-            act(T.X2[:, H + 2056:H + 2440], T.pS1[:, 0:24, :], ACT.Identity, 0.0, 1.0, ["pS1"], ["XTn"], 384)
-
-    def store(first, sem, after=()):
-        dma("Y", T.yx[first:128:2, 0:2432], T.X2[first:128:2, 8:2440], sem, XOWN + list(after), [], 311)
+            act(T.X2[:, H + N0:NX], T.pS1[:, 0:24, :], ACT.Identity, 0.0, 1.0, ["pS1"], ["XTn"], 384)
 
     for t in range(2):
         for s in SS:
             level[0] = 20 * t + st[s] - 0.5
             begin(s, t)
+        late(t)
         for k in range(4):
             for s in SS:
                 level[0] = 20 * t + NS * k + st[s]
-                if (t, k, s) == (1, 1, SS[0]):
-                    store(1, "de", ["R%s0" % s])
+                if (k, s) == (1, SS[0]):
+                    a, n = (2048, 384) if t else (0, 2048)
+                    dma("Y", T.yx[1:128:2, a:a + n], T.X2[1:128:2, P0 + a:P0 + a + n], "de%d" % t, (XO, ["XOn"])[t] + ["R%s0" % s], [], n // 8)
                 bulk(s, k, t)
                 if k == 3 and FLAT:
                     level[0] = 20 * t + 4 * NS - 1
                 choose(s, k, t)
                 if k == 3:
                     votes(s, t)
+                    if not t and LB_ == "L":
+                        lists(s, 14, BE[1], True)
         level[0] = 20 * t + 4 * NS
         if t:
-            dma("Y", T.yv[:, :], T.VF[0:128:16, :], "dv", each("VF"), [], 12)
+            ts(T.VF[:], T.VB[:], 1024.0, None, A_, None, each("VB"), ["VF"], 384)
+            dma("Y", T.yv[:, :], T.VF[0:128:16, :], "dv", ["VF"], [], 12)
             arrivals(t)
             dma("Y", T.yx[:, 2432:2816], T.XM[:], "dv", ["XM"], [], 96)
         flips(t)
         if not t:
             arrivals(t)
-    store(0, "do")
-    emit(g, T, schedule(ops))
+    dma("Y", T.yx[0:128:2, 0:2432], T.X2[0:128:2, P0:H], "do", XOWN, [], 304)
+    emit(g, T, schedule(ops), sent[0])

@@ -8,52 +8,33 @@ P0 = 272
 N0 = P0 + 2048
 H = N0 + 384
 NX = 2 * H
-RE = ((2, 2, 2), (8, 4, 4))
-EARLY = ""
 EPS = 2.0 ** -9
 LOW = -2048.0
 SS = "ABC"
 NK = 12 // len(SS)
 CW, W = 2 * NK, 32 * NK
-GS = 3
-LP = True
-XB = True
-FLEV = (1.0, 0.0)
-FLAT = False
-PASSES = 4
-XPE = 0
-RLAT = 3.0
-HEAVY = ()
-XE2 = "V"
-DLAT = 2.0
-BW = 300.0
-OE = "VSVS"
-BE = "VSSSVV"
-OTHER = "ABC"
-COPY = "P"
-POLISH = 4000
-HEAT = 0.0
-SETTINGS = ((1.0, 1.5, 3.5, 0.18, 0.19, 0.8, 1.0), (1.2, 1.15, 2.5, 0.12, 0.15, 0.6, 0.8), (1.3, 1.9, 5.0, 0.2, 0.3, 1.0, 1.2))
-ORDER = {}
-PLAN = ((("S", 11, 3), ("A", 0, 3), ("A", 3, 3), ("A", 6, 3), ("A", 9, 2)),
-        (("S", 12, 3), ("A", 0, 3), ("A", 3, 3), ("A", 6, 3), ("A", 9, 3)))
-NB = 0
-ZE = "SGG"
-GE = ("V", "S")
-SAME = 0.18
-NEAR = 0.04
-CY, FV, FS, FP, PE, WAKE = 0.83e-3, 0.015, 0.04, 0.015, 0.42e-3, 0.19
+GS = 4
+PLAN = ((("A", 1, 2), ("S", 11, 3), ("A", 3, 2), ("A", 5, 4), ("A", 9, 2), ("B", 0, 1)),
+        (("A", 1, 2), ("S", 12, 3), ("A", 3, 3), ("A", 6, 4), ("A", 10, 2), ("B", 0, 1)))
+NB = [sum(n for way, i, n in p if way == "B") for p in PLAN]
+ON = (("VVSS",), ("VVSS",))
+OFF2 = True
+LTP = True
+RE = ((2, 2, 2), (8, 4, 4))
+COPY = False
+
+CY, FV, FS, FP, PE, SAME, WAKE = 0.83e-3, 0.015, 0.04, 0.015, 0.42e-3, 0.18, 0.19
 GA_C, SC_C = 1.5, 3.5
-SLACK = {"V": 0.3, "S": 0.3, "P": 0.3, "G": 0.0, "Y": 0.0, "R": 0.0}
-NXL = 1
-Z2E = "V"
-KWB = True
-OFF2 = False
-LB_ = "S"
-GF = ""
-FTN = 400
-XFIRST = 3e3
-LOADS = {"dw": 4e3, "dl": 2e3, "dx0": XFIRST, "dx1": XFIRST - 100, "dx2": XFIRST - 200, "dx3": XFIRST - 300}
+DLAT, BW = 2.0, 300.0
+RLAT = 3.0
+SETTINGS = ((1.0, 1.5, 3.5, 0.18, 0.19, 1.0, 1.3), (1.2, 1.15, 2.5, 0.18, 0.19, 0.6, 0.8), (1.1, 1.25, 5.0, 0.1, 0.15, 0.6, 0.8), (1.3, 1.9, 5.0, 0.2, 0.3, 1.0, 1.2))
+STARTS = 40
+PASSES = 3
+MIX = 3500
+POLISH = 1500
+SEED = 3
+LOADS = {"dw": 4e3, "dx": 3e3, "dl": 2e3}
+ORDER = {}
 
 SCRATCH = {}
 
@@ -63,24 +44,23 @@ def _decl(dtype, where="sbuf", **shapes):
         SCRATCH[n] = (where, [128] + sh, dtype)
 
 
-_decl("bfloat16", X2=[NX], XM=[384], ZD=[144], Z2=[144], ZN=[144], BK=[128], ID2=[256], NI=[128], TRI=[128], TRL=[128], SWB=[512],
-      BS=[512], LA=[2, 138], LB=[128 * NK], EV=[128], IDS=[128], D14=[128], T1=[128], T2=[128], Q=[144], QG=[128], SX=[128],
-      QX=[24, 16], QC=[24, 16], DIAG=[W], QX8=[W], E=[48 * CW, 16], FL=[384], TRS=[128], EVX=[128], K30=[32], UZ=[64],
-      XN=[3, 2 * W], XV=[384], XW=[384], FG=[384], ZN0=[384], ZN1=[384], RZ0=[384], RZ1=[384], B14=[128], FT1=[H])
-_decl("float16", LG=[384], GA=[384], GA3=[24, 16], VB=[384], QW=[384], KD=[W], OFFS=[W], DMX=[CW, 16], SC=[384])
-_decl("float32", C=[40], TH=[8], DW0=[W], DMF=[W], WT=[24],
-      VF=[384], DM=[384], AS=[384], OF0=[W])
-_decl("int32", FT0=[N0], IDT=[H], ATI=[H], W0I=[24], PI=[8])
+_decl("bfloat16", X2=[NX], XM=[384], ZD=[144], Z2=[144], ZN=[144], BK=[128], B14=[128], ID2=[256], NI=[128], TRI=[128], TRL=[128],
+      TRS=[128], SWB=[512], SX=[128], LA=[2, 138], LB=[128 * NK], EV=[128], EVX=[128], IDS=[128], D14=[128], T1=[128], T2=[128],
+      Q=[144], QG=[128], QX=[W], DIAG=[W], K30=[32], SEL=[32], E=[24 * CW, 16], FL=[384], FG=[384], FT1=[H],
+      XN=[3, 2 * W], XV=[384], ZN0=[384], ZN1=[384], RZ0=[384], RZ1=[384])
+_decl("float16", GA=[384], GA3=[24, 16], LG=[384], VB=[384], QW=[384], KD=[W], OFFS=[W], SC=[384])
+_decl("float32", C=[40], TH=[8], DW0=[W], DMF=[W], WT=[24], VF=[384], DM=[384], AS=[384], OF0=[W])
+_decl("int32", ATI=[H], FT0=[N0], IDT=[H], W0I=[24], PI=[8])
 _decl("uint16", XOFF=[24], XOF2=[24], VL=[3, 2 * CW])
 for _s in SS:
-    _decl("bfloat16", **{"CD" + _s: [15 * W], "AB" + _s: [15 * W], "XG" + _s: [2, 4 * W], "Z" + _s: [4 * W], "ZF" + _s: [CW, 16],
+    _decl("bfloat16", **{"CD" + _s: [15 * W], "AB" + _s: [15 * W], "XG" + _s: [4 * W], "Z" + _s: [(GS + 1) * W], "ZF" + _s: [CW, 16],
                          "VAL" + _s: [W], "GT" + _s: [CW, 16]})
     _decl("float16", **{"LT" + _s: [W], "R" + _s: [4 * CW, 16]})
     _decl("float32", **{"KT" + _s: [32], "KW" + _s: [W]})
     _decl("uint16", **{"CL" + _s: [W]})
-    _decl("float32", "psum", **{"pD" + _s: [512], "pK" + _s: [32, 16]})
+    _decl("float32", "psum", **{"pD" + _s: [32, 16], "pK" + _s: [32, 16]})
 _decl("float32", "psum", pS0=[32, 16], pS1=[32, 16])
-SEMAPHORES = ["sv", "ss", "sp", "sg", "dw", "dl", "dx0", "dx1", "dx2", "dx3", "dd", "da", "de0", "de1", "do", "dv", "arr0", "arr1", "lsem"] + ["dg" + _s for _s in SS]
+SEMAPHORES = ["sv", "ss", "sp", "sg", "dw", "dl", "dx", "da", "dd", "df00", "df01", "df02", "df10", "df11", "df12", "de0", "de1", "do", "dv", "arr0", "arr1", "lsem"] + ["dg" + _s for _s in SS]
 
 
 def schedule(ops):
@@ -120,7 +100,8 @@ def schedule(ops):
     for j in range(n - 1, -1, -1):
         if lev[j] is None:
             lev[j] = min([lev[x] for x in succ[j]] or [99])
-    lag = lambda i, j: (SAME if ops[i]["e"] == ops[j]["e"] and not ops[i]["lat"] else WAKE) if preds[j][i] else 0.0
+    how = {}
+    lag = lambda i, j: (SAME if ops[i]["e"] == ops[j]["e"] and not ops[i]["lat"] else how["wake"]) if preds[j][i] else 0.0
 
     def place(rank, back):
         after, left = (preds, [len(x) for x in succ]) if back else (succ, [len(x) for x in preds])
@@ -131,11 +112,11 @@ def schedule(ops):
             t0 = min(st)
             e0 = ops[ready[st.index(t0)]]["e"]
             mine = [(x, s) for x, s in zip(ready, st) if ops[x]["e"] == e0]
-            j = max((x for x, s in mine if s <= t0 + NEAR), key=rank)
-            soon = [(x, s) for x, s in mine if rank(x) > rank(j) and s < t0 + SLACK[e0] * ops[j]["c"]]
+            j = max((x for x, s in mine if s <= t0 + how["near"]), key=rank)
+            soon = [(x, s) for x, s in mine if rank(x) > rank(j) and s < t0 + how["slack"] * (e0 in "VSP") * ops[j]["c"]]
             if soon:
                 k, sk = max(soon, key=lambda a: rank(a[0]))
-                fits = [x for x, s in mine if s + ops[x]["c"] <= sk + NEAR]
+                fits = [x for x, s in mine if s + ops[x]["c"] <= sk + how["near"]]
                 j = max(fits, key=rank) if fits else k
             ready.remove(j)
             o = ops[j]
@@ -148,21 +129,24 @@ def schedule(ops):
                 base[x] = max(base[x], fin + (lag(x, j) + ops[x]["lat"] + ops[x]["by"] if back else lag(j, x)))
                 left[x] -= 1
                 if not left[x]:
-                    base[x] = max(base[x], 0.0)
                     ready.append(x)
-        return out, end, max(end)
+        return out, end
 
-    best = now = place(lambda x: (-lev[x], bl[x] + ops[x]["first"], -x), False)
-    for _ in range(PASSES):
-        fin = now[1]
-        late = place(lambda x: (fin[x], x), True)[1]
-        now = place(lambda x: (late[x] + ops[x]["first"], -x), False)
-        best = min(best, now, key=lambda r: r[2])
-    ORDER[n] = polish(ops, preds, succ, best[0])
+    found = []
+    for a in range(STARTS):
+        how["near"], how["slack"] = 0.02 + 0.05 * (a * 0.618 % 1), 0.15 + 0.35 * (a * 0.755 % 1)
+        how["wake"] = WAKE - 0.03 + 0.1 * (a * 0.570 % 1)
+        now = place(lambda x: (-lev[x], bl[x] + ops[x]["first"], -x), False)
+        for _ in range(PASSES):
+            fin = now[1]
+            late = place(lambda x: (fin[x], x), True)[1]
+            now = place(lambda x: (late[x] + ops[x]["first"], -x), False)
+            found.append(now[0])
+    ORDER[n] = polish(ops, preds, succ, found)
     return [ops[j] for j in ORDER[n]]
 
 
-def polish(ops, preds, succ, order):
+def polish(ops, preds, succ, found):
     n = len(ops)
     eng = [o["e"] for o in ops]
     sets = []
@@ -188,39 +172,54 @@ def polish(ops, preds, succ, order):
             end[j] = t
         return max(end), end, why
 
-    rng = np.random.default_rng(1)
-    base = [run(order, st)[0] for st in sets]
-    score = lambda rs: sum(r[0] / b for r, b in zip(rs, base))
-    now = [run(order, st) for st in sets]
-    best, keep, pairs = score(now), order, None
-    for it in range(POLISH):
+    rng = np.random.default_rng(SEED)
+    base = [run(found[0], st)[0] for st in sets]
+    rate = lambda o: sum(run(o, st)[0] / b for st, b in zip(sets, base))
+    best, order = min((rate(o), o) for o in found)
+    for _ in range(MIX):
+        other = found[int(rng.integers(len(found)))]
+        a = int(rng.integers(n))
+        b = min(n, a + int(rng.integers(50, n // 2)))
+        part = set(order[a:b])
+        new = order[:a] + [x for x in other if x in part] + order[b:]
+        best, order = min((best, order), (rate(new), new))
+    pairs = None
+    for _ in range(POLISH):
         if pairs is None:
             pos = {j: p for p, j in enumerate(order)}
             pairs = []
-            for r in now:
-                j = r[1].index(r[0])
-                while r[2][j] >= 0:
-                    i = r[2][j]
-                    if eng[i] == eng[j] and i not in preds[j]:
-                        pairs.append((i, j))
-                    j = i
+            for st in sets:
+                top, end, why = run(order, st)
+                j = end.index(top)
+                while why[j] >= 0:
+                    if eng[why[j]] == eng[j] and why[j] not in preds[j]:
+                        pairs.append((why[j], j))
+                    j = why[j]
         u, v = pairs[int(rng.integers(len(pairs)))]
         a, b = pos[u], pos[v]
-        mid = order[a + 1:b]
-        up, down = {v}, {u}
-        for x in reversed(mid):
-            if any(y in up for y in succ[x]) or (eng[x] != eng[v] and any(eng[y] == eng[x] for y in up)):
-                up.add(x)
-        if any(y in up for y in succ[u]):
-            continue
-        new = order[:a] + [x for x in mid if x in up] + [v, u] + [x for x in mid if x not in up] + order[b + 1:]
-        res = [run(new, st) for st in sets]
-        s = score(res)
-        if s < score(now) + HEAT * (1.0 - it / POLISH) * rng.random():
-            order, now, pairs = new, res, None
-            if s < best:
-                best, keep = s, new
-    return keep
+        far = int(rng.integers(6)) * (rng.random() < 0.6)
+        if rng.random() < 0.7:
+            while far and a > 0:
+                a -= 1
+                far -= eng[order[a]] == eng[v]
+            mid, up = order[a:b], {v}
+            for x in reversed(mid):
+                if any(y in up for y in succ[x]):
+                    up.add(x)
+            new = order[:a] + [x for x in mid if x in up] + [v] + [x for x in mid if x not in up] + order[b + 1:]
+        else:
+            while far and b < n - 1:
+                b += 1
+                far -= eng[order[b]] == eng[u]
+            mid, down = order[a + 1:b + 1], {u}
+            for x in mid:
+                if any(y in down for y in preds[x]):
+                    down.add(x)
+            new = order[:a] + [x for x in mid if x not in down] + [u] + [x for x in mid if x in down] + order[b + 1:]
+        s = rate(new)
+        if s < best:
+            best, order, pairs = s, new, None
+    return order
 
 
 def emit(g, T, ops, sent):
@@ -297,8 +296,7 @@ def rank_program(g, core, T, topo):
     rank = T.rank_of(core)
     if rank is None:
         return
-    ops, moved = [], {}
-    level = [None]
+    ops, moved, level = [], {}, [None]
 
     def op(e, fn, r, w, c, sem=None, lat=0.0, by=0.0):
         ops.append({"e": e, "fn": fn, "r": list(r), "w": list(w), "c": c, "sem": sem, "lat": lat, "by": by,
@@ -326,8 +324,8 @@ def rank_program(g, core, T, topo):
     def act(out, in_, f, bias, scale, r, w, n):
         op("S", lambda s: s.activation(out, in_, f, bias=bias, scale=scale), r, w, FS + n * CY)
 
-    def mm(out, lhsT, rhs, start, stop, r, w, n):
-        op("P", lambda t: t.matmul(out, lhsT, rhs, start, stop), r, w, FP + max(64, n) * PE)
+    def mm(out, lhsT, rhs, start, stop, r, w, n, least=64):
+        op("P", lambda t: t.matmul(out, lhsT, rhs, start, stop), r, w, FP + max(least, n) * PE)
 
     def dma(e, out, in_, sem, r, w, kb):
         op(e, lambda q: q.dma_start(out=out, in_=in_), r, w, 0.07, sem, DLAT, kb / BW)
@@ -338,18 +336,20 @@ def rank_program(g, core, T, topo):
         else:
             op("G", lambda q: q.iota(out, pat, base, cm), after, [key], 0.13 + 2 * n * CY)
 
+    def select(out, in_, cmp, fill, sign, r, w, n=128):
+        op("G", lambda q: q.affine_select(out, in_, [[sign, n]], cmp, fill, 0, -sign), r, w, 0.17 + 2 * n * CY)
+
     B = lambda n, s: T[n + s]
     st = {s: i for i, s in enumerate(SS)}
     NS = len(SS)
     gat = lambda n: 40 + moved.setdefault("g", n) * GA_C
     sca = lambda: 40 + moved.setdefault("s", W) * SC_C
     each = lambda k: [k + s for s in SS]
+    I_ = ACT.Identity
 
     dma("S", T.W0I[:], T.w0[:], "dw", [], ["W0I"], 12)
-    XO = ["XO%d" % j for j in range(4)]
-    for j in range(NXL):
-        n = 2048 // NXL
-        dma("YS"[j % 2], T.X2[:, P0 + n * j:P0 + n * j + n], T.x0[:, n * j:n * j + n], "dx%d" % j, [], XO[4 * j // NXL:4 * (j + 1) // NXL], n // 4)
+    dma("Y", T.X2[:, P0:N0], T.x0[:, :], "dx", [], ["XO"], 512)
+    V(lambda v: v.memset(T.ATI[:, 0:P0], 0), [], ["ATp"], P0)
     dma("Y", T.ATI[15:128:16, P0:N0], T.nx[:, :], "dl", [], ["AT"], 64)
     for i in range(4):
         a = slice(2 ** i - 1, 128, 2 ** (i + 1))
@@ -358,27 +358,26 @@ def rank_program(g, core, T, topo):
     iota(T.PI[:, 0:1], [[1, 1]], 0, 1, "PI", 1, False)
     iota(T.Q[:], [[1, 144]], 0, 0, "Q", 144)
     iota(T.QG[:], [[1, 8], [0, 16]], 0, 0, "QG", 128)
-    V(lambda v: v.memset(T.ATI[:, 0:P0], 0), [], ["ATp"], P0)
     V(lambda v: v.memset(T.X2[:, 0:P0], 255.0), [], ["XOp"], P0 // 2)
     V(lambda v: v.memset(T.X2[:, N0:H + P0], 255.0), [], ["XOn", "XTp"], (384 + P0) // 2)
     V(lambda v: v.memset(T.DMF[:], 4096.0), [], ["DMF"], W)
-    iota(T.QX8[:], [[0, CW], [1, 16]], 0, 0, "QX8", W)
+    iota(T.QX[:], [[0, CW], [1, 16]], 0, 0, "QX", W)
     iota(T.DW0[:], [[2, W]], 2178 + P0, 0, "DW0", W)
-    if XPE:
-        iota(T.UZ[:], [[0, 64]], 0, 0, "UZ", 64)
     iota(T.K30[:], [[0, 32]], 30720, 0, "K30", 32)
-    FTK = [[], [], []]
+    FTK = [[], []]
 
     def late(t):
         after = ["G3" + SS[0]]
         if not t:
-            FTK[2].append("IDT")
             iota(T.IDT[:], [[1, H]], -P0 - 1024, 0, "IDT", H, False, ["TRI", "TRL", "TRS", "B14"])
-            op("G", lambda q: q.affine_select(T.QW[:], T.IDT[:, P0 + 1024:P0 + 1408], [[0, 384]], ALU.is_ge, 0.0, 0, 0), after + ["IDT"], ["QW"], 0.17 + 768 * CY)
-        for a in range(0, N0 + 384 * t, FTN):
-            n = min(FTN, N0 + 384 * t - a)
-            FTK[t].append("FT%d%d" % (t, a))
-            iota(T["FT%d" % t][:, a:a + n], [[0, n]], 2 * t - 1, 0, FTK[t][-1], n, t == 1, after)
+            select(T.QW[:], T.IDT[:, P0 + 1024:P0 + 1408], ALU.is_ge, 0.0, 0, after + ["IDT"], ["QW"], 384)
+            for u in range(2):
+                ft, n = T["FT%d" % u], (N0 + 384 * u) // 8
+                FTK[u].append("FT%d" % u)
+                iota(ft[:, 0:n], [[0, n]], 2 * u - 1, 0, FTK[u][0], n, u == 1, after)
+                for j in range(3):
+                    FTK[u].append("FT%d%d" % (u, j))
+                    dma("Y", ft[:, n << j:n << j + 1], ft[:, 0:n << j], "df%d%d" % (u, j), FTK[u][:-1], FTK[u][-1:], (n << j) // (2 + 2 * u))
 
     c = lambda i: T.C[:, i:i + 1]
     ts(T.PI[:, 1:2], T.PI[:, 0:1], 4, None, ALU.arith_shift_right, None, ["PI"], ["PI1"])
@@ -398,8 +397,12 @@ def rank_program(g, core, T, topo):
         (23, 6, 2048.0, -2048.0, M_, A_),
         (22, 2, 1.0, 23, A_, M_),
         (10, 22, -1.0, -32768.0, M_, A_),
-        (8, 6, 1.0e6, 69.5, M_, A_),
-        (9, 7, -1.0e6, 8, M_, A_),
+        (27, 2, float(NB[1]), 2048.0, ALU.is_lt, M_),
+        (28, 27, 69.5, None, A_, None),
+        (8, 6, 1.0e6, 28, M_, A_),
+        (29, 2, NB[0] + 0.5 * (NB[1] - NB[0]) - 0.5, -2048.0 * (NB[1] - NB[0]), EQ, M_),
+        (30, 7, -1.0e6, 29, M_, A_),
+        (9, 30, 8, None, A_, None),
         (11, 2, 1.0, -2048.0, A_, M_),
         (25, 3, -15.0, 15, M_, A_),
         (26, 3, NK - 16.0, 15, M_, A_),
@@ -411,6 +414,7 @@ def rank_program(g, core, T, topo):
         (14, 6, 1025.0, -1.0, M_, A_),
         (34, 3, -2.0 * H, float(H), M_, A_),
         (35, 3, float(-H), 1024.0 + P0 + H, M_, A_),
+        (24, 2, 2.0, 3, M_, A_),
         (39, 2, -2.0, 254.0 - 1024 - P0, M_, A_),
     ]:
         col = lambda x: c(x) if isinstance(x, int) else x
@@ -420,31 +424,29 @@ def rank_program(g, core, T, topo):
         ts(T.TH[:, 4 * t:4 * t + 4], T.Q[:, 0:4], c(11), c(9 - t), M_, A_, ["Q", "C11", "C%d" % (9 - t)], ["TH%d" % t])
     ID = T.ID2[:, 0:128]
     Q = T.Q[:, 0:128]
-    SW, BSK = ["SW%d" % j for j in range(4)], ["BS%d" % j for j in range(4)]
+    SW = ["SW%d" % j for j in range(4)]
     for j in range(4):
         u, d = j // 2, j % 2
         ts(T.SWB[:, 128 * j:128 * j + 128], Q, 16.0 * (u - d) - 1000.0 * u, c(16 + 3 * u), A_, EQ, ["Q", "C%d" % (16 + 3 * u)], [SW[j]])
     swb = lambda s, d: T.SWB[:, 128 * (2 * s + d):128 * (2 * s + d) + 128]
-    bs = lambda s, d: T.BS[:, 128 * (2 * s + d):128 * (2 * s + d) + 128]
     ts(T.SX[:], Q, -16.0, c(17), A_, EQ, ["Q", "C17"], ["SX"])
     ts(ID, Q, c(0), None, EQ, None, ["Q", "C0"], ["ID"])
-    act(T.ID2[:, 128:256], ID, ACT.Identity, 0.0, 1.0, ["ID"], ["ID2"], 128)
-    act(T.NI[:], ID, ACT.Identity, 0.0, -1.0, ["ID"], ["NI"], 128)
-    act(T.EV[:], ID, ACT.Identity, 0.0, c(12), ["ID", "C12"], ["EV"], 128)
-    act(T.EVX[:], T.SX[:], ACT.Identity, 0.0, c(12), ["SX", "C12"], ["EVX"], 128)
+    act(T.ID2[:, 128:256], ID, I_, 0.0, 1.0, ["ID"], ["ID2"], 128)
+    act(T.NI[:], ID, I_, 0.0, -1.0, ["ID"], ["NI"], 128)
+    act(T.EV[:], ID, I_, 0.0, c(12), ["ID", "C12"], ["EV"], 128)
+    act(T.EVX[:], T.SX[:], I_, 0.0, c(12), ["SX", "C12"], ["EVX"], 128)
     for m in ("EV", "EVX"):
-        act(T[m][:, 14:128:16], T[m][:, 12:128:16], ACT.Identity, 0.0, 1.0, [m], [m], 8)
-    act(T.IDS[:], ID, ACT.Identity, 0.0, -2.0 ** -23, ["ID"], ["IDS"], 128)
-    act(T.D14[:], ID, ACT.Identity, 0.0, c(7), ["ID", "C7"], ["D14"], 128)
+        act(T[m][:, 14:128:16], T[m][:, 12:128:16], I_, 0.0, 1.0, [m], [m], 8)
+    act(T.IDS[:], ID, I_, 0.0, -2.0 ** -23, ["ID"], ["IDS"], 128)
+    act(T.D14[:], ID, I_, 0.0, c(7), ["ID", "C7"], ["D14"], 128)
+    ts(T.SEL[:], T.Q[:, 0:32], c(24), None, EQ, None, ["Q", "C24"], ["SEL"])
     ts(T.ZD[:], T.Q[:], -15.0, c(15), A_, EQ, ["Q", "C15"], ["ZD"], 72)
     ts(T.BK[:], T.QG[:], c(1), None, EQ, None, ["QG", "C0"], ["BK"])
-
-    def select(out, in_, cmp, fill, sign, r, w):
-        op("G", lambda q: q.affine_select(out, in_, [[sign, 128]], cmp, fill, 0, -sign), r, w, 0.17 + 256 * CY)
-
-    act(T.T1[:], T.BK[:], ACT.Identity, 0.0, c(23), ["BK", "C23"], ["T1"], 128)
+    act(T.Z2[:], T.ZD[:], I_, 0.0, 2.0, ["ZD"], ["Z2"], 144)
+    act(T.ZN[:], T.ZD[:], I_, 0.0, -1.0, ["ZD"], ["ZN"], 144)
+    act(T.T1[:], T.BK[:], I_, 0.0, c(23), ["BK", "C23"], ["T1"], 128)
     select(T.T2[:], T.T1[:], ALU.is_gt, 0.0, -1, ["T1"], ["T2"])
-    act(T.T2[:, 15:128:16], T.T1[:, 15:128:16], ACT.Identity, 0.0, 1.0, ["T1"], ["T2"], 8)
+    act(T.T2[:, 15:128:16], T.T1[:, 15:128:16], I_, 0.0, 1.0, ["T1"], ["T2"], 8)
     select(T.TRI[:], T.T2[:], ALU.not_equal, 2048.0, 1, ["T2"], ["TRI"])
     select(T.TRL[:], T.BK[:], ALU.is_ge, 0.0, 1, ["BK"], ["TRL"])
     iota(T.TRL[:, 15:128:16], [[0, 8]], 0, 0, "TRL", 8)
@@ -458,33 +460,27 @@ def rank_program(g, core, T, topo):
         pk = "pD" + SS[b // hk]
         for j in range(2):
             o = 10 - (2 - j) * b
-            mm(T[pk][:, 128 * (b % hk):128 * (b % hk) + 128], ID, T.LA[:, j, o:o + 128], j == 0, j == 1, ["ID", "LA%d" % j], [pk], 128)
+            mm(T[pk][:, 8 * (b % hk):8 * (b % hk) + 8, :], ID, T.LA[:, j, o:o + 128], j == 0, j == 1, ["ID", "LA%d" % j], [pk], 128)
     for j in range(2):
-        act(T.LB[:, 128 * hk * j:128 * hk * (j + 1)], T["pD" + SS[j]][:, 0:128 * hk], ACT.Identity, 0.0, 1.0, ["pD" + SS[j]], ["LB%d" % j], 128 * hk)
+        act(T.LB[:, 128 * hk * j:128 * hk * (j + 1)], T["pD" + SS[j]][:, 0:8 * hk, :], I_, 0.0, 1.0, ["pD" + SS[j]], ["LB%d" % j], 128 * hk)
     iota(T.OF0[:], [[0, W // 2], [1, 2]], 0, 0, "OF0", W)
     ts(T.OFFS[:], T.OF0[:], c(34), c(5), M_, A_, ["OF0", "C34", "C5"], ["OFFS"], W)
-    ts(T.DIAG[:], T.QX8[:], c(2), None, EQ, None, ["QX8", "C0"], ["DIAG"], W // 2)
+    ts(T.DIAG[:], T.QX[:], c(2), None, EQ, None, ["QX", "C0"], ["DIAG"], W // 2)
     tt(T.KD[:], T.DIAG[:], T.DW0[:], M_, ["DIAG", "DW0"], ["KD"], 2 * W)
     ts(T.DMF[:, 0:W:16], T.Q[:, 0:W:16], -2.0, c(39), M_, A_, ["Q", "C39"], ["DMF"])
-    XT = ["XT%d" % j for j in range(4)]
-
-    def other():
-        for j in range(4):
-            pk = "pS%d" % (j % 2)
-            mm(T[pk][:], T.SX[:], T.X2[:, P0 + 512 * j:P0 + 512 * j + 512], True, True, ["SX", XO[j]], [pk], 512)
-            o = T.X2[:, H + P0 + 512 * j:H + P0 + 512 * j + 512]
-            if OE[j] == "V":
-                cp(o, T[pk][:], [pk], [XT[j]], 512)
-            else:
-                act(o, T[pk][:], ACT.Identity, 0.0, 1.0, [pk], [XT[j]], 512)
-
-    other()
-    XT = XT + ["XTp"]
+    XT = ["XT%d" % j for j in range(4)] + ["XTp"]
+    for j in range(4):
+        pk, o = "pS%d" % (j % 2), T.X2[:, H + P0 + 512 * j:H + P0 + 512 * j + 512]
+        mm(T[pk][:], T.SX[:], T.X2[:, P0 + 512 * j:P0 + 512 * j + 512], True, True, ["SX", "XO"], [pk], 512)
+        if j % 2:
+            act(o, T[pk][:], I_, 0.0, 1.0, [pk], [XT[j]], 512)
+        else:
+            cp(o, T[pk][:], [pk], [XT[j]], 512)
 
     ix = {s: NS - 1 - st[s] for s in SS}
     sl = lambda s: slice(CW * ix[s], CW * ix[s] + CW)
     sw = lambda s: slice(W * ix[s], W * ix[s] + W)
-    XOWN = XO + ["XOp", "XOn"]
+    XOWN = ["XO", "XOp", "XOn"]
     xall = lambda t: XOWN + XT + ["XTn"] * t
     xwin = lambda t: T.X2[:, 0:H + N0 + 384 * t]
     xown = lambda t: T.X2[:, 0:N0 + 384 * t]
@@ -499,85 +495,82 @@ def rank_program(g, core, T, topo):
         ts(T.VL[:, :, CW + NK * u:CW + NK * u + NK], T.W0I[:, u:24:2], float(P0), None, A_, None, ["W0I"], ["VX%s%d" % (s, u) for s in SS])
     vl = lambda s, a, b: T.VL[:, ix[s], a:b]
 
-    def agather(s, t, key=True, e="V"):
+    def agather(s, t, last=False, e="V"):
         src, r = T.ATI[:, 0:N0 + 384 * t].indirect(vl(s, 0, CW)), ["AT", "ATp", "VL" + s] + ["ATn"] * t
-        if e == "V":
-            ts(T.GA[:, sw(s)], src, -1024.0, None, A_, None, r, ["GA" + s], gat(W))
+        if e == "S":
+            act(T.GA[:, sw(s)], src, I_, -1024.0, 1.0, r, ["GA" + s], gat(W))
         else:
-            act(T.GA[:, sw(s)], src, ACT.Identity, -1024.0, 1.0, r, ["GA" + s], gat(W))
-        if key:
+            ts(T.GA[:, sw(s)], src, -1024.0, None, A_, None, r, ["GA" + s], gat(W))
+        if not last:
             dma("Y", T.GA3[:, sl(s), :], T.GA[:, sw(s)], "dg" + s, ["GA" + s], ["G3" + s], W // 4)
 
     def xgather(s, t, bias=0.0):
-        src, r = xown(t).indirect(vl(s, CW, 2 * CW)), XOWN[:5 + t] + ["VX%s0" % s, "VX%s1" % s]
-        act(T.XV[:, sw(s)], src, ACT.Identity, bias, 1.0, r, ["XV" + s], gat(W))
+        src, r = xown(t).indirect(vl(s, CW, 2 * CW)), XOWN[:2 + t] + ["VX%s0" % s, "VX%s1" % s]
+        act(T.XV[:, sw(s)], src, I_, bias, 1.0, r, ["XV" + s], gat(W))
 
-    def swap4(out, o0, mat, src, key, r, stop, start=False):
+    def swap4(out, o0, src, key, r, stop, start=False):
         for u in range(2):
             for v in range(2):
-                mm(out[:, o0 + v:o0 + CW:2, :], mat(v, u), src(u), start and u + v == 0, stop and u + v == 2, r, [key], W // 2)
+                mm(out[:, o0 + v:o0 + CW:2, :], swb(v, u), src(u), start and u + v == 0, stop and u + v == 2, r + SW, [key], W // 2)
 
     def xv(s):
         return lambda u: T.XV[:, W * ix[s] + W // 2 * u:W * ix[s] + W // 2 * (u + 1)]
 
-    def zstep(s, first, final=False):
-        pk, z = "pK" + s, B("Z", s)
+    def zstep(s, first, final=False, e="S"):
+        pk, z, z0 = "pK" + s, B("Z", s), "Z%s0" % s
         o = T[pk][:, CW:2 * CW, :]
         if not first:
-            mm(o, ID, z[:, 0:W], True, False, ["ID", "Z%s0" % s], [pk], W)
-        swap4(T[pk], CW, swb, xv(s), pk, ["XV" + s] + SW, True, first)
+            mm(o, ID, z[:, 0:W], True, False, ["ID", z0], [pk], W)
+        swap4(T[pk], CW, xv(s), pk, ["XV" + s], True, first)
         if final:
-            if Z2E == "S":
-                act(z[:, 3 * W:4 * W], z[:, 0:W], ACT.Identity, 0.0, 2.0, ["Z%s0" % s], ["Z%s3" % s], W)
-            else:
-                ts(z[:, 3 * W:4 * W], z[:, 0:W], 2.0, None, M_, None, ["Z%s0" % s], ["Z%s3" % s])
-            select(B("ZF", s)[:], z[:, 0:W], ALU.is_ge, 0.0, 0, ["Z%s0" % s], ["ZF" + s])
-            tt(B("GT", s)[:], o, z[:, 3 * W:4 * W], ALU.is_gt, [pk, "Z%s3" % s], ["GT" + s], W)
+            ts(z[:, GS * W:GS * W + W], z[:, 0:W], 2.0, None, M_, None, [z0], ["Z2" + s])
+            select(B("ZF", s)[:], z[:, 0:W], ALU.is_ge, 0.0, 0, [z0], ["ZF" + s])
+            tt(B("GT", s)[:], o, z[:, GS * W:GS * W + W], ALU.is_gt, [pk, "Z2" + s], ["GT" + s], W)
             return
-        bias, scale = 128.0 if first else 63.75, 1.0 if first else 0.5
-        for d in range(GS):
-            if ZE[min(d, len(ZE) - 1)] == "S":
-                act(z[:, W * d:W * d + W], o, ACT.Identity, bias, scale, [pk], ["Z%s%d" % (s, d)], W)
-            elif ZE[min(d, len(ZE) - 1)] == "G" and (not first or s in GF):
-                select(z[:, W * d:W * d + W], z[:, 0:W], ALU.is_ge, 0.0, 0, ["Z%s0" % s], ["Z%s%d" % (s, d)])
-            elif d:
-                cp(z[:, W * d:W * d + W], z[:, 0:W], ["Z%s0" % s], ["Z%s%d" % (s, d)], W // 2)
+        if e == "V":
+            ts(z[:, 0:W], o, 0.5, 63.75, M_, A_, [pk], [z0], W)
+        else:
+            act(z[:, 0:W], o, I_, 128.0 if first else 63.75, 1.0 if first else 0.5, [pk], [z0], W)
+        for d in range(1, GS):
+            if first:
+                cp(z[:, W * d:W * d + W], z[:, 0:W], [z0], ["Z%s%d" % (s, d)], W // 2)
             else:
-                ts(z[:, 0:W], o, scale, bias, M_, A_, [pk], ["Z%s0" % s], W)
+                select(z[:, W * d:W * d + W], z[:, 0:W], ALU.is_ge, 0.0, 0, [z0], ["Z%s%d" % (s, d)])
 
-    def lists(s, L, e="V", shared=False):
-        lt, cl, pd = B("LT", s), B("CL", s), (bank() if LB_ == "S" else "pK" + s) if shared else "pD" + s
-        o = T[pd][:, 24:24 + L // 2, :] if shared else T[pd][:, 256:256 + CW * L]
-        col = lambda j: o[:, :, j:16:CW] if shared else o[:, j:CW * L:CW]
-        keys = ["CL%s%d" % (s, x) for x in range(L - 13)]
-        tr(lt[:], T.GA[:, sw(s)], ["GA" + s], ["LT" + s], W // 2)
-        two = OFF2 and not shared
+    def lists(s, L, last=False):
+        pd = bank() if last else "pD" + s
+        o, keys = T[pd][:, 16:16 + L, 0:CW], ["CL%s%d%s" % (s, x, y) for x in range(L - 13) for y in "ab"]
+        two = OFF2 and not last
         if not two:
             mm(o, ID, T.OFFS[:, 0:CW * L], True, False, ["ID", "OFFS"], [pd], CW * L)
-        for j in range(CW):
-            mm(col(j), ID, lt[:, 16 * j:16 * j + L], two and not j, j == CW - 1, ["ID", "LT" + s], [pd], 64)
+        if not LTP:
+            tr(B("LT", s)[:], T.GA[:, sw(s)], ["GA" + s], ["LT" + s], W // 2)
+            for j in range(CW):
+                mm(o[:, :, j], ID, B("LT", s)[:, 16 * j:16 * j + L], two and not j, j == CW - 1, ["ID", "LT" + s], [pd], 64)
+        for b in range(NK * LTP):
+            for a in range(0, 128, 32):
+                w = W * ix[s] + 32 * b
+                mm(T[pd][a:a + 32, 16:16 + L, 2 * b:2 * b + 2], T.GA[a:a + 32, w:w + 32], T.SEL[a:a + 32, 0:2 * L], two and b == 0, b == NK - 1,
+                   ["SEL", "GA" + s], [pd], 32, 32)
         if two:
             for h in range(2):
-                ts(cl[:, h:CW * L:2], o[:, h:CW * L:2], c(5 + 30 * h), None, A_, None, [pd, "C5", "C35"], [k + "ab"[h] for k in keys], CW * L // 2)
-        elif e == "V":
-            cp(cl[:, 0:CW * L], o, [pd], [k + x for k in keys for x in "ab"], CW * L)
+                ts(B("CL", s)[:, h:CW * L:2], o[:, :, h:CW:2], c(5 + 30 * h), None, A_, None, [pd, "C5", "C35"], keys[h::2])
+        elif last:
+            act(B("CL", s)[:, 0:CW * L], o, I_, 0.0, 1.0, [pd], keys, CW * L)
         else:
-            act(cl[:, 0:CW * L], o, ACT.Identity, 0.0, 1.0, [pd], [k + x for k in keys for x in "ab"], CW * L)
+            cp(B("CL", s)[:, 0:CW * L], o, [pd], keys, CW * L)
 
     def begin(s, t):
         if t:
             w, lt, pd = sw(s), B("LT", s), "pD" + s
-            act(T.LG[:, w], T.FT0[:].indirect(vl(s, 0, CW)), ACT.Identity, -1024.0, 1.0, FTK[0] + ["VL" + s], ["LG" + s], gat(W))
+            act(T.LG[:, w], T.FT0[:].indirect(vl(s, 0, CW)), I_, -1024.0, 1.0, FTK[0] + ["VL" + s], ["LG" + s], gat(W))
             tr(lt[:], T.LG[:, w], ["LG" + s], ["LT" + s], W // 2)
             for h in range(2):
-                o, i, k = B("CL", s)[:, 14 * CW + h:15 * CW:2], lt[:, 16 * h + 14:W:32], "C%d" % (5 + 30 * h)
-                if BE[0] == "V":
-                    ts(o, i, c(5 + 30 * h), None, A_, None, ["LT" + s, k], ["CL%s1%s" % (s, "ab"[h])])
-                else:
-                    act(o, i, ACT.Identity, c(5 + 30 * h), 1.0, ["LT" + s, k], ["CL%s1%s" % (s, "ab"[h])], NK)
-            mm(T[pd][:, 0:W], ID, T.GA[:, w], True, False, ["ID", "GA" + s], [pd], W)
-            mm(T[pd][:, 0:W], T.D14[:], T.LG[:, w], False, True, ["D14", "LG" + s], [pd], W)
-            act(T.GA3[:, sl(s), :], T[pd][:, 0:W], ACT.Identity, c(36), 1.0, [pd, "C36"], ["G3" + s], W)
+                ts(B("CL", s)[:, 14 * CW + h:15 * CW:2], lt[:, 16 * h + 14:W:32], c(5 + 30 * h), None, A_, None,
+                   ["LT" + s, "C%d" % (5 + 30 * h)], ["CL%s1%s" % (s, "ab"[h])])
+            mm(T[pd][:, 0:CW, :], ID, T.GA[:, w], True, False, ["ID", "GA" + s], [pd], W)
+            mm(T[pd][:, 0:CW, :], T.D14[:], T.LG[:, w], False, True, ["D14", "LG" + s], [pd], W)
+            act(T.GA3[:, sl(s), :], T[pd][:, 0:CW, :], I_, c(36), 1.0, [pd, "C36"], ["G3" + s], W)
         else:
             agather(s, 0)
             lists(s, 14)
@@ -589,18 +582,12 @@ def rank_program(g, core, T, topo):
         zk = lambda n: ["Z%s%d" % (s, d) for d in range(n)]
         abk = lambda i, n: ["AB%s%d" % (s, x) for x in range(i, i + n)]
         cdk = lambda i, n: ["CD%s%d" % (s, x) for x in range(i, i + n)]
-        clk = lambda i, n: ["CL%s%d%s" % (s, x, y) for x in range(1 + (i + n > 14)) for y in "ab"]
-        sums, ns = [], 0
-        plan = PLAN[t]
-        if (t, k, s) in HEAVY:
-            plan = (plan[0], ("S", 0, 3)) + plan[2:]
-        for mode, i, n in plan:
-            part = slice(W * i, W * (i + n))
+        sums = []
+        for mode, i, n in PLAN[t]:
+            part, src = slice(W * i, W * (i + n)), xwin(t).indirect(cl[:, CW * i:CW * (i + n)])
+            r = xall(t) + ["CL%s%d%s" % (s, x, y) for x in range(1 + (i + n > 14)) for y in "ab"]
             if mode != "S":
-                for j in range(i, i + n, GS):
-                    m = min(GS, i + n - j)
-                    tt(cd[:, W * j:W * (j + m)], xwin(t).indirect(cl[:, CW * j:CW * (j + m)]), z[:, 0:W * m], ALU.subtract,
-                       xall(t) + clk(j, m) + zk(m), cdk(j, m), gat(W * m))
+                tt(cd[:, part], src, z[:, 0:W * n], ALU.subtract, r + zk(n), cdk(i, n), gat(W * n))
             if mode == "A":
                 act(ab[:, part], cd[:, part], ACT.Abs, 128.0, 1.0, cdk(i, n), abk(i, n), W * n)
             if mode == "B":
@@ -609,68 +596,58 @@ def rank_program(g, core, T, topo):
             else:
                 sums += [("ZD", ab, x, abk(x, 1)) for x in range(i, i + n)]
             if mode == "S":
-                q, xk = bank(), "XG%s%d" % (s, ns % 2)
-                xg, o = B("XG", s)[:, ns % 2, 0:W * n], T[q][:, 0:CW * n, :]
-                ns += 1
-                act(xg, xwin(t).indirect(cl[:, CW * i:CW * (i + n)]), ACT.Identity, 0.0, 1.0, xall(t) + clk(i, n), [xk], gat(W * n))
+                q = bank()
+                xg, o = B("XG", s)[:, 0:W * n], T[q][:, 0:CW * n, :]
+                act(xg, src, I_, 0.0, 1.0, r, ["XG" + s], gat(W * n))
                 mm(o, T.NI[:], z[:, 0:W * n], True, False, ["NI"] + zk(n), [q], W * n)
-                mm(o, ID, xg, False, True, ["ID", xk], [q], W * n)
+                mm(o, ID, xg, False, True, ["ID", "XG" + s], [q], W * n)
                 act(ab[:, part], o, ACT.Abs, 128.0, 1.0, [q], abk(i, n), W * n)
-        for j in range(XPE):
-            mm(pd[:, 384:512], T.D14[:], T.BK[:], True, True, ["D14", "BK"], ["pD" + s], 128)
         for j in range(k):
-            mm(pd[:, 0:W], T.TRL[:], B("R", s)[:, CW * j:CW * j + CW, :], j == 0, False, ["TRL", "R%s%d" % (s, j)], ["pD" + s], W)
+            mm(pd[:, 0:CW, :], T.TRL[:], B("R", s)[:, CW * j:CW * j + CW, :], j == 0, False, ["TRL", "R%s%d" % (s, j)], ["pD" + s], W)
         for j, (mat, src, x, keys) in enumerate(sums):
-            mm(pd[:, 0:W], T[mat][:, 15 - x:143 - x], src[:, W * x:W * x + W], j == 0 and not k, j == len(sums) - 1,
+            mm(pd[:, 0:CW, :], T[mat][:, 15 - x:143 - x], src[:, W * x:W * x + W], j == 0 and not k, j == len(sums) - 1,
                [mat] + keys, ["pD" + s], W)
-        swap4(B("pK", s), 0, swb, lambda u: T.GA3[:, CW * ix[s] + u:CW * ix[s] + CW:2, :], "pK" + s, ["G3" + s] + SW, False, True)
-
-    def turn(s, src, key, out, okey, col, add=False):
-        pd = "pD" + s if col else "pS0"
-        o = T[pd][:, col:col + 32] if col else T[pd][:, 0:2, :]
-        if add:
-            mm(o, ID, T.K30[:], True, False, ["ID", "K30"], [pd], 64)
-        for b in range(NK):
-            mm(o, T.LB[:, 128 * b:128 * b + 128], src[:, 2 * b:2 * b + 2, :], b == 0 and not add, b == NK - 1, ["LB0", "LB1", key], [pd], 64)
-        tr(out[:], o, [pd], [okey])
+        swap4(B("pK", s), 0, lambda u: T.GA3[:, CW * ix[s] + u:CW * ix[s] + CW:2, :], "pK" + s, ["G3" + s], False, True)
 
     def choose(s, k, t):
         last = k == 3
-        r, rk, kt, pk = B("R", s)[:, CW * k:CW * k + CW, :], "R%s%d" % (s, k), B("KT", s), "pK" + s
-        th, o = T.TH[:, 4 * t + k:4 * t + k + 1], T[pk][:, 0:CW, :]
-        ge = GE[t][(NS * k + st[s]) % len(GE[t])]
-        if ge == "V":
-            ts(B("VAL", s)[:], B("pD", s)[:, 0:W], th, 2.0, ALU.is_lt, M_, ["pD" + s, "TH%d" % t], ["VAL" + s], W)
+        r, rk, kt, pk, pd = B("R", s)[:, CW * k:CW * k + CW, :], "R%s%d" % (s, k), B("KT", s), "pK" + s, "pD" + s
+        on, th = ON[t][(NS * k + st[s]) % len(ON[t])], T.TH[:, 4 * t + k:4 * t + k + 1]
+        if on[0] == "V":
+            ts(B("VAL", s)[:], T[pd][:, 0:CW, :], th, 2.0, ALU.is_lt, M_, [pd, "TH%d" % t], ["VAL" + s], W)
         else:
-            act(B("VAL", s)[:], B("pD", s)[:, 0:W], ACT.Sign, th, -1.0, ["pD" + s, "TH%d" % t], ["VAL" + s], W)
-        mm(o, T.TRI[:], B("VAL", s)[:], False, True, ["TRI", "VAL" + s], [pk], W)
-        ts(r, o, -4096.0 if ge == "V" else c(10), LOW, A_, ALU.max, [pk, "C10"], [rk], W)
-        turn(s, r, rk, kt, "KT" + s, 192, last)
-        ts(vl(s, 0, 2 * CW), kt[:, 0:2 * CW], (1024.0 if last else 31744.0) + P0, None, A_, None, ["KT" + s], ["VL" + s, "VX%s0" % s, "VX%s1" % s])
+            act(B("VAL", s)[:], T[pd][:, 0:CW, :], ACT.Sign, th, -1.0, [pd, "TH%d" % t], ["VAL" + s], W)
+        mm(T[pk][:, 0:CW, :], T.TRI[:], B("VAL", s)[:], False, True, ["TRI", "VAL" + s], [pk], W)
+        ts(r, T[pk][:, 0:CW, :], -4096.0 if on[0] == "V" else c(10), LOW, A_, ALU.max, [pk, "C10"], [rk], W)
+        o = T[pd][:, 12:14, :]
         if last:
-            act(T.VB[:, sw(s)], T.IDT[:].indirect(vl(s, 0, CW)), ACT.Identity, 0.0, 1.0, FTK[2] + ["VL" + s], ["VB" + s], gat(W))
+            mm(o, ID, T.K30[:], True, False, ["ID", "K30"], [pd], 64)
+        for b in range(NK):
+            mm(o, T.LB[:, 128 * b:128 * b + 128], r[:, 2 * b:2 * b + 2, :], b == 0 and not last, b == NK - 1, ["LB0", "LB1", rk], [pd], 64)
+        tr(kt[:], o, [pd], ["KT" + s])
+        add, keys = (1024.0 if last else 31744.0) + P0, ["VL" + s, "VX%s0" % s, "VX%s1" % s]
+        if on[1] == "V":
+            ts(vl(s, 0, 2 * CW), kt[:, 0:2 * CW], add, None, A_, None, ["KT" + s], keys)
+        else:
+            act(vl(s, 0, 2 * CW), kt[:, 0:2 * CW], I_, add, 1.0, ["KT" + s], keys, 2 * CW)
+        if last:
+            act(T.VB[:, sw(s)], T.IDT[:].indirect(vl(s, 0, CW)), I_, 0.0, 1.0, ["IDT", "VL" + s], ["VB" + s], gat(W))
         if not (last and t):
-            agather(s, t, not last, BE[2] if last else BE[4])
+            agather(s, t, last, "S" if last else on[2])
         xgather(s, t, 128.0 * last)
-        zstep(s, False, last)
-        if not last:
-            lists(s, 14 + t, BE[5])
-        elif not t and LB_ != "L":
-            lists(s, 14, BE[1], True)
+        zstep(s, False, last, on[3])
+        if not (last and t):
+            lists(s, 14 + t, last)
 
     def votes(s, t):
-        pd, zn, pk = "pD" + s, "ZN%d" % t, "pK" + s
-        if KWB:
-            mm(T[pd][:, 0:W], T.BK[:], B("GT", s)[:], True, True, ["BK", "GT" + s], [pd], W)
-            tr(B("KW", s)[:], T[pd][:, 0:W], [pd], ["KW" + s], W)
-            ts(T.WT[:, sl(s)], B("KW", s)[:, 0:W:16], 8.5, EPS, ALU.is_lt, A_, ["KW" + s], ["WT" + s])
-        else:
-            turn(s, B("GT", s), "GT" + s, B("KW", s)[:, 0:32], "KW" + s, 224)
-            ts(T.WT[:, sl(s)], B("KW", s)[:, 0:CW], 8.5, EPS, ALU.is_lt, A_, ["KW" + s], ["WT" + s])
-        swap4(T[pk], 0, swb, lambda u: B("ZF", s)[:, u:CW:2, :], pk, ["ZF" + s] + SW, False, True)
+        pd, zn, pk = "pD" + s, "ZN%d" % t, bank() if s == SS[-1] else "pK" + s
+        mm(T[pd][:, 0:CW, :], T.BK[:], B("GT", s)[:], True, True, ["BK", "GT" + s], [pd], W)
+        tr(B("KW", s)[:], T[pd][:, 0:CW, :], [pd], ["KW" + s], W)
+        ts(T.WT[:, sl(s)], B("KW", s)[:, 0:W:16], 8.5, EPS, ALU.is_lt, A_, ["KW" + s], ["WT" + s])
+        swap4(T[pk], 0, lambda u: B("ZF", s)[:, u:CW:2, :], pk, ["ZF" + s], False, True)
         for u in range(2):
             mm(T[pk][:, u:CW:2, :], ID, xv(s)(u), False, u == 1, ["ID", "XV" + s], [pk], W // 2)
-        act(T[zn][:, sw(s)], T[pk][:, 0:CW, :], ACT.Identity, -0.25, 0.5, [pk], [zn + s], W)
+        act(T[zn][:, sw(s)], T[pk][:, 0:CW, :], I_, -0.25, 0.5, [pk], [zn + s], W)
         trs = []
         for q in range(8):
             if q == rank or 48 * q // W != ix[s]:
@@ -687,81 +664,52 @@ def rank_program(g, core, T, topo):
     def flips(t):
         top = level[0]
         if not t:
-            if BE[3] == "V":
-                ts(T.ATI[:, N0:H], T.GA[:], c(6), c(14), M_, A_, each("GA") + ["C6", "C14"], ["ATn"], 384)
-            else:
-                act(T.ATI[:, N0:H], T.GA[:], ACT.Identity, c(14), c(6), each("GA") + ["C6", "C14"], ["ATn"], 384)
-
+            act(T.ATI[:, N0:H], T.GA[:], I_, c(14), c(6), each("GA") + ["C6", "C14"], ["ATn"], 384)
         for h, s in enumerate(SS):
-            level[0] = top - FLEV[0] + FLEV[1] * h
-            pd, pk, w, bl = "pD" + s, "pK" + s, sw(s), sl(s)
-            ear, rest, ft = T[pd][:, 256:256 + W], T[pk][:, 2 * CW:3 * CW, :], "FT%d" % t
-            early, two = s in EARLY, not t and s in OTHER
-
-            def compare(e0, name, s2, o2, r, sums):
-                for b in range(CW - 1, -1, -1):
-                    e, key = e0 + CW * b, "%s%s%d" % (name, s, b)
-                    ts(T.E[:, e:e + CW, :], T.VB[:, w], B("KT", s)[:, b:b + 1], s2(b), EQ, o2, ["VB" + s, "KT" + s] + r, [key], W // 2)
-                    if "r" in sums:
-                        mm(rest[:, 0:b + 1, :], T.B14[:], T.E[:, e:e + b + 1, :], b == CW - 1 and t == 1, b == 0 and not h, ["B14", key], [pk], 16 + 16 * b)
-                    if "e" in sums and b < CW - 1:
-                        mm(ear[:, 16 * b + 16:W], T.BK[:], T.E[:, e + b + 1:e + CW, :], False, False, ["BK", key], [pd], W - 16 - 16 * b)
-                if "e" in sums:
-                    mm(ear, T.TRS[:], T.E[:, e0:e0 + CW * CW:CW + 1, :], False, True, ["TRS"] + ["%s%s%d" % (name, s, b) for b in range(CW)], [pd], W)
-
-            def listed():
-                act(T.DM[:, w], ear, ACT.Relu, -1408.0, -2.0 ** 23, [pd], ["DM" + s], W)
-                V(lambda v, w=w: v.tensor_tensor_scan(T.SC[:, w], T.DMF[:], T.DM[:, w], 4096.0, ALU.min, A_), ["DMF", "DM" + s], ["SC" + s], W)
-                sc = T.SC[:, w.start + 15:w.stop:16]
-                if XE2 == "V":
-                    ts(T.XOFF[:, bl], sc, 1024.0 + P0, None, A_, None, ["SC" + s], ["XOFF" + s])
-                else:
-                    act(T.XOFF[:, bl], sc, ACT.Identity, 1024.0 + P0, 1.0, ["SC" + s], ["XOFF" + s], CW)
-                if two:
-                    mm(T[pd][:, 0:CW], T.SX[:], sc, True, True, ["SX", "SC" + s], [pd], 64)
-                    if BE[1] == "V":
-                        ts(T.XOF2[:, bl], T[pd][:, 0:CW], 1024.0 + P0, None, A_, None, [pd], ["XOF2" + s])
-                    else:
-                        act(T.XOF2[:, bl], T[pd][:, 0:CW], ACT.Identity, 1024.0 + P0, 1.0, [pd], ["XOF2" + s], CW)
-
+            level[0] = top - 1
+            pd, pk, w, bl, e0, two = "pD" + s, "pK" + s, sw(s), sl(s), CW * CW * h, 1 if COPY else 2 - t
+            ear, rest, ft = T[pd][:, 16:16 + CW, :], T[pk][:, 2 * CW:3 * CW, :], T["FT%d" % t][:]
             mm(ear, T.IDS[:], T.KD[:], True, False, ["IDS", "KD"], [pd], W)
             mm(ear, T.IDS[:], T.VB[:, w], False, False, ["IDS", "VB" + s], [pd], W)
             if not t:
                 mm(rest, T.D14[:], T.QW[:, w], True, False, ["D14", "QW"], [pk], W)
-            if early:
-                compare(CW * CW * h, "E", lambda b: 1.0, M_, [], "e")
-            else:
-                compare(CW * CW * h, "E", lambda b: T.WT[:, bl.start + b:bl.start + b + 1], M_, ["WT" + s], "re")
-            listed()
-            if early:
-                compare(CW * CW * (3 + h), "N", lambda b: T.WT[:, bl.start + b:bl.start + b + 1], M_, ["WT" + s], "r")
+            for b in range(CW - 1, -1, -1):
+                e, key, n = e0 + CW * b, "E%s%d" % (s, b), bl.start + b
+                ts(T.E[:, e:e + CW, :], T.VB[:, w], B("KT", s)[:, b:b + 1], T.WT[:, n:n + 1], EQ, M_, ["VB" + s, "KT" + s, "WT" + s], [key], W // 2)
+                mm(rest[:, 0:b + 1, :], T.B14[:], T.E[:, e:e + b + 1, :], b == CW - 1 and t == 1, b == 0 and not h, ["B14", key], [pk], 16 + 16 * b)
+                if b < CW - 1:
+                    mm(ear[:, b + 1:CW, :], T.BK[:], T.E[:, e + b + 1:e + CW, :], False, False, ["BK", key], [pd], W - 16 - 16 * b)
+            mm(ear, T.TRS[:], T.E[:, e0:e0 + CW * CW:CW + 1, :], False, True, ["TRS"] + ["E%s%d" % (s, b) for b in range(CW)], [pd], W)
+            act(T.DM[:, w], ear, ACT.Relu, -1408.0, -2.0 ** 23, [pd], ["DM" + s], W)
+            V(lambda v, w=w: v.tensor_tensor_scan(T.SC[:, w], T.DMF[:], T.DM[:, w], 4096.0, ALU.min, A_), ["DMF", "DM" + s], ["SC" + s], W)
+            sc = T.SC[:, w.start + 15:w.stop:16]
+            ts(T.XOFF[:, bl], sc, 1024.0 + P0, None, A_, None, ["SC" + s], ["XOFF" + s])
+            if two == 2:
+                mm(T[pd][:, 0, 0:CW], T.SX[:], sc, True, True, ["SX", "SC" + s], [pd], 64)
+                act(T.XOF2[:, bl], T[pd][:, 0, 0:CW], I_, 1024.0 + P0, 1.0, [pd], ["XOF2" + s], CW)
             if h:
-                f, bias, scale = (ACT.Identity, 0.5, -0.5) if t else (ACT.Relu, 0.0, c(21))
-                act(T.FG[:, w], T[ft][:].indirect(vl(s, 0, CW)), f, bias, scale, FTK[t] + ["VL" + s, "C21"], ["FG" + s], gat(W))
+                f, bias, scale = (I_, 0.5, -0.5) if t else (ACT.Relu, 0.0, c(21))
+                act(T.FG[:, w], ft.indirect(vl(s, 0, CW)), f, bias, scale, FTK[t] + ["VL" + s, "C21"], ["FG" + s], gat(W))
                 mm(rest, ID, T.FG[:, w], False, True, ["ID", "FG" + s], [pk], W)
             if not t:
-                act(T.AS[:, w], rest, ACT.Identity, c(13), 1.0, [pk, "C13"], ["AS" + s], W)
-                cp(T[ft][:].indirect(T.XOFF[:, bl]), T.AS[:, w], ["AS" + s, "XOFF" + s], FTK[t], sca())
+                act(T.AS[:, w], rest, I_, c(13), 1.0, [pk, "C13"], ["AS" + s], W)
+                cp(ft.indirect(T.XOFF[:, bl]), T.AS[:, w], ["AS" + s, "XOFF" + s], FTK[t], sca())
             act(T.FL[:, w], rest, ACT.Sign, 0.875, -1.0, [pk], ["FL" + s], W)
             if t and h < NS - 1:
-                cp(T[ft][:].indirect(T.XOFF[:, bl]), T.FL[:, w], ["FL" + s, "XOFF" + s], FTK[t], sca())
-            for j, (a, b) in enumerate((("ID2", "EV"), ("SX", "EVX"))[:1 + two]):
+                cp(ft.indirect(T.XOFF[:, bl]), T.FL[:, w], ["FL" + s, "XOFF" + s], FTK[t], sca())
+            for j, (a, b) in enumerate((("ID2", "EV"), ("SX", "EVX"))[:two]):
                 o = T[pk][:, j * CW:j * CW + CW, :]
                 for u in range(2):
                     mm(o[:, u:CW:2, :], T[a][:, 0:128], xv(s)(u), u == 0, False, ["ID", a, "XV" + s], [pk], W // 2)
                 mm(o, T[b][:], T.FL[:, w], False, True, [b, "FL" + s], [pk], W)
-            act(T.XN[:, h, 0:W * (1 + two)], T[pk][:, 0:CW * (1 + two), :], ACT.Abs, c(20), 1.0, [pk, "C20"], ["XN" + s], W * (1 + two))
-            cp(xown(t).indirect(T.XOFF[:, bl]), T.XN[:, h, 0:W], ["XN" + s, "XOFF" + s], XOWN[:5 + t], sca())
-            if two:
+            act(T.XN[:, h, 0:W * two], T[pk][:, 0:CW * two, :], ACT.Abs, c(20), 1.0, [pk, "C20"], ["XN" + s], W * two)
+            cp(xown(t).indirect(T.XOFF[:, bl]), T.XN[:, h, 0:W], ["XN" + s, "XOFF" + s], XOWN[:2 + t], sca())
+            if two == 2:
                 cp(T.X2[:, H:H + N0].indirect(T.XOF2[:, bl]), T.XN[:, h, W:2 * W], ["XN" + s, "XOF2" + s], XT, sca())
-            elif not t and (h == NS - 1 or SS[h + 1] in OTHER):
-                if COPY == "P":
-                    other()
-                else:
-                    for i in range(8):
-                        a, o = 16 * i, 16 * (i ^ 1)
-                        dma("YS"[i % 2], T.X2[o:o + 16:2, H + P0:H + N0], T.X2[a:a + 16:2, P0:N0], "dd", XO, XT, 32)
         level[0] = top
+        for i in range(8 * (COPY and not t)):
+            a, o = 16 * i, 16 * (i ^ 1)
+            dma("YS"[i % 2], T.X2[o:o + 16:2, H + P0:H + N0], T.X2[a:a + 16:2, P0:N0], "dd", ["XO"], XT, 32)
         if not t:
             dma("Y", T.ATI[14:128:16, P0:N0], T.FT0[14:128:16, P0:N0], "da", FTK[0], ["AT"], 64)
 
@@ -773,10 +721,10 @@ def rank_program(g, core, T, topo):
             src = T[zn if r == rank else rz]
             mm(T[pk][:, 3 * r:3 * r + 3, :], T.ID2[:, o:o + 128], src[:, 48 * r:48 * r + 48], True, True, ["ID", "ID2", rz] + each(zn), [pk], 64)
         out, key = (T.XM[:], "XM") if t else (T.X2[:, N0:H], "XOn")
-        act(out, T[pk][:, 0:24, :], ACT.Identity, -128.0, 1.0, [pk], [key], 384)
+        act(out, T[pk][:, 0:24, :], I_, -128.0, 1.0, [pk], [key], 384)
         if not t:
             mm(T.pS1[:, 0:24, :], T.SX[:], out, True, True, ["SX", key], ["pS1"], 384)
-            act(T.X2[:, H + N0:NX], T.pS1[:, 0:24, :], ACT.Identity, 0.0, 1.0, ["pS1"], ["XTn"], 384)
+            act(T.X2[:, H + N0:NX], T.pS1[:, 0:24, :], I_, 0.0, 1.0, ["pS1"], ["XTn"], 384)
 
     for t in range(2):
         for s in SS:
@@ -788,15 +736,11 @@ def rank_program(g, core, T, topo):
                 level[0] = 20 * t + NS * k + st[s]
                 if (k, s) == (1, SS[0]):
                     a, n = (2048, 384) if t else (0, 2048)
-                    dma("Y", T.yx[1:128:2, a:a + n], T.X2[1:128:2, P0 + a:P0 + a + n], "de%d" % t, (XO, ["XOn"])[t] + ["R%s0" % s], [], n // 8)
+                    dma("Y", T.yx[1:128:2, a:a + n], T.X2[1:128:2, P0 + a:P0 + a + n], "de%d" % t, [XOWN[2 * t], "R%s0" % s], [], n // 8)
                 bulk(s, k, t)
-                if k == 3 and FLAT:
-                    level[0] = 20 * t + 4 * NS - 1
                 choose(s, k, t)
                 if k == 3:
                     votes(s, t)
-                    if not t and LB_ == "L":
-                        lists(s, 14, BE[1], True)
         level[0] = 20 * t + 4 * NS
         if t:
             ts(T.VF[:], T.VB[:], 1024.0, None, A_, None, each("VB"), ["VF"], 384)

import numpy as np
from concourse.bass import DstId, RemoteDMATransfer
from concourse.mybir import AluOpType, ActivationFunctionType

ALU = AluOpType
ACT = ActivationFunctionType
P0 = 272
N0 = P0 + 2048
H = N0 + 384
NX = 2 * H
EPS = 2.0 ** -9
LOW = -2048.0
SS = "ABC"
NK = 12 // len(SS)
CW, W = 2 * NK, 32 * NK
GS = 4
PLAN = ((("A", 1, 2), ("S", 11, 3), ("A", 3, 2), ("A", 5, 4), ("A", 9, 2), ("B", 0, 1)),
        (("A", 1, 2), ("S", 12, 3), ("A", 3, 3), ("A", 6, 4), ("A", 10, 2), ("B", 0, 1)))
NB = [sum(n for way, i, n in p if way == "B") for p in PLAN]
ON = (("VVSS",), ("VVSS",))
OFF2 = True
LTP = True
RE = ((2, 2, 2), (8, 4, 4))
COPY = False

CY, FV, FS, FP, PE, SAME, WAKE = 0.83e-3, 0.015, 0.04, 0.015, 0.42e-3, 0.18, 0.19
GA_C, SC_C = 1.5, 3.5
DLAT, BW = 2.0, 300.0
RLAT = 3.0
SETTINGS = ((1.0, 1.5, 3.5, 0.18, 0.19, 1.0, 1.3), (1.2, 1.15, 2.5, 0.18, 0.19, 0.6, 0.8), (1.1, 1.25, 5.0, 0.1, 0.15, 0.6, 0.8), (1.3, 1.9, 5.0, 0.2, 0.3, 1.0, 1.2))
STARTS = 40
PASSES = 3
MIX = 3500
POLISH = 1500
SEED = 3
LOADS = {"dw": 4e3, "dx": 3e3, "dl": 2e3}
ORDER = {}

SCRATCH = {}


def _decl(dtype, where="sbuf", **shapes):
    for n, sh in shapes.items():
        SCRATCH[n] = (where, [128] + sh, dtype)


_decl("bfloat16", X2=[NX], XM=[384], ZD=[144], Z2=[144], ZN=[144], BK=[128], B14=[128], ID2=[256], NI=[128], TRI=[128], TRL=[128],
      TRS=[128], SWB=[512], SX=[128], LA=[2, 138], LB=[128 * NK], EV=[128], EVX=[128], IDS=[128], D14=[128], T1=[128], T2=[128],
      Q=[144], QG=[128], QX=[W], DIAG=[W], K30=[32], SEL=[32], E=[24 * CW, 16], FL=[384], FG=[384], FT1=[H],
      XN=[3, 2 * W], XV=[384], ZN0=[384], ZN1=[384], RZ0=[384], RZ1=[384])
_decl("float16", GA=[384], GA3=[24, 16], LG=[384], VB=[384], QW=[384], KD=[W], OFFS=[W], SC=[384])
_decl("float32", C=[40], TH=[8], DW0=[W], DMF=[W], WT=[24], VF=[384], DM=[384], AS=[384], OF0=[W])
_decl("int32", ATI=[H], FT0=[N0], IDT=[H], W0I=[24], PI=[8])
_decl("uint16", XOFF=[24], XOF2=[24], VL=[3, 2 * CW])
for _s in SS:
    _decl("bfloat16", **{"CD" + _s: [15 * W], "AB" + _s: [15 * W], "XG" + _s: [4 * W], "Z" + _s: [(GS + 1) * W], "ZF" + _s: [CW, 16],
                         "VAL" + _s: [W], "GT" + _s: [CW, 16]})
    _decl("float16", **{"LT" + _s: [W], "R" + _s: [4 * CW, 16]})
    _decl("float32", **{"KT" + _s: [32], "KW" + _s: [W]})
    _decl("uint16", **{"CL" + _s: [W]})
    _decl("float32", "psum", **{"pD" + _s: [32, 16], "pK" + _s: [32, 16]})
_decl("float32", "psum", pS0=[32, 16], pS1=[32, 16])
SEMAPHORES = ["sv", "ss", "sp", "sg", "dw", "dl", "dx", "da", "dd", "df00", "df01", "df02", "df10", "df11", "df12", "de0", "de1", "do", "dv", "arr0", "arr1", "lsem"] + ["dg" + _s for _s in SS]


def schedule(ops):
    if len(ops) in ORDER:
        return [ops[j] for j in ORDER[len(ops)]]
    preds, lastw, readers = [], {}, {}
    for j, o in enumerate(ops):
        p = {}
        for k in o["r"]:
            for x in lastw.get(k, ()):
                p[x] = 0 if k[0] == "p" and ops[x]["e"] == o["e"] else 1
            if k[0] == "p":
                for x in readers.get(k, ()):
                    p.setdefault(x, 0 if ops[x]["e"] == o["e"] else 1)
        group = {}
        for k in o["w"]:
            group[k] = [x for x in lastw.get(k, ()) if o["sem"] and ops[x]["sem"] == o["sem"] and not readers.get(k)]
            for x in lastw.get(k, []) + readers.get(k, []):
                if x not in group[k]:
                    p.setdefault(x, 0 if ops[x]["e"] == o["e"] == "P" else 1)
        p.pop(j, None)
        preds.append(p)
        for k in o["r"]:
            readers.setdefault(k, []).append(j)
        for k in o["w"]:
            lastw[k] = group[k] + [j]
            readers[k] = []
    n = len(ops)
    succ = [[] for _ in range(n)]
    for j in range(n):
        for i in preds[j]:
            succ[i].append(j)
    bl = [0.0] * n
    for j in range(n - 1, -1, -1):
        bl[j] = ops[j]["c"] + ops[j]["lat"] + max([bl[x] + (SAME if ops[x]["e"] == ops[j]["e"] else WAKE) for x in succ[j]] or [0.0])
    lev = [o["lev"] for o in ops]
    for j in range(n - 1, -1, -1):
        if lev[j] is None:
            lev[j] = min([lev[x] for x in succ[j]] or [99])
    how = {}
    lag = lambda i, j: (SAME if ops[i]["e"] == ops[j]["e"] and not ops[i]["lat"] else how["wake"]) if preds[j][i] else 0.0

    def place(rank, back):
        after, left = (preds, [len(x) for x in succ]) if back else (succ, [len(x) for x in preds])
        base, end, free, out, dmaq = [0.0] * n, [0.0] * n, {}, [], 0.0
        ready = [j for j in range(n) if not left[j]]
        while ready:
            st = [max(base[j], free.get(ops[j]["e"], 0.0)) for j in ready]
            t0 = min(st)
            e0 = ops[ready[st.index(t0)]]["e"]
            mine = [(x, s) for x, s in zip(ready, st) if ops[x]["e"] == e0]
            j = max((x for x, s in mine if s <= t0 + how["near"]), key=rank)
            soon = [(x, s) for x, s in mine if rank(x) > rank(j) and s < t0 + how["slack"] * (e0 in "VSP") * ops[j]["c"]]
            if soon:
                k, sk = max(soon, key=lambda a: rank(a[0]))
                fits = [x for x, s in mine if s + ops[x]["c"] <= sk + how["near"]]
                j = max(fits, key=rank) if fits else k
            ready.remove(j)
            o = ops[j]
            fin = end[j] = free[o["e"]] = max(base[j], free.get(o["e"], 0.0)) + o["c"]
            if o["lat"] and not back:
                dmaq = max(dmaq, fin) + o["by"]
                fin = end[j] = dmaq + o["lat"]
            out.append(j)
            for x in after[j]:
                base[x] = max(base[x], fin + (lag(x, j) + ops[x]["lat"] + ops[x]["by"] if back else lag(j, x)))
                left[x] -= 1
                if not left[x]:
                    ready.append(x)
        return out, end

    found = []
    for a in range(STARTS):
        how["near"], how["slack"] = 0.02 + 0.05 * (a * 0.618 % 1), 0.15 + 0.35 * (a * 0.755 % 1)
        how["wake"] = WAKE - 0.03 + 0.1 * (a * 0.570 % 1)
        now = place(lambda x: (-lev[x], bl[x] + ops[x]["first"], -x), False)
        for _ in range(PASSES):
            fin = now[1]
            late = place(lambda x: (fin[x], x), True)[1]
            now = place(lambda x: (late[x] + ops[x]["first"], -x), False)
            found.append(now[0])
    ORDER[n] = polish(ops, preds, succ, found)
    return [ops[j] for j in ORDER[n]]


def polish(ops, preds, succ, found):
    n = len(ops)
    eng = [o["e"] for o in ops]
    sets = []
    for f, ga, sc, same, wake, dl, bw in SETTINGS:
        cost = [o["c"] if o["sem"] else f * (o["c"] + CY * (o["ng"] * (ga - GA_C) + o["ns"] * (sc - SC_C))) for o in ops]
        pl = [[(i, (same if eng[i] == eng[j] and not ops[i]["lat"] else wake) if k else 0.0) for i, k in preds[j].items()] for j in range(n)]
        sets.append((cost, pl, [o["lat"] * dl for o in ops], [o["by"] * bw for o in ops]))

    def run(seq, st):
        cost, pl, lat, by = st
        end, why, free, last, dmaq = [0.0] * n, [-1] * n, {}, {}, 0.0
        for j in seq:
            e = eng[j]
            t, w = free.get(e, 0.0), last.get(e, -1)
            for i, g in pl[j]:
                if end[i] + g > t:
                    t, w = end[i] + g, i
            t += cost[j]
            free[e], last[e], why[j] = t, j, w
            if lat[j]:
                dmaq = max(dmaq, t) + by[j]
                t = dmaq + lat[j]
            end[j] = t
        return max(end), end, why

    rng = np.random.default_rng(SEED)
    base = [run(found[0], st)[0] for st in sets]
    rate = lambda o: sum(run(o, st)[0] / b for st, b in zip(sets, base))
    best, order = min((rate(o), o) for o in found)
    for _ in range(MIX):
        other = found[int(rng.integers(len(found)))]
        a = int(rng.integers(n))
        b = min(n, a + int(rng.integers(50, n // 2)))
        part = set(order[a:b])
        new = order[:a] + [x for x in other if x in part] + order[b:]
        best, order = min((best, order), (rate(new), new))
    pairs = None
    for _ in range(POLISH):
        if pairs is None:
            pos = {j: p for p, j in enumerate(order)}
            pairs = []
            for st in sets:
                top, end, why = run(order, st)
                j = end.index(top)
                while why[j] >= 0:
                    if eng[why[j]] == eng[j] and why[j] not in preds[j]:
                        pairs.append((why[j], j))
                    j = why[j]
        u, v = pairs[int(rng.integers(len(pairs)))]
        a, b = pos[u], pos[v]
        far = int(rng.integers(6)) * (rng.random() < 0.6)
        if rng.random() < 0.7:
            while far and a > 0:
                a -= 1
                far -= eng[order[a]] == eng[v]
            mid, up = order[a:b], {v}
            for x in reversed(mid):
                if any(y in up for y in succ[x]):
                    up.add(x)
            new = order[:a] + [x for x in mid if x in up] + [v] + [x for x in mid if x not in up] + order[b + 1:]
        else:
            while far and b < n - 1:
                b += 1
                far -= eng[order[b]] == eng[u]
            mid, down = order[a + 1:b + 1], {u}
            for x in mid:
                if any(y in down for y in preds[x]):
                    down.add(x)
            new = order[:a] + [x for x in mid if x not in down] + [u] + [x for x in mid if x in down] + order[b + 1:]
        s = rate(new)
        if s < best:
            best, order, pairs = s, new, None
    return order


def emit(g, T, ops, sent):
    eng = {"V": g.vector, "S": g.scalar, "P": g.tensor, "G": g, "Y": g.sync}
    sem = {"V": "sv", "S": "ss", "P": "sp", "G": "sg"}
    cnt = {}
    know = {e: {} for e in eng}
    lastw, readers, snaps = {}, {}, {}

    def wait_for(e, r, w, me):
        need = []
        for k in r:
            if k in lastw:
                need.append((lastw[k], False))
            if k[0] == "p":
                need.extend((x, True) for x in readers.get(k, ()))
        for k in w:
            if k in lastw:
                need.append((lastw[k], False))
            need.extend((x, False) for x in readers.get(k, ()))
        mx = {}
        for (s, c), both_read in need:
            if (s == e and (both_read or e == "P")) or s == me:
                continue
            if s not in eng:
                c = cnt[s]
            if know[e].get(s, 0) < c:
                mx[s] = max(mx.get(s, 0), c)
        for s in list(mx):
            if any(s2 != s and mx[s2] and snaps.get((s2, mx[s2]), {}).get(s, 0) >= mx[s] for s2 in mx):
                know[e][s] = max(know[e].get(s, 0), mx[s])
                mx[s] = 0
        for s, c in mx.items():
            if c:
                eng[e].wait_ge(T.sem[sem.get(s, s)], c)
                for s2, c2 in snaps.get((s, c), {}).items():
                    know[e][s2] = max(know[e].get(s2, 0), c2)
                know[e][s] = max(know[e].get(s, 0), c)

    for o in ops:
        e, r, w = o["e"], o["r"], o["w"]
        if e == "R":
            cnt[o["sem"]] = o["fn"]
            for k in w:
                lastw[k] = (o["sem"], o["fn"])
            continue
        wait_for(e, r, w, o["sem"])
        if o["sem"] == "lsem":
            o["fn"](eng[e])
            continue
        s, add = (o["sem"], 16) if o["sem"] else (e, 1)
        cnt[s] = cnt.get(s, 0) + add
        o["fn"](eng[e]).then_inc(T.sem[sem.get(s, s)], add)
        tok = (s, cnt[s])
        sn = dict(know[e])
        if s in eng:
            sn[s] = cnt[s]
        else:
            for s2, c2 in snaps.get((s, cnt[s] - 16), {}).items():
                sn[s2] = max(sn.get(s2, 0), c2)
        snaps[tok] = sn
        for k in r:
            readers.setdefault(k, []).append(tok)
        for k in w:
            lastw[k] = tok
            readers[k] = []
    for s, c in sorted(cnt.items()):
        if know["G"].get(s, 0) < c:
            g.wait_ge(T.sem[sem.get(s, s)], c)
    g.wait_ge(T.sem.lsem, sent)


def rank_program(g, core, T, topo):
    rank = T.rank_of(core)
    if rank is None:
        return
    ops, moved, level = [], {}, [None]

    def op(e, fn, r, w, c, sem=None, lat=0.0, by=0.0):
        ops.append({"e": e, "fn": fn, "r": list(r), "w": list(w), "c": c, "sem": sem, "lat": lat, "by": by,
                    "ng": moved.pop("g", 0), "ns": moved.pop("s", 0),
                    "first": LOADS.get(sem, 0.0), "lev": -9 if sem in LOADS else level[0]})

    def V(fn, r, w, n):
        op("V", fn, r, w, FV + max(64, n) * CY)

    def ts(out, in0, s1, s2, op0, op1, r, w, n=64):
        if op1 is None:
            V(lambda v: v.tensor_scalar(out, in0, s1, None, op0), r, w, n)
        else:
            V(lambda v: v.tensor_scalar(out, in0, s1, s2, op0, op1), r, w, n)

    def tt(out, in0, in1, o, r, w, n=64):
        V(lambda v: v.tensor_tensor(out, in0, in1, o), r, w, n)

    def cp(out, in_, r, w, n=64):
        V(lambda v: v.tensor_copy(out, in_), r, w, n)

    def tr(out, in_, r, w, n=64):
        V(lambda v: v.transpose(out, in_), r, w, n)

    def act(out, in_, f, bias, scale, r, w, n):
        op("S", lambda s: s.activation(out, in_, f, bias=bias, scale=scale), r, w, FS + n * CY)

    def mm(out, lhsT, rhs, start, stop, r, w, n, least=64):
        op("P", lambda t: t.matmul(out, lhsT, rhs, start, stop), r, w, FP + max(least, n) * PE)

    def dma(e, out, in_, sem, r, w, kb):
        op(e, lambda q: q.dma_start(out=out, in_=in_), r, w, 0.07, sem, DLAT, kb / BW)

    def iota(out, pat, base, cm, key, n, flag=True, after=()):
        if flag:
            op("G", lambda q: q.iota(out, pat, base, cm, allow_small_or_imprecise_dtypes=True), after, [key], 0.13 + 2 * n * CY)
        else:
            op("G", lambda q: q.iota(out, pat, base, cm), after, [key], 0.13 + 2 * n * CY)

    def select(out, in_, cmp, fill, sign, r, w, n=128):
        op("G", lambda q: q.affine_select(out, in_, [[sign, n]], cmp, fill, 0, -sign), r, w, 0.17 + 2 * n * CY)

    B = lambda n, s: T[n + s]
    st = {s: i for i, s in enumerate(SS)}
    NS = len(SS)
    gat = lambda n: 40 + moved.setdefault("g", n) * GA_C
    sca = lambda: 40 + moved.setdefault("s", W) * SC_C
    each = lambda k: [k + s for s in SS]
    I_ = ACT.Identity

    dma("S", T.W0I[:], T.w0[:], "dw", [], ["W0I"], 12)
    dma("Y", T.X2[:, P0:N0], T.x0[:, :], "dx", [], ["XO"], 512)
    V(lambda v: v.memset(T.ATI[:, 0:P0], 0), [], ["ATp"], P0)
    dma("Y", T.ATI[15:128:16, P0:N0], T.nx[:, :], "dl", [], ["AT"], 64)
    for i in range(4):
        a = slice(2 ** i - 1, 128, 2 ** (i + 1))
        dma("SY"[i % 2], T.ATI[a, P0:N0], T.lk[a, :], "dl", [], ["AT"], 512 >> i)

    iota(T.PI[:, 0:1], [[1, 1]], 0, 1, "PI", 1, False)
    iota(T.Q[:], [[1, 144]], 0, 0, "Q", 144)
    iota(T.QG[:], [[1, 8], [0, 16]], 0, 0, "QG", 128)
    V(lambda v: v.memset(T.X2[:, 0:P0], 255.0), [], ["XOp"], P0 // 2)
    V(lambda v: v.memset(T.X2[:, N0:H + P0], 255.0), [], ["XOn", "XTp"], (384 + P0) // 2)
    V(lambda v: v.memset(T.DMF[:], 4096.0), [], ["DMF"], W)
    iota(T.QX[:], [[0, CW], [1, 16]], 0, 0, "QX", W)
    iota(T.DW0[:], [[2, W]], 2178 + P0, 0, "DW0", W)
    iota(T.K30[:], [[0, 32]], 30720, 0, "K30", 32)
    FTK = [[], []]

    def late(t):
        after = ["G3" + SS[0]]
        if not t:
            iota(T.IDT[:], [[1, H]], -P0 - 1024, 0, "IDT", H, False, ["TRI", "TRL", "TRS", "B14"])
            select(T.QW[:], T.IDT[:, P0 + 1024:P0 + 1408], ALU.is_ge, 0.0, 0, after + ["IDT"], ["QW"], 384)
            for u in range(2):
                ft, n = T["FT%d" % u], (N0 + 384 * u) // 8
                FTK[u].append("FT%d" % u)
                iota(ft[:, 0:n], [[0, n]], 2 * u - 1, 0, FTK[u][0], n, u == 1, after)
                for j in range(3):
                    FTK[u].append("FT%d%d" % (u, j))
                    dma("Y", ft[:, n << j:n << j + 1], ft[:, 0:n << j], "df%d%d" % (u, j), FTK[u][:-1], FTK[u][-1:], (n << j) // (2 + 2 * u))

    c = lambda i: T.C[:, i:i + 1]
    ts(T.PI[:, 1:2], T.PI[:, 0:1], 4, None, ALU.arith_shift_right, None, ["PI"], ["PI1"])
    ts(T.PI[:, 2:3], T.PI[:, 0:1], 15, None, ALU.bitwise_and, None, ["PI"], ["PI2"])
    ts(T.PI[:, 3:4], T.PI[:, 0:1], 4, 1, ALU.arith_shift_right, ALU.bitwise_and, ["PI"], ["PI3"])
    ts(T.PI[:, 4:5], T.PI[:, 0:1], 1, None, ALU.bitwise_and, None, ["PI"], ["PI4"])
    cp(T.C[:, 0:5], T.PI[:, 0:5], ["PI", "PI1", "PI2", "PI3", "PI4"], ["C0"])
    A_, M_, EQ = ALU.add, ALU.mult, ALU.is_equal
    for o, i, s1, s2, o0, o1 in [
        (5, 3, float(H), 1024.0 + P0, M_, A_),
        (6, 2, 15.0, None, EQ, None),
        (7, 2, 14.0, None, EQ, None),
        (15, 2, -1.0, 0, M_, A_),
        (16, 3, 1000.0, 0, M_, A_),
        (19, 3, -1000.0, 0, M_, A_),
        (17, 3, -32.0, 0, M_, A_),
        (23, 6, 2048.0, -2048.0, M_, A_),
        (22, 2, 1.0, 23, A_, M_),
        (10, 22, -1.0, -32768.0, M_, A_),
        (27, 2, float(NB[1]), 2048.0, ALU.is_lt, M_),
        (28, 27, 69.5, None, A_, None),
        (8, 6, 1.0e6, 28, M_, A_),
        (29, 2, NB[0] + 0.5 * (NB[1] - NB[0]) - 0.5, -2048.0 * (NB[1] - NB[0]), EQ, M_),
        (30, 7, -1.0e6, 29, M_, A_),
        (9, 30, 8, None, A_, None),
        (11, 2, 1.0, -2048.0, A_, M_),
        (25, 3, -15.0, 15, M_, A_),
        (26, 3, NK - 16.0, 15, M_, A_),
        (12, 4, 7.5, -7.5, M_, A_),
        (20, 12, -128.0, None, A_, None),
        (13, 7, 2048.0, None, M_, None),
        (36, 7, 1025.0, None, M_, None),
        (21, 7, -1.0, 1.0, M_, A_),
        (14, 6, 1025.0, -1.0, M_, A_),
        (34, 3, -2.0 * H, float(H), M_, A_),
        (35, 3, float(-H), 1024.0 + P0 + H, M_, A_),
        (24, 2, 2.0, 3, M_, A_),
        (39, 2, -2.0, 254.0 - 1024 - P0, M_, A_),
    ]:
        col = lambda x: c(x) if isinstance(x, int) else x
        key = lambda x: "C%d" % (x if x > 4 else 0)
        ts(c(o), c(i), col(s1), col(s2), o0, o1, [key(x) for x in (i, s1, s2) if isinstance(x, int)], [key(o)])
    for t in range(2):
        ts(T.TH[:, 4 * t:4 * t + 4], T.Q[:, 0:4], c(11), c(9 - t), M_, A_, ["Q", "C11", "C%d" % (9 - t)], ["TH%d" % t])
    ID = T.ID2[:, 0:128]
    Q = T.Q[:, 0:128]
    SW = ["SW%d" % j for j in range(4)]
    for j in range(4):
        u, d = j // 2, j % 2
        ts(T.SWB[:, 128 * j:128 * j + 128], Q, 16.0 * (u - d) - 1000.0 * u, c(16 + 3 * u), A_, EQ, ["Q", "C%d" % (16 + 3 * u)], [SW[j]])
    swb = lambda s, d: T.SWB[:, 128 * (2 * s + d):128 * (2 * s + d) + 128]
    ts(T.SX[:], Q, -16.0, c(17), A_, EQ, ["Q", "C17"], ["SX"])
    ts(ID, Q, c(0), None, EQ, None, ["Q", "C0"], ["ID"])
    act(T.ID2[:, 128:256], ID, I_, 0.0, 1.0, ["ID"], ["ID2"], 128)
    act(T.NI[:], ID, I_, 0.0, -1.0, ["ID"], ["NI"], 128)
    act(T.EV[:], ID, I_, 0.0, c(12), ["ID", "C12"], ["EV"], 128)
    act(T.EVX[:], T.SX[:], I_, 0.0, c(12), ["SX", "C12"], ["EVX"], 128)
    for m in ("EV", "EVX"):
        act(T[m][:, 14:128:16], T[m][:, 12:128:16], I_, 0.0, 1.0, [m], [m], 8)
    act(T.IDS[:], ID, I_, 0.0, -2.0 ** -23, ["ID"], ["IDS"], 128)
    act(T.D14[:], ID, I_, 0.0, c(7), ["ID", "C7"], ["D14"], 128)
    ts(T.SEL[:], T.Q[:, 0:32], c(24), None, EQ, None, ["Q", "C24"], ["SEL"])
    ts(T.ZD[:], T.Q[:], -15.0, c(15), A_, EQ, ["Q", "C15"], ["ZD"], 72)
    ts(T.BK[:], T.QG[:], c(1), None, EQ, None, ["QG", "C0"], ["BK"])
    act(T.Z2[:], T.ZD[:], I_, 0.0, 2.0, ["ZD"], ["Z2"], 144)
    act(T.ZN[:], T.ZD[:], I_, 0.0, -1.0, ["ZD"], ["ZN"], 144)
    act(T.T1[:], T.BK[:], I_, 0.0, c(23), ["BK", "C23"], ["T1"], 128)
    select(T.T2[:], T.T1[:], ALU.is_gt, 0.0, -1, ["T1"], ["T2"])
    act(T.T2[:, 15:128:16], T.T1[:, 15:128:16], I_, 0.0, 1.0, ["T1"], ["T2"], 8)
    select(T.TRI[:], T.T2[:], ALU.not_equal, 2048.0, 1, ["T2"], ["TRI"])
    select(T.TRL[:], T.BK[:], ALU.is_ge, 0.0, 1, ["BK"], ["TRL"])
    iota(T.TRL[:, 15:128:16], [[0, 8]], 0, 0, "TRL", 8)
    select(T.TRS[:], T.BK[:], ALU.is_gt, 0.0, 1, ["BK"], ["TRS"])
    select(T.B14[:], T.BK[:], ALU.is_ge, 0.0, 0, ["BK"], ["B14"])
    iota(T.B14[:, 14:128:16], [[0, 8]], 0, 0, "B14", 8)
    ts(T.LA[:, 0, :], T.Q[:, 0:138], -10.0, c(25), A_, EQ, ["Q", "C25"], ["LA0"], 69)
    ts(T.LA[:, 1, :], T.Q[:, 0:138], -10.0 - CW, c(26), A_, EQ, ["Q", "C26"], ["LA1"], 69)
    hk = NK // 2
    for b in range(NK):
        pk = "pD" + SS[b // hk]
        for j in range(2):
            o = 10 - (2 - j) * b
            mm(T[pk][:, 8 * (b % hk):8 * (b % hk) + 8, :], ID, T.LA[:, j, o:o + 128], j == 0, j == 1, ["ID", "LA%d" % j], [pk], 128)
    for j in range(2):
        act(T.LB[:, 128 * hk * j:128 * hk * (j + 1)], T["pD" + SS[j]][:, 0:8 * hk, :], I_, 0.0, 1.0, ["pD" + SS[j]], ["LB%d" % j], 128 * hk)
    iota(T.OF0[:], [[0, W // 2], [1, 2]], 0, 0, "OF0", W)
    ts(T.OFFS[:], T.OF0[:], c(34), c(5), M_, A_, ["OF0", "C34", "C5"], ["OFFS"], W)
    ts(T.DIAG[:], T.QX[:], c(2), None, EQ, None, ["QX", "C0"], ["DIAG"], W // 2)
    tt(T.KD[:], T.DIAG[:], T.DW0[:], M_, ["DIAG", "DW0"], ["KD"], 2 * W)
    ts(T.DMF[:, 0:W:16], T.Q[:, 0:W:16], -2.0, c(39), M_, A_, ["Q", "C39"], ["DMF"])
    XT = ["XT%d" % j for j in range(4)] + ["XTp"]
    for j in range(4):
        pk, o = "pS%d" % (j % 2), T.X2[:, H + P0 + 512 * j:H + P0 + 512 * j + 512]
        mm(T[pk][:], T.SX[:], T.X2[:, P0 + 512 * j:P0 + 512 * j + 512], True, True, ["SX", "XO"], [pk], 512)
        if j % 2:
            act(o, T[pk][:], I_, 0.0, 1.0, [pk], [XT[j]], 512)
        else:
            cp(o, T[pk][:], [pk], [XT[j]], 512)

    ix = {s: NS - 1 - st[s] for s in SS}
    sl = lambda s: slice(CW * ix[s], CW * ix[s] + CW)
    sw = lambda s: slice(W * ix[s], W * ix[s] + W)
    XOWN = ["XO", "XOp", "XOn"]
    xall = lambda t: XOWN + XT + ["XTn"] * t
    xwin = lambda t: T.X2[:, 0:H + N0 + 384 * t]
    xown = lambda t: T.X2[:, 0:N0 + 384 * t]
    turns, sent = [0], [0]

    def bank():
        turns[0] += 1
        return "pS%d" % (turns[0] % 2)

    ts(T.VL[:, :, 0:CW], T.W0I[:], float(P0), None, A_, None, ["W0I"], each("VL"))
    for u in range(2):
        ts(T.VL[:, :, CW + NK * u:CW + NK * u + NK], T.W0I[:, u:24:2], float(P0), None, A_, None, ["W0I"], ["VX%s%d" % (s, u) for s in SS])
    vl = lambda s, a, b: T.VL[:, ix[s], a:b]

    def agather(s, t, last=False, e="V"):
        src, r = T.ATI[:, 0:N0 + 384 * t].indirect(vl(s, 0, CW)), ["AT", "ATp", "VL" + s] + ["ATn"] * t
        if e == "S":
            act(T.GA[:, sw(s)], src, I_, -1024.0, 1.0, r, ["GA" + s], gat(W))
        else:
            ts(T.GA[:, sw(s)], src, -1024.0, None, A_, None, r, ["GA" + s], gat(W))
        if not last:
            dma("Y", T.GA3[:, sl(s), :], T.GA[:, sw(s)], "dg" + s, ["GA" + s], ["G3" + s], W // 4)

    def xgather(s, t, bias=0.0):
        src, r = xown(t).indirect(vl(s, CW, 2 * CW)), XOWN[:2 + t] + ["VX%s0" % s, "VX%s1" % s]
        act(T.XV[:, sw(s)], src, I_, bias, 1.0, r, ["XV" + s], gat(W))

    def swap4(out, o0, src, key, r, stop, start=False):
        for u in range(2):
            for v in range(2):
                mm(out[:, o0 + v:o0 + CW:2, :], swb(v, u), src(u), start and u + v == 0, stop and u + v == 2, r + SW, [key], W // 2)

    def xv(s):
        return lambda u: T.XV[:, W * ix[s] + W // 2 * u:W * ix[s] + W // 2 * (u + 1)]

    def zstep(s, first, final=False, e="S"):
        pk, z, z0 = "pK" + s, B("Z", s), "Z%s0" % s
        o = T[pk][:, CW:2 * CW, :]
        if not first:
            mm(o, ID, z[:, 0:W], True, False, ["ID", z0], [pk], W)
        swap4(T[pk], CW, xv(s), pk, ["XV" + s], True, first)
        if final:
            ts(z[:, GS * W:GS * W + W], z[:, 0:W], 2.0, None, M_, None, [z0], ["Z2" + s])
            select(B("ZF", s)[:], z[:, 0:W], ALU.is_ge, 0.0, 0, [z0], ["ZF" + s])
            tt(B("GT", s)[:], o, z[:, GS * W:GS * W + W], ALU.is_gt, [pk, "Z2" + s], ["GT" + s], W)
            return
        if e == "V":
            ts(z[:, 0:W], o, 0.5, 63.75, M_, A_, [pk], [z0], W)
        else:
            act(z[:, 0:W], o, I_, 128.0 if first else 63.75, 1.0 if first else 0.5, [pk], [z0], W)
        for d in range(1, GS):
            if first:
                cp(z[:, W * d:W * d + W], z[:, 0:W], [z0], ["Z%s%d" % (s, d)], W // 2)
            else:
                select(z[:, W * d:W * d + W], z[:, 0:W], ALU.is_ge, 0.0, 0, [z0], ["Z%s%d" % (s, d)])

    def lists(s, L, last=False):
        pd = bank() if last else "pD" + s
        o, keys = T[pd][:, 16:16 + L, 0:CW], ["CL%s%d%s" % (s, x, y) for x in range(L - 13) for y in "ab"]
        two = OFF2 and not last
        if not two:
            mm(o, ID, T.OFFS[:, 0:CW * L], True, False, ["ID", "OFFS"], [pd], CW * L)
        if not LTP:
            tr(B("LT", s)[:], T.GA[:, sw(s)], ["GA" + s], ["LT" + s], W // 2)
            for j in range(CW):
                mm(o[:, :, j], ID, B("LT", s)[:, 16 * j:16 * j + L], two and not j, j == CW - 1, ["ID", "LT" + s], [pd], 64)
        for b in range(NK * LTP):
            for a in range(0, 128, 32):
                w = W * ix[s] + 32 * b
                mm(T[pd][a:a + 32, 16:16 + L, 2 * b:2 * b + 2], T.GA[a:a + 32, w:w + 32], T.SEL[a:a + 32, 0:2 * L], two and b == 0, b == NK - 1,
                   ["SEL", "GA" + s], [pd], 32, 32)
        if two:
            for h in range(2):
                ts(B("CL", s)[:, h:CW * L:2], o[:, :, h:CW:2], c(5 + 30 * h), None, A_, None, [pd, "C5", "C35"], keys[h::2])
        elif last:
            act(B("CL", s)[:, 0:CW * L], o, I_, 0.0, 1.0, [pd], keys, CW * L)
        else:
            cp(B("CL", s)[:, 0:CW * L], o, [pd], keys, CW * L)

    def begin(s, t):
        if t:
            w, lt, pd = sw(s), B("LT", s), "pD" + s
            act(T.LG[:, w], T.FT0[:].indirect(vl(s, 0, CW)), I_, -1024.0, 1.0, FTK[0] + ["VL" + s], ["LG" + s], gat(W))
            tr(lt[:], T.LG[:, w], ["LG" + s], ["LT" + s], W // 2)
            for h in range(2):
                ts(B("CL", s)[:, 14 * CW + h:15 * CW:2], lt[:, 16 * h + 14:W:32], c(5 + 30 * h), None, A_, None,
                   ["LT" + s, "C%d" % (5 + 30 * h)], ["CL%s1%s" % (s, "ab"[h])])
            mm(T[pd][:, 0:CW, :], ID, T.GA[:, w], True, False, ["ID", "GA" + s], [pd], W)
            mm(T[pd][:, 0:CW, :], T.D14[:], T.LG[:, w], False, True, ["D14", "LG" + s], [pd], W)
            act(T.GA3[:, sl(s), :], T[pd][:, 0:CW, :], I_, c(36), 1.0, [pd, "C36"], ["G3" + s], W)
        else:
            agather(s, 0)
            lists(s, 14)
        xgather(s, 0)
        zstep(s, True)

    def bulk(s, k, t):
        pd, ab, cd, cl, z = B("pD", s), B("AB", s), B("CD", s), B("CL", s), B("Z", s)
        zk = lambda n: ["Z%s%d" % (s, d) for d in range(n)]
        abk = lambda i, n: ["AB%s%d" % (s, x) for x in range(i, i + n)]
        cdk = lambda i, n: ["CD%s%d" % (s, x) for x in range(i, i + n)]
        sums = []
        for mode, i, n in PLAN[t]:
            part, src = slice(W * i, W * (i + n)), xwin(t).indirect(cl[:, CW * i:CW * (i + n)])
            r = xall(t) + ["CL%s%d%s" % (s, x, y) for x in range(1 + (i + n > 14)) for y in "ab"]
            if mode != "S":
                tt(cd[:, part], src, z[:, 0:W * n], ALU.subtract, r + zk(n), cdk(i, n), gat(W * n))
            if mode == "A":
                act(ab[:, part], cd[:, part], ACT.Abs, 128.0, 1.0, cdk(i, n), abk(i, n), W * n)
            if mode == "B":
                ts(ab[:, part], cd[:, part], 128.0, 0.0, A_, ALU.max, cdk(i, n), abk(i, n), W * n // 2)
                sums += [("ZN", cd, x, cdk(x, 1)) for x in range(i, i + n)] + [("Z2", ab, x, abk(x, 1)) for x in range(i, i + n)]
            else:
                sums += [("ZD", ab, x, abk(x, 1)) for x in range(i, i + n)]
            if mode == "S":
                q = bank()
                xg, o = B("XG", s)[:, 0:W * n], T[q][:, 0:CW * n, :]
                act(xg, src, I_, 0.0, 1.0, r, ["XG" + s], gat(W * n))
                mm(o, T.NI[:], z[:, 0:W * n], True, False, ["NI"] + zk(n), [q], W * n)
                mm(o, ID, xg, False, True, ["ID", "XG" + s], [q], W * n)
                act(ab[:, part], o, ACT.Abs, 128.0, 1.0, [q], abk(i, n), W * n)
        for j in range(k):
            mm(pd[:, 0:CW, :], T.TRL[:], B("R", s)[:, CW * j:CW * j + CW, :], j == 0, False, ["TRL", "R%s%d" % (s, j)], ["pD" + s], W)
        for j, (mat, src, x, keys) in enumerate(sums):
            mm(pd[:, 0:CW, :], T[mat][:, 15 - x:143 - x], src[:, W * x:W * x + W], j == 0 and not k, j == len(sums) - 1,
               [mat] + keys, ["pD" + s], W)
        swap4(B("pK", s), 0, lambda u: T.GA3[:, CW * ix[s] + u:CW * ix[s] + CW:2, :], "pK" + s, ["G3" + s], False, True)

    def choose(s, k, t):
        last = k == 3
        r, rk, kt, pk, pd = B("R", s)[:, CW * k:CW * k + CW, :], "R%s%d" % (s, k), B("KT", s), "pK" + s, "pD" + s
        on, th = ON[t][(NS * k + st[s]) % len(ON[t])], T.TH[:, 4 * t + k:4 * t + k + 1]
        if on[0] == "V":
            ts(B("VAL", s)[:], T[pd][:, 0:CW, :], th, 2.0, ALU.is_lt, M_, [pd, "TH%d" % t], ["VAL" + s], W)
        else:
            act(B("VAL", s)[:], T[pd][:, 0:CW, :], ACT.Sign, th, -1.0, [pd, "TH%d" % t], ["VAL" + s], W)
        mm(T[pk][:, 0:CW, :], T.TRI[:], B("VAL", s)[:], False, True, ["TRI", "VAL" + s], [pk], W)
        ts(r, T[pk][:, 0:CW, :], -4096.0 if on[0] == "V" else c(10), LOW, A_, ALU.max, [pk, "C10"], [rk], W)
        o = T[pd][:, 12:14, :]
        if last:
            mm(o, ID, T.K30[:], True, False, ["ID", "K30"], [pd], 64)
        for b in range(NK):
            mm(o, T.LB[:, 128 * b:128 * b + 128], r[:, 2 * b:2 * b + 2, :], b == 0 and not last, b == NK - 1, ["LB0", "LB1", rk], [pd], 64)
        tr(kt[:], o, [pd], ["KT" + s])
        add, keys = (1024.0 if last else 31744.0) + P0, ["VL" + s, "VX%s0" % s, "VX%s1" % s]
        if on[1] == "V":
            ts(vl(s, 0, 2 * CW), kt[:, 0:2 * CW], add, None, A_, None, ["KT" + s], keys)
        else:
            act(vl(s, 0, 2 * CW), kt[:, 0:2 * CW], I_, add, 1.0, ["KT" + s], keys, 2 * CW)
        if last:
            act(T.VB[:, sw(s)], T.IDT[:].indirect(vl(s, 0, CW)), I_, 0.0, 1.0, ["IDT", "VL" + s], ["VB" + s], gat(W))
        if not (last and t):
            agather(s, t, last, "S" if last else on[2])
        xgather(s, t, 128.0 * last)
        zstep(s, False, last, on[3])
        if not (last and t):
            lists(s, 14 + t, last)

    def votes(s, t):
        pd, zn, pk = "pD" + s, "ZN%d" % t, bank() if s == SS[-1] else "pK" + s
        mm(T[pd][:, 0:CW, :], T.BK[:], B("GT", s)[:], True, True, ["BK", "GT" + s], [pd], W)
        tr(B("KW", s)[:], T[pd][:, 0:CW, :], [pd], ["KW" + s], W)
        ts(T.WT[:, sl(s)], B("KW", s)[:, 0:W:16], 8.5, EPS, ALU.is_lt, A_, ["KW" + s], ["WT" + s])
        swap4(T[pk], 0, lambda u: B("ZF", s)[:, u:CW:2, :], pk, ["ZF" + s], False, True)
        for u in range(2):
            mm(T[pk][:, u:CW:2, :], ID, xv(s)(u), False, u == 1, ["ID", "XV" + s], [pk], W // 2)
        act(T[zn][:, sw(s)], T[pk][:, 0:CW, :], I_, -0.25, 0.5, [pk], [zn + s], W)
        trs = []
        for q in range(8):
            if q == rank or 48 * q // W != ix[s]:
                continue
            dst = T.cores[q]
            rid, pid, _e = topo.addr(dst)
            n = RE[t][st[s]]
            sent[0] += n
            mask = sum(1 << e for e in topo.engines(core, dst)[n * len(trs):n * len(trs) + n])
            trs.append(RemoteDMATransfer(dst_ids=[DstId(rid=rid, pnc=pid)], dma_engine_mask=mask, remote_sem=T.sem["arr%d" % t],
                                         src=T[zn][:, 48 * q:48 * q + 48], dst=T["RZ%d" % t][:, 48 * rank:48 * rank + 48]))
        op("G", lambda q: q.remote_dma_fused(trs, local_sem=T.sem.lsem), [zn + x for x in SS[:st[s] + 1]], [], 1.0, "lsem")

    def flips(t):
        top = level[0]
        if not t:
            act(T.ATI[:, N0:H], T.GA[:], I_, c(14), c(6), each("GA") + ["C6", "C14"], ["ATn"], 384)
        for h, s in enumerate(SS):
            level[0] = top - 1
            pd, pk, w, bl, e0, two = "pD" + s, "pK" + s, sw(s), sl(s), CW * CW * h, 1 if COPY else 2 - t
            ear, rest, ft = T[pd][:, 16:16 + CW, :], T[pk][:, 2 * CW:3 * CW, :], T["FT%d" % t][:]
            mm(ear, T.IDS[:], T.KD[:], True, False, ["IDS", "KD"], [pd], W)
            mm(ear, T.IDS[:], T.VB[:, w], False, False, ["IDS", "VB" + s], [pd], W)
            if not t:
                mm(rest, T.D14[:], T.QW[:, w], True, False, ["D14", "QW"], [pk], W)
            for b in range(CW - 1, -1, -1):
                e, key, n = e0 + CW * b, "E%s%d" % (s, b), bl.start + b
                ts(T.E[:, e:e + CW, :], T.VB[:, w], B("KT", s)[:, b:b + 1], T.WT[:, n:n + 1], EQ, M_, ["VB" + s, "KT" + s, "WT" + s], [key], W // 2)
                mm(rest[:, 0:b + 1, :], T.B14[:], T.E[:, e:e + b + 1, :], b == CW - 1 and t == 1, b == 0 and not h, ["B14", key], [pk], 16 + 16 * b)
                if b < CW - 1:
                    mm(ear[:, b + 1:CW, :], T.BK[:], T.E[:, e + b + 1:e + CW, :], False, False, ["BK", key], [pd], W - 16 - 16 * b)
            mm(ear, T.TRS[:], T.E[:, e0:e0 + CW * CW:CW + 1, :], False, True, ["TRS"] + ["E%s%d" % (s, b) for b in range(CW)], [pd], W)
            act(T.DM[:, w], ear, ACT.Relu, -1408.0, -2.0 ** 23, [pd], ["DM" + s], W)
            V(lambda v, w=w: v.tensor_tensor_scan(T.SC[:, w], T.DMF[:], T.DM[:, w], 4096.0, ALU.min, A_), ["DMF", "DM" + s], ["SC" + s], W)
            sc = T.SC[:, w.start + 15:w.stop:16]
            ts(T.XOFF[:, bl], sc, 1024.0 + P0, None, A_, None, ["SC" + s], ["XOFF" + s])
            if two == 2:
                mm(T[pd][:, 0, 0:CW], T.SX[:], sc, True, True, ["SX", "SC" + s], [pd], 64)
                act(T.XOF2[:, bl], T[pd][:, 0, 0:CW], I_, 1024.0 + P0, 1.0, [pd], ["XOF2" + s], CW)
            if h:
                f, bias, scale = (I_, 0.5, -0.5) if t else (ACT.Relu, 0.0, c(21))
                act(T.FG[:, w], ft.indirect(vl(s, 0, CW)), f, bias, scale, FTK[t] + ["VL" + s, "C21"], ["FG" + s], gat(W))
                mm(rest, ID, T.FG[:, w], False, True, ["ID", "FG" + s], [pk], W)
            if not t:
                act(T.AS[:, w], rest, I_, c(13), 1.0, [pk, "C13"], ["AS" + s], W)
                cp(ft.indirect(T.XOFF[:, bl]), T.AS[:, w], ["AS" + s, "XOFF" + s], FTK[t], sca())
            act(T.FL[:, w], rest, ACT.Sign, 0.875, -1.0, [pk], ["FL" + s], W)
            if t and h < NS - 1:
                cp(ft.indirect(T.XOFF[:, bl]), T.FL[:, w], ["FL" + s, "XOFF" + s], FTK[t], sca())
            for j, (a, b) in enumerate((("ID2", "EV"), ("SX", "EVX"))[:two]):
                o = T[pk][:, j * CW:j * CW + CW, :]
                for u in range(2):
                    mm(o[:, u:CW:2, :], T[a][:, 0:128], xv(s)(u), u == 0, False, ["ID", a, "XV" + s], [pk], W // 2)
                mm(o, T[b][:], T.FL[:, w], False, True, [b, "FL" + s], [pk], W)
            act(T.XN[:, h, 0:W * two], T[pk][:, 0:CW * two, :], ACT.Abs, c(20), 1.0, [pk, "C20"], ["XN" + s], W * two)
            cp(xown(t).indirect(T.XOFF[:, bl]), T.XN[:, h, 0:W], ["XN" + s, "XOFF" + s], XOWN[:2 + t], sca())
            if two == 2:
                cp(T.X2[:, H:H + N0].indirect(T.XOF2[:, bl]), T.XN[:, h, W:2 * W], ["XN" + s, "XOF2" + s], XT, sca())
        level[0] = top
        for i in range(8 * (COPY and not t)):
            a, o = 16 * i, 16 * (i ^ 1)
            dma("YS"[i % 2], T.X2[o:o + 16:2, H + P0:H + N0], T.X2[a:a + 16:2, P0:N0], "dd", ["XO"], XT, 32)
        if not t:
            dma("Y", T.ATI[14:128:16, P0:N0], T.FT0[14:128:16, P0:N0], "da", FTK[0], ["AT"], 64)

    def arrivals(t):
        rz, zn, pk = "RZ%d" % t, "ZN%d" % t, "pS0"
        op("R", 7 * RE[t][NS - 1 - 48 * rank // W], each(zn), [rz], RLAT, "arr%d" % t)
        for r in range(8):
            o = 128 - 16 * ((rank - r) % 8)
            src = T[zn if r == rank else rz]
            mm(T[pk][:, 3 * r:3 * r + 3, :], T.ID2[:, o:o + 128], src[:, 48 * r:48 * r + 48], True, True, ["ID", "ID2", rz] + each(zn), [pk], 64)
        out, key = (T.XM[:], "XM") if t else (T.X2[:, N0:H], "XOn")
        act(out, T[pk][:, 0:24, :], I_, -128.0, 1.0, [pk], [key], 384)
        if not t:
            mm(T.pS1[:, 0:24, :], T.SX[:], out, True, True, ["SX", key], ["pS1"], 384)
            act(T.X2[:, H + N0:NX], T.pS1[:, 0:24, :], I_, 0.0, 1.0, ["pS1"], ["XTn"], 384)

    for t in range(2):
        for s in SS:
            level[0] = 20 * t + st[s] - 0.5
            begin(s, t)
        late(t)
        for k in range(4):
            for s in SS:
                level[0] = 20 * t + NS * k + st[s]
                if (k, s) == (1, SS[0]):
                    a, n = (2048, 384) if t else (0, 2048)
                    dma("Y", T.yx[1:128:2, a:a + n], T.X2[1:128:2, P0 + a:P0 + a + n], "de%d" % t, [XOWN[2 * t], "R%s0" % s], [], n // 8)
                bulk(s, k, t)
                choose(s, k, t)
                if k == 3:
                    votes(s, t)
        level[0] = 20 * t + 4 * NS
        if t:
            ts(T.VF[:], T.VB[:], 1024.0, None, A_, None, each("VB"), ["VF"], 384)
            dma("Y", T.yv[:, :], T.VF[0:128:16, :], "dv", ["VF"], [], 12)
            arrivals(t)
            dma("Y", T.yx[:, 2432:2816], T.XM[:], "dv", ["XM"], [], 96)
        flips(t)
        if not t:
            arrivals(t)
    dma("Y", T.yx[0:128:2, 0:2432], T.X2[0:128:2, P0:H], "do", XOWN, [], 304)
    emit(g, T, schedule(ops), sent[0])
